import numpy as np
import ml_dtypes


def mxq(x, axis, fmt="e4m3"):
    dtype, down = {"e4m3": (ml_dtypes.float8_e4m3fn, 7), "e5m2": (ml_dtypes.float8_e5m2, 14)}[fmt]
    v = np.moveaxis(np.asarray(x, np.float32).astype(ml_dtypes.bfloat16).astype(np.float64), axis, -1)
    blocks = v.reshape(v.shape[:-1] + (-1, 32))
    amax = np.abs(blocks).max(-1, keepdims=True)
    byte = np.maximum(np.where(amax > 0, np.frexp(amax)[1] - 1 + 127, 0) - down, 1)
    scale = np.exp2(byte - 127.0)
    codes = (blocks / scale).astype(np.float32).astype(dtype).astype(np.float64)
    return np.moveaxis((codes * scale).reshape(v.shape), -1, axis)


WIDE = False


def mx_kscale(k):
    if not WIDE:
        return np.ones(k)
    levels = np.array([10, -10, 5, -5, 0])
    if k % 512:
        return np.exp2(np.random.permutation(np.resize(levels, k // 32))).repeat(32)
    a = np.empty((k // 512, 16))
    for p in range(k // 512):
        a[p, :8] = np.random.permutation(np.resize(levels, 8))
        for g in range(8):
            far = levels[np.abs(levels - a[p, g]) >= 10]
            a[p, g + 8] = far[np.random.randint(len(far))]
    return np.exp2(a.ravel()).repeat(32)


def f64(x):
    return np.asarray(x).astype(np.float64)


def striped(idx):
    return np.tile(idx.reshape(-1, 16).T, (8, 1)).astype(np.uint16)


def unstriped(offs):
    return offs[:16].T.reshape(-1).astype(np.int64)


E2M1 = np.array([0.0, 0.5, 1.0, 1.5, 2.0, 3.0, 4.0, 6.0, -0.0, -0.5, -1.0, -1.5, -2.0, -3.0, -4.0, -6.0])


def pack_weight(w, fmt):
    k, n = w.shape
    w = f64(np.asarray(w, np.float32).astype(ml_dtypes.bfloat16)).reshape(k // 32, 32, n)
    amax = np.abs(w).max(1)
    if fmt == "e4m3":
        byte = np.frexp(amax)[1] - 1 + 127 - 7
    else:
        mant, ex = np.frexp(amax / 6.0)
        byte = np.where(mant > 0.5, ex, ex - 1) + 127
    byte = np.clip(np.where(amax > 0, byte, 1), 1, 254)
    scaled = (w * np.exp2(127.0 - byte)[:, None, :]).reshape(k, n).astype(np.float32)
    by_word = np.ascontiguousarray(scaled.reshape(k // 512, 128, 4, n).transpose(0, 1, 3, 2))
    if fmt == "e4m3":
        words = by_word.astype(ml_dtypes.float8_e4m3fn).view(np.uint8)
    else:
        c = by_word.astype(ml_dtypes.float4_e2m1fn).view(np.uint8) & 0xF
        words = (c[..., 0::2] | (c[..., 1::2] << 4)).reshape(k // 512, 128, 2 * n)
    return np.ascontiguousarray(words), np.ascontiguousarray(byte.astype(np.uint8).reshape(k // 512, 16, n))


def unpack_weight(words, scales, fmt):
    g, _, n = scales.shape
    words = np.ascontiguousarray(words).reshape(g, 128, n, -1)
    if fmt == "e4m3":
        vals = words.view(ml_dtypes.float8_e4m3fn).astype(np.float64)
    else:
        nib = np.empty((g, 128, n, 4), np.uint8)
        nib[..., 0::2] = words & 0xF
        nib[..., 1::2] = words >> 4
        vals = E2M1[nib]
    vals = vals * np.repeat(np.exp2(scales.astype(np.float64) - 127.0), 8, axis=1)[..., None]
    return vals.transpose(0, 1, 3, 2).reshape(g * 512, n)


def gelu(v):
    return 0.5 * v * (1.0 + np.tanh(np.sqrt(2.0 / np.pi) * (v + 0.044715 * v**3)))


K, T, E, C, N = 1024, 1024, 16, 256, 128
TOP = 4


def by_expert(wq, xq):
    return np.concatenate([wq[e].T @ xq[:, e * C:(e + 1) * C] for e in range(E)], axis=1)


def setup_inputs():
    n = np.random.standard_normal
    s = mx_kscale(K)[:, None]
    deal = np.repeat(np.arange(E), C).reshape(TOP, T)[:, np.random.permutation(T)]
    deal = np.take_along_axis(deal, np.argsort(np.random.rand(TOP, T), axis=0), axis=0)
    for _ in range(8):
        s_, t_ = np.random.permutation(T).reshape(2, -1); r = np.random.randint(TOP, size=T // 2); x, y = deal[r, s_].copy(), deal[r, t_].copy()
        ok = ~((deal[:, s_] == y).any(0) | (deal[:, t_] == x).any(0)); deal[r[ok], s_[ok]] = y[ok]; deal[r[ok], t_[ok]] = x[ok]
    order = np.lexsort((np.random.rand(TOP * T), deal.reshape(-1)))
    slot_token = order % T; pos = np.empty(TOP * T, np.int64); pos[order] = np.arange(TOP * T); pos = pos.reshape(TOP, T)
    g = np.random.uniform(0.5, 1.5, (TOP, T)); g = g / g.sum(0)
    w = [pack_weight(m, "e2m1") for m in n((E, K, N)) / np.sqrt(K) / s[None]]
    w_slot = np.empty(E * C)
    for r in range(TOP): w_slot[pos[r]] = g[r]
    return {
        "xT": (n((K, T)) * s).astype(np.float32),
        "w_words": np.stack([m[0] for m in w]),
        "w_scales": np.stack([m[1] for m in w]),
        "b": (0.3 * n((N, E))).astype(np.float32),
        "gate": np.tile(w_slot, (K, 1)).astype(np.float32),
        "offs": striped(slot_token),
        "pos1": striped(pos[0]),
        "pos2": striped(pos[1]),
        "pos3": striped(pos[2]),
        "pos4": striped(pos[3]),
    }


def reference(xT, w_words, w_scales, b, gate, offs, pos1, pos2, pos3, pos4):
    idx = unstriped(offs)
    w = np.stack([unpack_weight(w_words[e], w_scales[e], "e2m1") for e in range(E)])
    xq = mxq(f64(gate) * f64(xT)[:, idx], 0, "e4m3")
    y = by_expert(w, xq)
    y = gelu(y + np.repeat(f64(b), C, axis=1))
    return y[:, unstriped(pos1)] + y[:, unstriped(pos2)] + y[:, unstriped(pos3)] + y[:, unstriped(pos4)]

@@ -1,0 +1,178 @@
+from contextlib import ExitStack
+
+import concourse.mybir as mybir
+
+K, T, E, C, N = 1024, 1024, 16, 256, 128
+S = E * C
+FLOPS = 2 * K * N * S
+
+F32 = mybir.dt.float32
+BF16 = mybir.dt.bfloat16
+I32 = mybir.dt.int32
+U32 = mybir.dt.uint32
+U16 = mybir.dt.uint16
+U8 = mybir.dt.uint8
+FP8X4 = mybir.dt.float8_e4m3fn_x4
+FP4X4 = mybir.dt.float4_e2m1fn_x4
+MULT = mybir.AluOpType.mult
+ADD = mybir.AluOpType.add
+GELU = mybir.ActivationFunctionType.Gelu_apprx_tanh
+
+P = 128
+PACK = 4
+PASSES = K // (P * PACK)
+WIDE = 2048
+WINDOW = WIDE + 32
+PIECE = 1024
+MM_N = 128
+BANK = 512
+
+UNITS = [(0, 0, 2048), (1, 0, 2048), (0, 2048, 4096), (1, 2048, 3072), (1, 3072, 3584),
+         (1, 3584, 3840), (1, 3840, 3968), (1, 3968, 4096)]
+GATE_CUTS = [0, 256, 1024, 2048, 4096]
+HALF = 512
+
+
+def tile_moe_pre_lin_gelu_kernel(
+    tc, xT, w_words, w_scales, b, gate, offs, pos1, pos2, pos3, pos4, out
+):
+    nc = tc.nc
+    with ExitStack() as ctx:
+        keep = ctx.enter_context(tc.tile_pool(name="keep", bufs=1))
+        gpool = ctx.enter_context(tc.tile_pool(name="gpool", bufs=2))
+        xpool = ctx.enter_context(tc.tile_pool(name="xpool", bufs=2))
+        cpool = ctx.enter_context(tc.tile_pool(name="cpool", bufs=5))
+        psum = ctx.enter_context(tc.psum_pool(name="psum", bufs=6))
+
+        offs_sb = keep.tile([P, S // 16], U16, name="offs_sb")
+        pos_sb = [keep.tile([P, T // 16], U16, name="pos_sb%d" % r) for r in range(4)]
+        windows = [[keep.tile([P, WINDOW], F32, name="win%d_%d" % (a, j)) for j in range(PACK)] for a in range(PASSES)]
+        gate_sb = keep.tile([P, S], F32, name="gate_sb")
+        w_sb = keep.tile([P, E * PASSES * 2 * N], U8, name="w_sb", align_bytes=64)
+        ws_sb = keep.tile([P, E * PASSES * N], U8, name="ws_sb", align_bytes=64)
+        b_sb = keep.tile([P, E], F32, name="b_sb")
+        y = keep.tile([P, S], F32, name="y")
+
+        x_rows = xT.rearrange("(a p j) t -> a j p t", a=PASSES, j=PACK)
+
+        nc.vector.memset(ws_sb[:].bitcast(I32), 0)
+
+        nc.sync.dma_start(offs_sb[:], offs)
+        nc.sync.dma_start(windows[0][0][:, 0:T], x_rows[0, 0])
+        for lo, hi in zip(GATE_CUTS[:-2], GATE_CUTS[1:-1]):
+            nc.sync.dma_start(gate_sb[:, lo:hi], gate[0:P, lo:hi])
+        for a in range(PASSES):
+            for j in range(PACK):
+                if (a, j) != (0, 0):
+                    nc.sync.dma_start(windows[a][j][:, 0:T], x_rows[a, j])
+        nc.sync.dma_start(gate_sb[:, GATE_CUTS[-2]:S], gate[0:P, GATE_CUTS[-2]:S])
+        nc.sync.dma_start(
+            w_sb[:].bitcast(I32).rearrange("p (g n) -> p g n", g=E * PASSES),
+            w_words.rearrange("e a p n -> p (e a) n").bitcast(I32),
+        )
+        for q in range(4):
+            nc.sync.dma_start(
+                ws_sb[32 * q : 32 * q + 4, :].bitcast(I32).rearrange("p (g n) -> p g n", g=E * PASSES),
+                w_scales[:, :, 4 * q : 4 * q + 4, :].rearrange("e a q n -> q (e a) n").bitcast(I32),
+            )
+        nc.sync.dma_start(b_sb[:], b)
+        for r, pos in enumerate((pos1, pos2, pos3, pos4)):
+            nc.sync.dma_start(pos_sb[r][:], pos)
+
+        quantised = {}
+
+        def gather(u):
+            a, lo, hi = UNITS[u]
+            g = gpool.tile([P, PACK, hi - lo], F32, name="g")
+            for j in range(PACK):
+                cuts = [lo, hi]
+                if u == 0 and j == 0:
+                    cuts = GATE_CUTS[:-1]
+                elif j == PACK - 1 and hi - lo > PIECE:
+                    cuts = list(range(lo, hi + 1, PIECE))
+                for c0, c1 in zip(cuts[:-1], cuts[1:]):
+                    nc.vector.tensor_tensor(
+                        g[:, j, c0 - lo : c1 - lo],
+                        windows[a][j][:].indirect(offs_sb[:, c0 // 16 : c1 // 16]),
+                        gate_sb[:, c0:c1],
+                        MULT,
+                    )
+            return g
+
+        def quantise(u, g):
+            a, lo, hi = UNITS[u]
+            for c0 in range(lo, hi, PIECE):
+                w = min(PIECE, hi - c0)
+                xb = xpool.tile([P, w * PACK], BF16, name="xb", align_bytes=64)
+                nc.scalar.copy(
+                    xb[:].rearrange("p (c i t) -> p c t i", i=4, t=PACK),
+                    g[:, :, c0 - lo : c0 - lo + w].rearrange("p t (c i) -> p c t i", i=4),
+                )
+                codes = cpool.tile([P, w], U32, name="codes", align_bytes=64)
+                scales = cpool.tile([P, w], U8, name="scales", align_bytes=64)
+                nc.vector.quantize_mx(out=codes[:].bitcast(FP8X4), scales=scales[:], in_=xb[:])
+                for m0 in range(c0, c0 + w, MM_N):
+                    quantised[(a, m0)] = (codes, scales, m0 - c0)
+
+        def multiply(u):
+            a_last, lo, hi = UNITS[u]
+            if a_last != PASSES - 1:
+                return
+            for c0 in range(lo, hi, BANK):
+                w = min(BANK, hi - c0)
+                acc = psum.tile([P, w], F32, name="acc")
+                for m0 in range(c0, c0 + w, MM_N):
+                    e = m0 // C
+                    for a in range(PASSES):
+                        codes, scales, at = quantised[(a, m0)]
+                        grp = e * PASSES + a
+                        nc.tensor.matmul_mx(
+                            out=acc[:, m0 - c0 : m0 - c0 + MM_N],
+                            lhsT=w_sb[:, grp * 2 * N : (grp + 1) * 2 * N].bitcast(FP4X4),
+                            lhsT_scale=ws_sb[:, grp * N : (grp + 1) * N],
+                            rhs=codes[:, at : at + MM_N].bitcast(FP8X4),
+                            rhs_scale=scales[:, at : at + MM_N],
+                            start=(a == 0),
+                            stop=(a == PASSES - 1),
+                        )
+                for e0 in range(c0, c0 + w, C):
+                    we = min(C, c0 + w - e0)
+                    e = e0 // C
+                    nc.scalar.activation(
+                        y[:, e0 : e0 + we], acc[:, e0 - c0 : e0 - c0 + we], GELU, bias=b_sb[:, e : e + 1]
+                    )
+
+        g_prev = gather(0)
+        for u in range(1, len(UNITS)):
+            g_next = gather(u)
+            quantise(u - 1, g_prev)
+            multiply(u - 1)
+            g_prev = g_next
+        quantise(len(UNITS) - 1, g_prev)
+        multiply(len(UNITS) - 1)
+
+        back = gpool.tile([P, 4, T], F32, name="g")
+        acc_sb = xpool.tile([P, 3, T], F32, name="xb", align_bytes=64)
+
+        def fetch(r, h):
+            cols = slice(h * HALF, (h + 1) * HALF)
+            nc.vector.tensor_copy(back[:, r, cols], y[:].indirect(pos_sb[r][:, h * HALF // 16 : (h + 1) * HALF // 16]))
+
+        def add(r, h):
+            cols = slice(h * HALF, (h + 1) * HALF)
+            first = back[:, 0, cols] if r == 1 else acc_sb[:, r - 2, cols]
+            nc.vector.tensor_tensor(acc_sb[:, r - 1, cols], first, back[:, r, cols], ADD)
+
+        for h in range(T // HALF):
+            fetch(0, h)
+            if h > 0:
+                add(3, h - 1)
+                nc.sync.dma_start(out[:, (h - 1) * HALF : h * HALF], acc_sb[:, 2, (h - 1) * HALF : h * HALF])
+            fetch(1, h)
+            fetch(2, h)
+            add(1, h)
+            fetch(3, h)
+            add(2, h)
+        h = T // HALF - 1
+        add(3, h)
+        nc.sync.dma_start(out[:, h * HALF : T], acc_sb[:, 2, h * HALF : T])

@@ -27,8 +27,8 @@ PIECE = 1024
 MM_N = 128
 BANK = 512
 
-UNITS = [(0, 0, 2048), (1, 0, 2048), (0, 2048, 4096), (1, 2048, 3072), (1, 3072, 3584),
-         (1, 3584, 3840), (1, 3840, 3968), (1, 3968, 4096)]
+UNITS = [(0, 0, 2048), (1, 0, 2048), (0, 2048, 3072), (0, 3072, 4096), (1, 2048, 3072), (1, 3072, 3584),
+         (1, 3584, 3840), (1, 3840, 4096)]
 GATE_CUTS = [0, 256, 1024, 2048, 4096]
 HALF = 512
 
@@ -41,8 +41,8 @@ def tile_moe_pre_lin_gelu_kernel(
         keep = ctx.enter_context(tc.tile_pool(name="keep", bufs=1))
         gpool = ctx.enter_context(tc.tile_pool(name="gpool", bufs=2))
         xpool = ctx.enter_context(tc.tile_pool(name="xpool", bufs=2))
-        cpool = ctx.enter_context(tc.tile_pool(name="cpool", bufs=5))
-        psum = ctx.enter_context(tc.psum_pool(name="psum", bufs=6))
+        cpool = ctx.enter_context(tc.tile_pool(name="cpool", bufs=6))
+        psum = ctx.enter_context(tc.psum_pool(name="psum", bufs=8))
 
         offs_sb = keep.tile([P, S // 16], U16, name="offs_sb")
         pos_sb = [keep.tile([P, T // 16], U16, name="pos_sb%d" % r) for r in range(4)]
@@ -81,6 +81,10 @@ def tile_moe_pre_lin_gelu_kernel(
 
         quantised = {}
 
+        def piece(u):
+            a, lo, hi = UNITS[u]
+            return MM_N if u == len(UNITS) - 1 else min(PIECE, hi - lo)
+
         def gather(u):
             a, lo, hi = UNITS[u]
             g = gpool.tile([P, PACK, hi - lo], F32, name="g")
@@ -88,8 +92,8 @@ def tile_moe_pre_lin_gelu_kernel(
                 cuts = [lo, hi]
                 if u == 0 and j == 0:
                     cuts = GATE_CUTS[:-1]
-                elif j == PACK - 1 and hi - lo > PIECE:
-                    cuts = list(range(lo, hi + 1, PIECE))
+                elif j == PACK - 1:
+                    cuts = list(range(lo, hi + 1, piece(u)))
                 for c0, c1 in zip(cuts[:-1], cuts[1:]):
                     nc.vector.tensor_tensor(
                         g[:, j, c0 - lo : c1 - lo],
@@ -101,8 +105,8 @@ def tile_moe_pre_lin_gelu_kernel(
 
         def quantise(u, g):
             a, lo, hi = UNITS[u]
-            for c0 in range(lo, hi, PIECE):
-                w = min(PIECE, hi - c0)
+            w = piece(u)
+            for c0 in range(lo, hi, w):
                 xb = xpool.tile([P, w * PACK], BF16, name="xb", align_bytes=64)
                 nc.scalar.copy(
                     xb[:].rearrange("p (c i t) -> p c t i", i=4, t=PACK),
@@ -117,9 +121,10 @@ def tile_moe_pre_lin_gelu_kernel(
         def multiply(u):
             a_last, lo, hi = UNITS[u]
             if a_last != PASSES - 1:
-                return
-            for c0 in range(lo, hi, BANK):
-                w = min(BANK, hi - c0)
+                return []
+            banks = []
+            w = min(BANK, piece(u))
+            for c0 in range(lo, hi, w):
                 acc = psum.tile([P, w], F32, name="acc")
                 for m0 in range(c0, c0 + w, MM_N):
                     e = m0 // C
@@ -135,6 +140,11 @@ def tile_moe_pre_lin_gelu_kernel(
                             start=(a == 0),
                             stop=(a == PASSES - 1),
                         )
+                banks.append((acc, c0, w))
+            return banks
+
+        def activate(banks):
+            for acc, c0, w in banks:
                 for e0 in range(c0, c0 + w, C):
                     we = min(C, c0 + w - e0)
                     e = e0 // C
@@ -143,36 +153,34 @@ def tile_moe_pre_lin_gelu_kernel(
                     )
 
         g_prev = gather(0)
-        for u in range(1, len(UNITS)):
-            g_next = gather(u)
+        banks = []
+        for u in range(1, len(UNITS) + 1):
+            g_next = gather(u) if u < len(UNITS) else None
             quantise(u - 1, g_prev)
-            multiply(u - 1)
+            activate(banks)
+            banks = multiply(u - 1)
             g_prev = g_next
-        quantise(len(UNITS) - 1, g_prev)
-        multiply(len(UNITS) - 1)
+        activate(banks)
 
         back = gpool.tile([P, 4, T], F32, name="g")
         acc_sb = xpool.tile([P, 3, T], F32, name="xb", align_bytes=64)
 
-        def fetch(r, h):
-            cols = slice(h * HALF, (h + 1) * HALF)
-            nc.vector.tensor_copy(back[:, r, cols], y[:].indirect(pos_sb[r][:, h * HALF // 16 : (h + 1) * HALF // 16]))
+        def add(engine, r, lo, hi):
+            first = back[:, 0, lo:hi] if r == 1 else acc_sb[:, r - 2, lo:hi]
+            engine.tensor_tensor(acc_sb[:, r - 1, lo:hi], first, back[:, r, lo:hi], ADD)
 
-        def add(r, h):
-            cols = slice(h * HALF, (h + 1) * HALF)
-            first = back[:, 0, cols] if r == 1 else acc_sb[:, r - 2, cols]
-            nc.vector.tensor_tensor(acc_sb[:, r - 1, cols], first, back[:, r, cols], ADD)
+        def fetch(r, lo):
+            nc.vector.tensor_copy(back[:, r, lo : lo + HALF], y[:].indirect(pos_sb[r][:, lo // 16 : (lo + HALF) // 16]))
 
-        for h in range(T // HALF):
-            fetch(0, h)
-            if h > 0:
-                add(3, h - 1)
-                nc.sync.dma_start(out[:, (h - 1) * HALF : h * HALF], acc_sb[:, 2, (h - 1) * HALF : h * HALF])
-            fetch(1, h)
-            fetch(2, h)
-            add(1, h)
-            fetch(3, h)
-            add(2, h)
-        h = T // HALF - 1
-        add(3, h)
-        nc.sync.dma_start(out[:, h * HALF : T], acc_sb[:, 2, h * HALF : T])
+        for lo in range(0, T, HALF):
+            fetch(0, lo)
+            fetch(1, lo)
+            add(nc.gpsimd, 1, lo, lo + HALF)
+        for lo in range(0, T, HALF):
+            fetch(2, lo)
+            add(nc.gpsimd, 2, lo, lo + HALF)
+        for lo in range(0, T, HALF):
+            fetch(3, lo)
+        for queue, lo, hi in ((nc.sync, 0, HALF), (nc.scalar, HALF, T - HALF // 2), (nc.sync, T - HALF // 2, T)):
+            add(nc.vector, 3, lo, hi)
+            queue.dma_start(out[:, lo:hi], acc_sb[:, 2, lo:hi])

@@ -29,8 +29,9 @@ BANK = 512
 
 UNITS = [(0, 0, 2048), (1, 0, 2048), (0, 2048, 3072), (0, 3072, 4096), (1, 2048, 3072), (1, 3072, 3584),
          (1, 3584, 3840), (1, 3840, 4096)]
-GATE_CUTS = [0, 256, 1024, 2048, 4096]
+GATE_CUTS = [0, 128, 384, 896, 2048, 4096]
 HALF = 512
+QUARTER = 256
 
 
 def tile_moe_pre_lin_gelu_kernel(
@@ -40,7 +41,7 @@ def tile_moe_pre_lin_gelu_kernel(
     with ExitStack() as ctx:
         keep = ctx.enter_context(tc.tile_pool(name="keep", bufs=1))
         gpool = ctx.enter_context(tc.tile_pool(name="gpool", bufs=2))
-        xpool = ctx.enter_context(tc.tile_pool(name="xpool", bufs=2))
+        xpool = ctx.enter_context(tc.tile_pool(name="xpool", bufs=3))
         cpool = ctx.enter_context(tc.tile_pool(name="cpool", bufs=6))
         psum = ctx.enter_context(tc.psum_pool(name="psum", bufs=8))
 
@@ -57,8 +58,8 @@ def tile_moe_pre_lin_gelu_kernel(
 
         nc.vector.memset(ws_sb[:].bitcast(I32), 0)
 
-        nc.sync.dma_start(offs_sb[:], offs)
         nc.sync.dma_start(windows[0][0][:, 0:T], x_rows[0, 0])
+        nc.sync.dma_start(offs_sb[:], offs)
         for lo, hi in zip(GATE_CUTS[:-2], GATE_CUTS[1:-1]):
             nc.sync.dma_start(gate_sb[:, lo:hi], gate[0:P, lo:hi])
         for a in range(PASSES):
@@ -108,7 +109,8 @@ def tile_moe_pre_lin_gelu_kernel(
             w = piece(u)
             for c0 in range(lo, hi, w):
                 xb = xpool.tile([P, w * PACK], BF16, name="xb", align_bytes=64)
-                nc.scalar.copy(
+                interleave = nc.vector.tensor_copy if c0 + w == S and a == PASSES - 1 else nc.scalar.copy
+                interleave(
                     xb[:].rearrange("p (c i t) -> p c t i", i=4, t=PACK),
                     g[:, :, c0 - lo : c0 - lo + w].rearrange("p t (c i) -> p c t i", i=4),
                 )
@@ -163,7 +165,7 @@ def tile_moe_pre_lin_gelu_kernel(
         activate(banks)
 
         back = gpool.tile([P, 4, T], F32, name="g")
-        acc_sb = xpool.tile([P, 3, T], F32, name="xb", align_bytes=64)
+        acc_sb = gpool.tile([P, 3, T], F32, name="g")
 
         def add(engine, r, lo, hi):
             first = back[:, 0, lo:hi] if r == 1 else acc_sb[:, r - 2, lo:hi]
@@ -172,6 +174,11 @@ def tile_moe_pre_lin_gelu_kernel(
         def fetch(r, lo):
             nc.vector.tensor_copy(back[:, r, lo : lo + HALF], y[:].indirect(pos_sb[r][:, lo // 16 : (lo + HALF) // 16]))
 
+        def finish(engine, queue, lo):
+            hi = lo + QUARTER
+            add(engine, 3, lo, hi)
+            queue.dma_start(out[:, lo:hi], acc_sb[:, 2, lo:hi])
+
         for lo in range(0, T, HALF):
             fetch(0, lo)
             fetch(1, lo)
@@ -179,8 +186,9 @@ def tile_moe_pre_lin_gelu_kernel(
         for lo in range(0, T, HALF):
             fetch(2, lo)
             add(nc.gpsimd, 2, lo, lo + HALF)
-        for lo in range(0, T, HALF):
-            fetch(3, lo)
-        for queue, lo, hi in ((nc.sync, 0, HALF), (nc.scalar, HALF, T - HALF // 2), (nc.sync, T - HALF // 2, T)):
-            add(nc.vector, 3, lo, hi)
-            queue.dma_start(out[:, lo:hi], acc_sb[:, 2, lo:hi])
+        fetch(3, 0)
+        finish(nc.gpsimd, nc.scalar, 0)
+        fetch(3, HALF)
+        finish(nc.vector, nc.sync, QUARTER)
+        finish(nc.vector, nc.scalar, 2 * QUARTER)
+        finish(nc.vector, nc.sync, 3 * QUARTER)

@@ -27,11 +27,12 @@ PIECE = 1024
 MM_N = 128
 BANK = 512
 
-UNITS = [(0, 0, 2048), (1, 0, 2048), (0, 2048, 3072), (0, 3072, 4096), (1, 2048, 3072), (1, 3072, 3584),
+UNITS = [(0, 0, 2048), (1, 0, 2048), (0, 2048, 4096), (1, 2048, 3072), (1, 3072, 3584),
          (1, 3584, 3840), (1, 3840, 4096)]
 GATE_CUTS = [0, 128, 384, 896, 2048, 4096]
 HALF = 512
 QUARTER = 256
+EIGHTH = 128
 
 
 def tile_moe_pre_lin_gelu_kernel(
@@ -93,7 +94,7 @@ def tile_moe_pre_lin_gelu_kernel(
                 cuts = [lo, hi]
                 if u == 0 and j == 0:
                     cuts = GATE_CUTS[:-1]
-                elif j == PACK - 1:
+                elif j == PACK - 1 and u > 0:
                     cuts = list(range(lo, hi + 1, piece(u)))
                 for c0, c1 in zip(cuts[:-1], cuts[1:]):
                     nc.vector.tensor_tensor(
@@ -174,8 +175,8 @@ def tile_moe_pre_lin_gelu_kernel(
         def fetch(r, lo):
             nc.vector.tensor_copy(back[:, r, lo : lo + HALF], y[:].indirect(pos_sb[r][:, lo // 16 : (lo + HALF) // 16]))
 
-        def finish(engine, queue, lo):
-            hi = lo + QUARTER
+        def finish(engine, queue, lo, width=QUARTER):
+            hi = lo + width
             add(engine, 3, lo, hi)
             queue.dma_start(out[:, lo:hi], acc_sb[:, 2, lo:hi])
 
@@ -191,4 +192,5 @@ def tile_moe_pre_lin_gelu_kernel(
         fetch(3, HALF)
         finish(nc.vector, nc.sync, QUARTER)
         finish(nc.vector, nc.scalar, 2 * QUARTER)
-        finish(nc.vector, nc.sync, 3 * QUARTER)
+        finish(nc.vector, nc.sync, 3 * QUARTER, EIGHTH)
+        finish(nc.vector, nc.scalar, 3 * QUARTER + EIGHTH, EIGHTH)

@@ -31,7 +31,6 @@ UNITS = [(0, 0, 2048), (1, 0, 2048), (0, 2048, 4096), (1, 2048, 3072), (1, 3072,
          (1, 3584, 3840), (1, 3840, 4096)]
 GATE_CUTS = [0, 128, 384, 896, 2048, 4096]
 HALF = 512
-QUARTER = 256
 EIGHTH = 128
 
 
@@ -94,7 +93,7 @@ def tile_moe_pre_lin_gelu_kernel(
                 cuts = [lo, hi]
                 if u == 0 and j == 0:
                     cuts = GATE_CUTS[:-1]
-                elif j == PACK - 1 and u > 0:
+                elif j == PACK - 1 and u == len(UNITS) - 1:
                     cuts = list(range(lo, hi + 1, piece(u)))
                 for c0, c1 in zip(cuts[:-1], cuts[1:]):
                     nc.vector.tensor_tensor(
@@ -108,6 +107,7 @@ def tile_moe_pre_lin_gelu_kernel(
         def quantise(u, g):
             a, lo, hi = UNITS[u]
             w = piece(u)
+            rounded = []
             for c0 in range(lo, hi, w):
                 xb = xpool.tile([P, w * PACK], BF16, name="xb", align_bytes=64)
                 interleave = nc.vector.tensor_copy if c0 + w == S and a == PASSES - 1 else nc.scalar.copy
@@ -115,6 +115,8 @@ def tile_moe_pre_lin_gelu_kernel(
                     xb[:].rearrange("p (c i t) -> p c t i", i=4, t=PACK),
                     g[:, :, c0 - lo : c0 - lo + w].rearrange("p t (c i) -> p c t i", i=4),
                 )
+                rounded.append((c0, xb))
+            for c0, xb in rounded:
                 codes = cpool.tile([P, w], U32, name="codes", align_bytes=64)
                 scales = cpool.tile([P, w], U8, name="scales", align_bytes=64)
                 nc.vector.quantize_mx(out=codes[:].bitcast(FP8X4), scales=scales[:], in_=xb[:])
@@ -165,32 +167,18 @@ def tile_moe_pre_lin_gelu_kernel(
             g_prev = g_next
         activate(banks)
 
-        back = gpool.tile([P, 4, T], F32, name="g")
-        acc_sb = gpool.tile([P, 3, T], F32, name="g")
+        sums = gpool.tile([P, 4, T], F32, name="g")
 
-        def add(engine, r, lo, hi):
-            first = back[:, 0, lo:hi] if r == 1 else acc_sb[:, r - 2, lo:hi]
-            engine.tensor_tensor(acc_sb[:, r - 1, lo:hi], first, back[:, r, lo:hi], ADD)
+        def fetch(r, lo, hi):
+            picked = y[:].indirect(pos_sb[r][:, lo // 16 : hi // 16])
+            if r == 0:
+                nc.vector.tensor_copy(sums[:, 0, lo:hi], picked)
+            else:
+                nc.vector.tensor_tensor(sums[:, r, lo:hi], picked, sums[:, r - 1, lo:hi], ADD)
 
-        def fetch(r, lo):
-            nc.vector.tensor_copy(back[:, r, lo : lo + HALF], y[:].indirect(pos_sb[r][:, lo // 16 : (lo + HALF) // 16]))
-
-        def finish(engine, queue, lo, width=QUARTER):
-            hi = lo + width
-            add(engine, 3, lo, hi)
-            queue.dma_start(out[:, lo:hi], acc_sb[:, 2, lo:hi])
-
-        for lo in range(0, T, HALF):
-            fetch(0, lo)
-            fetch(1, lo)
-            add(nc.gpsimd, 1, lo, lo + HALF)
-        for lo in range(0, T, HALF):
-            fetch(2, lo)
-            add(nc.gpsimd, 2, lo, lo + HALF)
-        fetch(3, 0)
-        finish(nc.gpsimd, nc.scalar, 0)
-        fetch(3, HALF)
-        finish(nc.vector, nc.sync, QUARTER)
-        finish(nc.vector, nc.scalar, 2 * QUARTER)
-        finish(nc.vector, nc.sync, 3 * QUARTER, EIGHTH)
-        finish(nc.vector, nc.scalar, 3 * QUARTER + EIGHTH, EIGHTH)
+        for r in range(3):
+            for lo in range(0, T, HALF):
+                fetch(r, lo, lo + HALF)
+        for lo, hi, queue in ((0, HALF, nc.sync), (HALF, T - EIGHTH, nc.scalar), (T - EIGHTH, T, nc.sync)):
+            fetch(3, lo, hi)
+            queue.dma_start(out[:, lo:hi], sums[:, 3, lo:hi])

@@ -28,7 +28,7 @@ MM_N = 128
 BANK = 512
 
 UNITS = [(0, 0, 2048), (1, 0, 2048), (0, 2048, 4096), (1, 2048, 3072), (1, 3072, 3584),
-         (1, 3584, 3840), (1, 3840, 4096)]
+         (1, 3584, 3968), (1, 3968, 4096)]
 GATE_CUTS = [0, 128, 384, 896, 2048, 4096]
 HALF = 512
 EIGHTH = 128
@@ -82,19 +82,21 @@ def tile_moe_pre_lin_gelu_kernel(
 
         quantised = {}
 
-        def piece(u):
-            a, lo, hi = UNITS[u]
-            return MM_N if u == len(UNITS) - 1 else min(PIECE, hi - lo)
+        def pieces(lo, hi, widest):
+            cuts = []
+            while lo < hi:
+                w = widest
+                while lo + w > hi:
+                    w = w // 2
+                cuts.append((lo, lo + w))
+                lo = lo + w
+            return cuts
 
         def gather(u):
             a, lo, hi = UNITS[u]
-            g = gpool.tile([P, PACK, hi - lo], F32, name="g")
+            g = gpool.tile([P, PACK, hi - lo], F32, name="g", align_bytes=64)
             for j in range(PACK):
-                cuts = [lo, hi]
-                if u == 0 and j == 0:
-                    cuts = GATE_CUTS[:-1]
-                elif j == PACK - 1 and u == len(UNITS) - 1:
-                    cuts = list(range(lo, hi + 1, piece(u)))
+                cuts = GATE_CUTS[:-1] if u == 0 and j == 0 else [lo, hi]
                 for c0, c1 in zip(cuts[:-1], cuts[1:]):
                     nc.vector.tensor_tensor(
                         g[:, j, c0 - lo : c1 - lo],
@@ -104,34 +106,37 @@ def tile_moe_pre_lin_gelu_kernel(
                     )
             return g
 
-        def quantise(u, g):
+        def interleave(u, g, into=None):
             a, lo, hi = UNITS[u]
-            w = piece(u)
+            move = nc.scalar.copy if into is None else nc.vector.tensor_copy
             rounded = []
-            for c0 in range(lo, hi, w):
-                xb = xpool.tile([P, w * PACK], BF16, name="xb", align_bytes=64)
-                interleave = nc.vector.tensor_copy if c0 + w == S and a == PASSES - 1 else nc.scalar.copy
-                interleave(
-                    xb[:].rearrange("p (c i t) -> p c t i", i=4, t=PACK),
-                    g[:, :, c0 - lo : c0 - lo + w].rearrange("p t (c i) -> p c t i", i=4),
+            for c0, c1 in pieces(lo, hi, PIECE):
+                if into is None:
+                    xb = xpool.tile([P, (c1 - c0) * PACK], BF16, name="xb", align_bytes=64)
+                    xb = xb[:]
+                else:
+                    xb = into
+                move(
+                    xb.rearrange("p (c i t) -> p c t i", i=4, t=PACK),
+                    g[:, :, c0 - lo : c1 - lo].rearrange("p t (c i) -> p c t i", i=4),
                 )
-                rounded.append((c0, xb))
-            for c0, xb in rounded:
-                codes = cpool.tile([P, w], U32, name="codes", align_bytes=64)
-                scales = cpool.tile([P, w], U8, name="scales", align_bytes=64)
-                nc.vector.quantize_mx(out=codes[:].bitcast(FP8X4), scales=scales[:], in_=xb[:])
-                for m0 in range(c0, c0 + w, MM_N):
-                    quantised[(a, m0)] = (codes, scales, m0 - c0)
+                rounded.append((a, c0, c1, xb))
+            return rounded
 
-        def multiply(u):
-            a_last, lo, hi = UNITS[u]
+        def quantise(a, c0, c1, xb):
+            codes = cpool.tile([P, c1 - c0], U32, name="codes", align_bytes=64)
+            scales = cpool.tile([P, c1 - c0], U8, name="scales", align_bytes=64)
+            nc.vector.quantize_mx(out=codes[:].bitcast(FP8X4), scales=scales[:], in_=xb)
+            for m0 in range(c0, c1, MM_N):
+                quantised[(a, m0)] = (codes, scales, m0 - c0)
+
+        def multiply(a_last, lo, hi):
             if a_last != PASSES - 1:
                 return []
             banks = []
-            w = min(BANK, piece(u))
-            for c0 in range(lo, hi, w):
-                acc = psum.tile([P, w], F32, name="acc")
-                for m0 in range(c0, c0 + w, MM_N):
+            for c0, c1 in pieces(lo, hi, BANK):
+                acc = psum.tile([P, c1 - c0], F32, name="acc")
+                for m0 in range(c0, c1, MM_N):
                     e = m0 // C
                     for a in range(PASSES):
                         codes, scales, at = quantised[(a, m0)]
@@ -145,29 +150,37 @@ def tile_moe_pre_lin_gelu_kernel(
                             start=(a == 0),
                             stop=(a == PASSES - 1),
                         )
-                banks.append((acc, c0, w))
+                banks.append((acc, c0, c1))
             return banks
 
         def activate(banks):
-            for acc, c0, w in banks:
-                for e0 in range(c0, c0 + w, C):
-                    we = min(C, c0 + w - e0)
+            for acc, c0, c1 in banks:
+                for e0, e1 in pieces(c0, c1, C):
                     e = e0 // C
                     nc.scalar.activation(
-                        y[:, e0 : e0 + we], acc[:, e0 - c0 : e0 - c0 + we], GELU, bias=b_sb[:, e : e + 1]
+                        y[:, e0:e1], acc[:, e0 - c0 : e1 - c0], GELU, bias=b_sb[:, e : e + 1]
                     )
 
+        last = len(UNITS) - 1
         g_prev = gather(0)
         banks = []
-        for u in range(1, len(UNITS) + 1):
-            g_next = gather(u) if u < len(UNITS) else None
-            quantise(u - 1, g_prev)
+        for u in range(1, last):
+            g_next = gather(u)
+            for a, c0, c1, xb in interleave(u - 1, g_prev):
+                quantise(a, c0, c1, xb)
             activate(banks)
-            banks = multiply(u - 1)
+            banks = multiply(*UNITS[u - 1])
             g_prev = g_next
+        g_last = gather(last)
+        before = interleave(last - 1, g_prev)
         activate(banks)
+        quantise(*before[0])
+        final = interleave(last, g_last, g_prev[:, 0, 0 : 2 * MM_N].bitcast(BF16))
+        for item in before[1:] + final:
+            quantise(*item)
+        activate(multiply(*UNITS[last - 1]) + multiply(*UNITS[last]))
 
-        sums = gpool.tile([P, 4, T], F32, name="g")
+        sums = gpool.tile([P, 4, T], F32, name="g", align_bytes=64)
 
         def fetch(r, lo, hi):
             picked = y[:].indirect(pos_sb[r][:, lo // 16 : hi // 16])

@@ -58,9 +58,10 @@ def tile_moe_pre_lin_gelu_kernel(
 
         nc.vector.memset(ws_sb[:].bitcast(I32), 0)
 
-        nc.sync.dma_start(windows[0][0][:, 0:T], x_rows[0, 0])
         nc.sync.dma_start(offs_sb[:], offs)
-        for lo, hi in zip(GATE_CUTS[:-2], GATE_CUTS[1:-1]):
+        nc.scalar.dma_start(gate_sb[:, 0 : GATE_CUTS[1]], gate[0:P, 0 : GATE_CUTS[1]])
+        nc.sync.dma_start(windows[0][0][:, 0:T], x_rows[0, 0])
+        for lo, hi in zip(GATE_CUTS[1:-2], GATE_CUTS[2:-1]):
             nc.sync.dma_start(gate_sb[:, lo:hi], gate[0:P, lo:hi])
         for a in range(PASSES):
             for j in range(PACK):

@@ -58,9 +58,9 @@ def tile_moe_pre_lin_gelu_kernel(
 
         nc.vector.memset(ws_sb[:].bitcast(I32), 0)
 
-        nc.sync.dma_start(offs_sb[:], offs)
-        nc.scalar.dma_start(gate_sb[:, 0 : GATE_CUTS[1]], gate[0:P, 0 : GATE_CUTS[1]])
         nc.sync.dma_start(windows[0][0][:, 0:T], x_rows[0, 0])
+        nc.scalar.dma_start(gate_sb[:, 0 : GATE_CUTS[1]], gate[0:P, 0 : GATE_CUTS[1]])
+        nc.sync.dma_start(offs_sb[:], offs)
         for lo, hi in zip(GATE_CUTS[1:-2], GATE_CUTS[2:-1]):
             nc.sync.dma_start(gate_sb[:, lo:hi], gate[0:P, lo:hi])
         for a in range(PASSES):

@@ -30,6 +30,7 @@ BANK = 512
 UNITS = [(0, 0, 2048), (1, 0, 2048), (0, 2048, 4096), (1, 2048, 3072), (1, 3072, 3584),
          (1, 3584, 3968), (1, 3968, 4096)]
 GATE_CUTS = [0, 128, 384, 896, 2048, 4096]
+FIRST_SPLIT = 768
 HALF = 512
 EIGHTH = 128
 
@@ -58,9 +59,10 @@ def tile_moe_pre_lin_gelu_kernel(
 
         nc.vector.memset(ws_sb[:].bitcast(I32), 0)
 
-        nc.sync.dma_start(windows[0][0][:, 0:T], x_rows[0, 0])
-        nc.scalar.dma_start(gate_sb[:, 0 : GATE_CUTS[1]], gate[0:P, 0 : GATE_CUTS[1]])
+        nc.scalar.dma_start(windows[0][0][:, 0:FIRST_SPLIT], x_rows[0, 0][:, 0:FIRST_SPLIT])
         nc.sync.dma_start(offs_sb[:], offs)
+        nc.sync.dma_start(gate_sb[:, 0 : GATE_CUTS[1]], gate[0:P, 0 : GATE_CUTS[1]])
+        nc.sync.dma_start(windows[0][0][:, FIRST_SPLIT:T], x_rows[0, 0][:, FIRST_SPLIT:T])
         for lo, hi in zip(GATE_CUTS[1:-2], GATE_CUTS[2:-1]):
             nc.sync.dma_start(gate_sb[:, lo:hi], gate[0:P, lo:hi])
         for a in range(PASSES):

@@ -4,6 +4,7 @@ import concourse.mybir as mybir
 
 K, T, E, C, N = 1024, 1024, 16, 256, 128
 S = E * C
+TOP = 4
 FLOPS = 2 * K * N * S
 
 F32 = mybir.dt.float32
@@ -21,6 +22,7 @@ GELU = mybir.ActivationFunctionType.Gelu_apprx_tanh
 P = 128
 PACK = 4
 PASSES = K // (P * PACK)
+LIST = 16
 WIDE = 2048
 WINDOW = WIDE + 32
 PIECE = 1024
@@ -31,8 +33,8 @@ UNITS = [(0, 0, 2048), (1, 0, 2048), (0, 2048, 4096), (1, 2048, 3072), (1, 3072,
          (1, 3584, 3968), (1, 3968, 4096)]
 GATE_CUTS = [0, 128, 384, 896, 2048, 4096]
 FIRST_SPLIT = 768
-HALF = 512
-EIGHTH = 128
+HALF = T // 2
+LAST_STORE = 128
 
 
 def tile_moe_pre_lin_gelu_kernel(
@@ -46,18 +48,20 @@ def tile_moe_pre_lin_gelu_kernel(
         cpool = ctx.enter_context(tc.tile_pool(name="cpool", bufs=6))
         psum = ctx.enter_context(tc.psum_pool(name="psum", bufs=8))
 
-        offs_sb = keep.tile([P, S // 16], U16, name="offs_sb")
-        pos_sb = [keep.tile([P, T // 16], U16, name="pos_sb%d" % r) for r in range(4)]
-        windows = [[keep.tile([P, WINDOW], F32, name="win%d_%d" % (a, j)) for j in range(PACK)] for a in range(PASSES)]
+        offs_sb = keep.tile([P, S // LIST], U16, name="offs_sb")
+        pos_sb = [keep.tile([P, T // LIST], U16, name="pos_sb%d" % r) for r in range(TOP)]
+        windows = [[keep.tile([P, WINDOW], F32, name="win%d_%d" % (a, t)) for t in range(PACK)] for a in range(PASSES)]
         gate_sb = keep.tile([P, S], F32, name="gate_sb")
         w_sb = keep.tile([P, E * PASSES * 2 * N], U8, name="w_sb", align_bytes=64)
         ws_sb = keep.tile([P, E * PASSES * N], U8, name="ws_sb", align_bytes=64)
         b_sb = keep.tile([P, E], F32, name="b_sb")
         y = keep.tile([P, S], F32, name="y")
+        zeros = keep.tile([P, HALF], F32, name="zeros")
 
-        x_rows = xT.rearrange("(a p j) t -> a j p t", a=PASSES, j=PACK)
+        x_rows = xT.rearrange("(a p t) c -> a t p c", a=PASSES, t=PACK)
 
         nc.vector.memset(ws_sb[:].bitcast(I32), 0)
+        nc.vector.memset(zeros[:], 0.0)
 
         nc.scalar.dma_start(windows[0][0][:, 0:FIRST_SPLIT], x_rows[0, 0][:, 0:FIRST_SPLIT])
         nc.sync.dma_start(offs_sb[:], offs)
@@ -66,10 +70,10 @@ def tile_moe_pre_lin_gelu_kernel(
         for lo, hi in zip(GATE_CUTS[1:-2], GATE_CUTS[2:-1]):
             nc.sync.dma_start(gate_sb[:, lo:hi], gate[0:P, lo:hi])
         for a in range(PASSES):
-            for j in range(PACK):
-                if (a, j) != (0, 0):
-                    nc.sync.dma_start(windows[a][j][:, 0:T], x_rows[a, j])
-        nc.sync.dma_start(gate_sb[:, GATE_CUTS[-2]:S], gate[0:P, GATE_CUTS[-2]:S])
+            for t in range(PACK):
+                if (a, t) != (0, 0):
+                    nc.sync.dma_start(windows[a][t][:, 0:T], x_rows[a, t])
+        nc.sync.dma_start(gate_sb[:, GATE_CUTS[-2] : S], gate[0:P, GATE_CUTS[-2] : S])
         nc.sync.dma_start(
             w_sb[:].bitcast(I32).rearrange("p (g n) -> p g n", g=E * PASSES),
             w_words.rearrange("e a p n -> p (e a) n").bitcast(I32),
@@ -88,42 +92,40 @@ def tile_moe_pre_lin_gelu_kernel(
         def pieces(lo, hi, widest):
             cuts = []
             while lo < hi:
-                w = widest
-                while lo + w > hi:
-                    w = w // 2
-                cuts.append((lo, lo + w))
-                lo = lo + w
+                width = widest
+                while lo + width > hi:
+                    width = width // 2
+                cuts.append((lo, lo + width))
+                lo = lo + width
             return cuts
 
         def gather(u):
             a, lo, hi = UNITS[u]
             g = gpool.tile([P, PACK, hi - lo], F32, name="g", align_bytes=64)
-            for j in range(PACK):
-                cuts = GATE_CUTS[:-1] if u == 0 and j == 0 else [lo, hi]
+            for t in range(PACK):
+                cuts = GATE_CUTS[:-1] if (u, t) == (0, 0) else [lo, hi]
                 for c0, c1 in zip(cuts[:-1], cuts[1:]):
                     nc.vector.tensor_tensor(
-                        g[:, j, c0 - lo : c1 - lo],
-                        windows[a][j][:].indirect(offs_sb[:, c0 // 16 : c1 // 16]),
+                        g[:, t, c0 - lo : c1 - lo],
+                        windows[a][t][:].indirect(offs_sb[:, c0 // LIST : c1 // LIST]),
                         gate_sb[:, c0:c1],
                         MULT,
                     )
             return g
 
-        def interleave(u, g, into=None):
+        def interleave(move, xb, planes):
+            move(
+                xb.rearrange("p (c i t) -> p c t i", i=4, t=PACK),
+                planes.rearrange("p t (c i) -> p c t i", i=4),
+            )
+
+        def interleave_unit(u, g):
             a, lo, hi = UNITS[u]
-            move = nc.scalar.copy if into is None else nc.vector.tensor_copy
             rounded = []
             for c0, c1 in pieces(lo, hi, PIECE):
-                if into is None:
-                    xb = xpool.tile([P, (c1 - c0) * PACK], BF16, name="xb", align_bytes=64)
-                    xb = xb[:]
-                else:
-                    xb = into
-                move(
-                    xb.rearrange("p (c i t) -> p c t i", i=4, t=PACK),
-                    g[:, :, c0 - lo : c1 - lo].rearrange("p t (c i) -> p c t i", i=4),
-                )
-                rounded.append((a, c0, c1, xb))
+                xb = xpool.tile([P, (c1 - c0) * PACK], BF16, name="xb", align_bytes=64)
+                interleave(nc.scalar.copy, xb[:], g[:, :, c0 - lo : c1 - lo])
+                rounded.append((a, c0, c1, xb[:]))
             return rounded
 
         def quantise(a, c0, c1, xb):
@@ -133,21 +135,20 @@ def tile_moe_pre_lin_gelu_kernel(
             for m0 in range(c0, c1, MM_N):
                 quantised[(a, m0)] = (codes, scales, m0 - c0)
 
-        def multiply(a_last, lo, hi):
-            if a_last != PASSES - 1:
+        def multiply(unit_pass, lo, hi):
+            if unit_pass != PASSES - 1:
                 return []
             banks = []
             for c0, c1 in pieces(lo, hi, BANK):
                 acc = psum.tile([P, c1 - c0], F32, name="acc")
                 for m0 in range(c0, c1, MM_N):
-                    e = m0 // C
                     for a in range(PASSES):
                         codes, scales, at = quantised[(a, m0)]
-                        grp = e * PASSES + a
+                        matrix = (m0 // C) * PASSES + a
                         nc.tensor.matmul_mx(
                             out=acc[:, m0 - c0 : m0 - c0 + MM_N],
-                            lhsT=w_sb[:, grp * 2 * N : (grp + 1) * 2 * N].bitcast(FP4X4),
-                            lhsT_scale=ws_sb[:, grp * N : (grp + 1) * N],
+                            lhsT=w_sb[:, matrix * 2 * N : (matrix + 1) * 2 * N].bitcast(FP4X4),
+                            lhsT_scale=ws_sb[:, matrix * N : (matrix + 1) * N],
                             rhs=codes[:, at : at + MM_N].bitcast(FP8X4),
                             rhs_scale=scales[:, at : at + MM_N],
                             start=(a == 0),
@@ -160,41 +161,40 @@ def tile_moe_pre_lin_gelu_kernel(
             for acc, c0, c1 in banks:
                 for e0, e1 in pieces(c0, c1, C):
                     e = e0 // C
-                    nc.scalar.activation(
-                        y[:, e0:e1], acc[:, e0 - c0 : e1 - c0], GELU, bias=b_sb[:, e : e + 1]
-                    )
+                    nc.scalar.activation(y[:, e0:e1], acc[:, e0 - c0 : e1 - c0], GELU, bias=b_sb[:, e : e + 1])
 
         last = len(UNITS) - 1
         g_prev = gather(0)
         banks = []
         for u in range(1, last):
             g_next = gather(u)
-            for a, c0, c1, xb in interleave(u - 1, g_prev):
-                quantise(a, c0, c1, xb)
+            for piece in interleave_unit(u - 1, g_prev):
+                quantise(*piece)
             activate(banks)
             banks = multiply(*UNITS[u - 1])
             g_prev = g_next
+
         g_last = gather(last)
-        before = interleave(last - 1, g_prev)
+        before = interleave_unit(last - 1, g_prev)
         activate(banks)
         quantise(*before[0])
-        final = interleave(last, g_last, g_prev[:, 0, 0 : 2 * MM_N].bitcast(BF16))
-        for item in before[1:] + final:
-            quantise(*item)
+        last_pass, last_lo, last_hi = UNITS[last]
+        xb_last = g_prev[:, 0, 0 : (last_hi - last_lo) * PACK // 2].bitcast(BF16)
+        interleave(nc.vector.tensor_copy, xb_last, g_last[:])
+        quantise(*before[1])
+        quantise(last_pass, last_lo, last_hi, xb_last)
         activate(multiply(*UNITS[last - 1]) + multiply(*UNITS[last]))
 
-        sums = gpool.tile([P, 4, T], F32, name="g", align_bytes=64)
+        sums = gpool.tile([P, TOP, T], F32, name="g", align_bytes=64)
 
         def fetch(r, lo, hi):
-            picked = y[:].indirect(pos_sb[r][:, lo // 16 : hi // 16])
-            if r == 0:
-                nc.vector.tensor_copy(sums[:, 0, lo:hi], picked)
-            else:
-                nc.vector.tensor_tensor(sums[:, r, lo:hi], picked, sums[:, r - 1, lo:hi], ADD)
+            picked = y[:].indirect(pos_sb[r][:, lo // LIST : hi // LIST])
+            so_far = zeros[:] if r == 0 else sums[:, r - 1, lo:hi]
+            nc.vector.tensor_tensor(sums[:, r, lo:hi], picked, so_far, ADD)
 
-        for r in range(3):
+        for r in range(TOP - 1):
             for lo in range(0, T, HALF):
                 fetch(r, lo, lo + HALF)
-        for lo, hi, queue in ((0, HALF, nc.sync), (HALF, T - EIGHTH, nc.scalar), (T - EIGHTH, T, nc.sync)):
-            fetch(3, lo, hi)
-            queue.dma_start(out[:, lo:hi], sums[:, 3, lo:hi])
+        for lo, hi, queue in ((0, HALF, nc.sync), (HALF, T - LAST_STORE, nc.scalar), (T - LAST_STORE, T, nc.sync)):
+            fetch(TOP - 1, lo, hi)
+            queue.dma_start(out[:, lo:hi], sums[:, TOP - 1, lo:hi])

@@ -195,6 +195,6 @@ def tile_moe_pre_lin_gelu_kernel(
         for r in range(TOP - 1):
             for lo in range(0, T, HALF):
                 fetch(r, lo, lo + HALF)
-        for lo, hi, queue in ((0, HALF, nc.sync), (HALF, T - LAST_STORE, nc.scalar), (T - LAST_STORE, T, nc.sync)):
+        for lo, hi in pieces(0, T - LAST_STORE, HALF) + [(T - LAST_STORE, T)]:
             fetch(TOP - 1, lo, hi)
-            queue.dma_start(out[:, lo:hi], sums[:, TOP - 1, lo:hi])
+            nc.sync.dma_start(out[:, lo:hi], sums[:, TOP - 1, lo:hi])

@@ -29,10 +29,11 @@ PIECE = 1024
 MM_N = 128
 BANK = 512
 
-UNITS = [(0, 0, 2048), (1, 0, 2048), (0, 2048, 4096), (1, 2048, 3072), (1, 3072, 3584),
-         (1, 3584, 3968), (1, 3968, 4096)]
+UNITS = [(0, 0, 2048), (1, 0, 2048), (0, 2048, 4096), (1, 2048, 3200), (1, 3200, 3712),
+         (1, 3712, 3968), (1, 3968, 4096)]
 GATE_CUTS = [0, 128, 384, 896, 2048, 4096]
 FIRST_SPLIT = 768
+KEPT = S - 3 * C
 HALF = T // 2
 LAST_STORE = 128
 
@@ -45,12 +46,12 @@ def tile_moe_pre_lin_gelu_kernel(
         keep = ctx.enter_context(tc.tile_pool(name="keep", bufs=1))
         gpool = ctx.enter_context(tc.tile_pool(name="gpool", bufs=2))
         xpool = ctx.enter_context(tc.tile_pool(name="xpool", bufs=3))
-        cpool = ctx.enter_context(tc.tile_pool(name="cpool", bufs=6))
+        cpool = ctx.enter_context(tc.tile_pool(name="cpool", bufs=5))
         psum = ctx.enter_context(tc.psum_pool(name="psum", bufs=8))
 
         offs_sb = keep.tile([P, S // LIST], U16, name="offs_sb")
         pos_sb = [keep.tile([P, T // LIST], U16, name="pos_sb%d" % r) for r in range(TOP)]
-        windows = [[keep.tile([P, WINDOW], F32, name="win%d_%d" % (a, t)) for t in range(PACK)] for a in range(PASSES)]
+        windows = [[keep.tile([P, WINDOW], F32, name="win%d_%d" % (a, t), align_bytes=64) for t in range(PACK)] for a in range(PASSES)]
         gate_sb = keep.tile([P, S], F32, name="gate_sb")
         w_sb = keep.tile([P, E * PASSES * 2 * N], U8, name="w_sb", align_bytes=64)
         ws_sb = keep.tile([P, E * PASSES * N], U8, name="ws_sb", align_bytes=64)
@@ -122,27 +123,33 @@ def tile_moe_pre_lin_gelu_kernel(
         def interleave_unit(u, g):
             a, lo, hi = UNITS[u]
             rounded = []
-            for c0, c1 in pieces(lo, hi, PIECE):
-                xb = xpool.tile([P, (c1 - c0) * PACK], BF16, name="xb", align_bytes=64)
+            cuts = pieces(lo, KEPT, PIECE) + [(KEPT, hi)] if (a, hi) == (0, S) else pieces(lo, hi, PIECE)
+            for c0, c1 in cuts:
+                if (a, c0) == (0, KEPT):
+                    xb = keep.tile([P, (c1 - c0) * PACK], BF16, name="xb_kept", align_bytes=64)
+                else:
+                    xb = xpool.tile([P, (c1 - c0) * PACK], BF16, name="xb", align_bytes=64)
                 interleave(nc.scalar.copy, xb[:], g[:, :, c0 - lo : c1 - lo])
                 rounded.append((a, c0, c1, xb[:]))
             return rounded
 
-        def quantise(a, c0, c1, xb):
-            codes = cpool.tile([P, c1 - c0], U32, name="codes", align_bytes=64)
-            scales = cpool.tile([P, c1 - c0], U8, name="scales", align_bytes=64)
-            nc.vector.quantize_mx(out=codes[:].bitcast(FP8X4), scales=scales[:], in_=xb)
+        def quantise(a, c0, c1, xb, codes=None):
+            if codes is None:
+                codes = cpool.tile([P, c1 - c0], U32, name="codes", align_bytes=64)
+            scales = cpool.tile([P, c1 - c0], U8, name="scales", align_bytes=64, bufs=10)
+            nc.vector.quantize_mx(out=codes[:, :].bitcast(FP8X4), scales=scales[:], in_=xb)
             for m0 in range(c0, c1, MM_N):
                 quantised[(a, m0)] = (codes, scales, m0 - c0)
 
-        def multiply(unit_pass, lo, hi):
+        def multiply(unit_pass, lo, hi, widest=BANK, order=range(PASSES)):
             if unit_pass != PASSES - 1:
                 return []
             banks = []
-            for c0, c1 in pieces(lo, hi, BANK):
+            for c0 in range(lo, hi, widest):
+                c1 = min(c0 + widest, hi)
                 acc = psum.tile([P, c1 - c0], F32, name="acc")
                 for m0 in range(c0, c1, MM_N):
-                    for a in range(PASSES):
+                    for a in order:
                         codes, scales, at = quantised[(a, m0)]
                         matrix = (m0 // C) * PASSES + a
                         nc.tensor.matmul_mx(
@@ -151,15 +158,16 @@ def tile_moe_pre_lin_gelu_kernel(
                             lhsT_scale=ws_sb[:, matrix * N : (matrix + 1) * N],
                             rhs=codes[:, at : at + MM_N].bitcast(FP8X4),
                             rhs_scale=scales[:, at : at + MM_N],
-                            start=(a == 0),
-                            stop=(a == PASSES - 1),
+                            start=(a == order[0]),
+                            stop=(a == order[-1]),
                         )
                 banks.append((acc, c0, c1))
             return banks
 
         def activate(banks):
             for acc, c0, c1 in banks:
-                for e0, e1 in pieces(c0, c1, C):
+                cuts = [c0] + list(range((c0 // C + 1) * C, c1, C)) + [c1]
+                for e0, e1 in zip(cuts[:-1], cuts[1:]):
                     e = e0 // C
                     nc.scalar.activation(y[:, e0:e1], acc[:, e0 - c0 : e1 - c0], GELU, bias=b_sb[:, e : e + 1])
 
@@ -169,21 +177,27 @@ def tile_moe_pre_lin_gelu_kernel(
         for u in range(1, last):
             g_next = gather(u)
             for piece in interleave_unit(u - 1, g_prev):
-                quantise(*piece)
+                if piece[:2] == (0, KEPT):
+                    kept = piece
+                else:
+                    quantise(*piece)
             activate(banks)
-            banks = multiply(*UNITS[u - 1])
+            banks = multiply(UNITS[u - 1][0], UNITS[u - 1][1], min(UNITS[u - 1][2], KEPT))
             g_prev = g_next
 
         g_last = gather(last)
         before = interleave_unit(last - 1, g_prev)
         activate(banks)
-        quantise(*before[0])
-        last_pass, last_lo, last_hi = UNITS[last]
-        xb_last = g_prev[:, 0, 0 : (last_hi - last_lo) * PACK // 2].bitcast(BF16)
-        interleave(nc.vector.tensor_copy, xb_last, g_last[:])
-        quantise(*before[1])
-        quantise(last_pass, last_lo, last_hi, xb_last)
-        activate(multiply(*UNITS[last - 1]) + multiply(*UNITS[last]))
+        final = interleave_unit(last, g_last)
+        late = [(0, c0, c0 + C, kept[3][:, (c0 - KEPT) * PACK : (c0 - KEPT + C) * PACK]) for c0 in range(KEPT, S, C)]
+        late = late[:1] + before + late[1:] + final
+        width = sum(c1 - c0 for a, c0, c1, xb in late)
+        late_codes = keep.tile([P, width], U32, name="win%d_%d" % (PASSES - 1, PACK - 2), align_bytes=64)
+        at = 0
+        for a, c0, c1, xb in late:
+            quantise(a, c0, c1, xb, codes=late_codes[:, at : at + c1 - c0])
+            at = at + c1 - c0
+        activate(multiply(PASSES - 1, KEPT, S - MM_N, MM_N, (1, 0)) + multiply(PASSES - 1, S - MM_N, S, MM_N))
 
         sums = gpool.tile([P, TOP, T], F32, name="g", align_bytes=64)
 

@@ -29,8 +29,8 @@ PIECE = 1024
 MM_N = 128
 BANK = 512
 
-UNITS = [(0, 0, 2048), (1, 0, 2048), (0, 2048, 4096), (1, 2048, 3200), (1, 3200, 3712),
-         (1, 3712, 3968), (1, 3968, 4096)]
+UNITS = [(0, 0, 2048), (1, 0, 2048), (0, 2048, 4096), (1, 2048, 3328), (1, 3328, 3840),
+         (1, 3840, 4096)]
 GATE_CUTS = [0, 128, 384, 896, 2048, 4096]
 FIRST_SPLIT = 768
 KEPT = S - 3 * C
@@ -123,7 +123,7 @@ def tile_moe_pre_lin_gelu_kernel(
         def interleave_unit(u, g):
             a, lo, hi = UNITS[u]
             rounded = []
-            cuts = pieces(lo, KEPT, PIECE) + [(KEPT, hi)] if (a, hi) == (0, S) else pieces(lo, hi, PIECE)
+            cuts = pieces(lo, KEPT, PIECE) + [(KEPT, hi)] if (a, hi) == (0, S) else pieces(lo, hi, MM_N if u == len(UNITS) - 1 else PIECE)
             for c0, c1 in cuts:
                 if (a, c0) == (0, KEPT):
                     xb = keep.tile([P, (c1 - c0) * PACK], BF16, name="xb_kept", align_bytes=64)
@@ -190,14 +190,32 @@ def tile_moe_pre_lin_gelu_kernel(
         activate(banks)
         final = interleave_unit(last, g_last)
         late = [(0, c0, c0 + C, kept[3][:, (c0 - KEPT) * PACK : (c0 - KEPT + C) * PACK]) for c0 in range(KEPT, S, C)]
-        late = late[:1] + before + late[1:] + final
+        late = [late[0], before[0], late[1], final[0], late[2], final[1]]
         width = sum(c1 - c0 for a, c0, c1, xb in late)
         late_codes = keep.tile([P, width], U32, name="win%d_%d" % (PASSES - 1, PACK - 2), align_bytes=64)
         at = 0
         for a, c0, c1, xb in late:
             quantise(a, c0, c1, xb, codes=late_codes[:, at : at + c1 - c0])
             at = at + c1 - c0
-        activate(multiply(PASSES - 1, KEPT, S - MM_N, MM_N, (1, 0)) + multiply(PASSES - 1, S - MM_N, S, MM_N))
+        shared = []
+        for c0 in range(KEPT, S - C, C):
+            acc = psum.tile([P, C], F32, name="acc")
+            order = (0, 1) if c0 == KEPT else (1, 0)
+            for a in order:
+                for m0 in range(c0, c0 + C, MM_N):
+                    codes, scales, at = quantised[(a, m0)]
+                    matrix = (m0 // C) * PASSES + a
+                    nc.tensor.matmul_mx(
+                        out=acc[:, m0 - c0 : m0 - c0 + MM_N],
+                        lhsT=w_sb[:, matrix * 2 * N : (matrix + 1) * 2 * N].bitcast(FP4X4),
+                        lhsT_scale=ws_sb[:, matrix * N : (matrix + 1) * N],
+                        rhs=codes[:, at : at + MM_N].bitcast(FP8X4),
+                        rhs_scale=scales[:, at : at + MM_N],
+                        start=(a == order[0] and m0 == c0),
+                        stop=(a == order[1] and m0 == c0 + C - MM_N),
+                    )
+            shared.append((acc, c0, c0 + C))
+        activate(shared + multiply(PASSES - 1, S - C, S - MM_N, MM_N, (1, 0)) + multiply(PASSES - 1, S - MM_N, S, MM_N))
 
         sums = gpool.tile([P, TOP, T], F32, name="g", align_bytes=64)
 

@@ -34,6 +34,7 @@ UNITS = [(0, 0, 2048), (1, 0, 2048), (0, 2048, 4096), (1, 2048, 3328), (1, 3328,
 GATE_CUTS = [0, 128, 384, 896, 2048, 4096]
 FIRST_SPLIT = 768
 KEPT = S - 3 * C
+WARM_UPS = 2
 HALF = T // 2
 LAST_STORE = 128
 
@@ -141,35 +142,27 @@ def tile_moe_pre_lin_gelu_kernel(
             for m0 in range(c0, c1, MM_N):
                 quantised[(a, m0)] = (codes, scales, m0 - c0)
 
-        def multiply(unit_pass, lo, hi, widest=BANK, order=range(PASSES)):
-            if unit_pass != PASSES - 1:
-                return []
-            banks = []
-            for c0 in range(lo, hi, widest):
-                c1 = min(c0 + widest, hi)
-                acc = psum.tile([P, c1 - c0], F32, name="acc")
-                for m0 in range(c0, c1, MM_N):
-                    for a in order:
-                        codes, scales, at = quantised[(a, m0)]
-                        matrix = (m0 // C) * PASSES + a
-                        nc.tensor.matmul_mx(
-                            out=acc[:, m0 - c0 : m0 - c0 + MM_N],
-                            lhsT=w_sb[:, matrix * 2 * N : (matrix + 1) * 2 * N].bitcast(FP4X4),
-                            lhsT_scale=ws_sb[:, matrix * N : (matrix + 1) * N],
-                            rhs=codes[:, at : at + MM_N].bitcast(FP8X4),
-                            rhs_scale=scales[:, at : at + MM_N],
-                            start=(a == order[0]),
-                            stop=(a == order[-1]),
-                        )
-                banks.append((acc, c0, c1))
-            return banks
+        def multiply(lo, hi, order):
+            acc = psum.tile([P, hi - lo], F32, name="acc")
+            steps = [(a, m0) for a in order for m0 in range(lo, hi, MM_N)]
+            for a, m0 in steps:
+                codes, scales, at = quantised[(a, m0)]
+                matrix = (m0 // C) * PASSES + a
+                nc.tensor.matmul_mx(
+                    out=acc[:, m0 - lo : m0 - lo + MM_N],
+                    lhsT=w_sb[:, matrix * 2 * N : (matrix + 1) * 2 * N].bitcast(FP4X4),
+                    lhsT_scale=ws_sb[:, matrix * N : (matrix + 1) * N],
+                    rhs=codes[:, at : at + MM_N].bitcast(FP8X4),
+                    rhs_scale=scales[:, at : at + MM_N],
+                    start=((a, m0) == steps[0]),
+                    stop=((a, m0) == steps[-1]),
+                )
+            return acc, lo, hi
 
         def activate(banks):
-            for acc, c0, c1 in banks:
-                cuts = [c0] + list(range((c0 // C + 1) * C, c1, C)) + [c1]
-                for e0, e1 in zip(cuts[:-1], cuts[1:]):
-                    e = e0 // C
-                    nc.scalar.activation(y[:, e0:e1], acc[:, e0 - c0 : e1 - c0], GELU, bias=b_sb[:, e : e + 1])
+            for acc, lo, hi in banks:
+                e = lo // C
+                nc.scalar.activation(y[:, lo:hi], acc[:], GELU, bias=b_sb[:, e : e + 1])
 
         last = len(UNITS) - 1
         g_prev = gather(0)
@@ -182,7 +175,21 @@ def tile_moe_pre_lin_gelu_kernel(
                 else:
                     quantise(*piece)
             activate(banks)
-            banks = multiply(UNITS[u - 1][0], UNITS[u - 1][1], min(UNITS[u - 1][2], KEPT))
+            a, lo, hi = UNITS[u - 1]
+            banks = [multiply(c0, c0 + C, (0, 1)) for c0 in range(lo, hi, C)] if a == PASSES - 1 else []
+            if u == last - 1:
+                codes, scales, at = quantised[(PASSES - 1, lo)]
+                idle = psum.tile([P, BANK], F32, name="acc")
+                for repeat in range(WARM_UPS):
+                    nc.tensor.matmul_mx(
+                        out=idle[:],
+                        lhsT=w_sb[:, 0 : 2 * N].bitcast(FP4X4),
+                        lhsT_scale=ws_sb[:, 0:N],
+                        rhs=codes[:, 0:BANK].bitcast(FP8X4),
+                        rhs_scale=scales[:, 0:BANK],
+                        start=True,
+                        stop=True,
+                    )
             g_prev = g_next
 
         g_last = gather(last)
@@ -197,25 +204,14 @@ def tile_moe_pre_lin_gelu_kernel(
         for a, c0, c1, xb in late:
             quantise(a, c0, c1, xb, codes=late_codes[:, at : at + c1 - c0])
             at = at + c1 - c0
-        shared = []
-        for c0 in range(KEPT, S - C, C):
-            acc = psum.tile([P, C], F32, name="acc")
-            order = (0, 1) if c0 == KEPT else (1, 0)
-            for a in order:
-                for m0 in range(c0, c0 + C, MM_N):
-                    codes, scales, at = quantised[(a, m0)]
-                    matrix = (m0 // C) * PASSES + a
-                    nc.tensor.matmul_mx(
-                        out=acc[:, m0 - c0 : m0 - c0 + MM_N],
-                        lhsT=w_sb[:, matrix * 2 * N : (matrix + 1) * 2 * N].bitcast(FP4X4),
-                        lhsT_scale=ws_sb[:, matrix * N : (matrix + 1) * N],
-                        rhs=codes[:, at : at + MM_N].bitcast(FP8X4),
-                        rhs_scale=scales[:, at : at + MM_N],
-                        start=(a == order[0] and m0 == c0),
-                        stop=(a == order[1] and m0 == c0 + C - MM_N),
-                    )
-            shared.append((acc, c0, c0 + C))
-        activate(shared + multiply(PASSES - 1, S - C, S - MM_N, MM_N, (1, 0)) + multiply(PASSES - 1, S - MM_N, S, MM_N))
+        activate(
+            [
+                multiply(KEPT, KEPT + C, (0, 1)),
+                multiply(KEPT + C, S - C, (1, 0)),
+                multiply(S - C, S - MM_N, (1, 0)),
+                multiply(S - MM_N, S, (0, 1)),
+            ]
+        )
 
         sums = gpool.tile([P, TOP, T], F32, name="g", align_bytes=64)
 

@@ -33,7 +33,7 @@ UNITS = [(0, 0, 2048), (1, 0, 2048), (0, 2048, 4096), (1, 2048, 3328), (1, 3328,
          (1, 3840, 4096)]
 GATE_CUTS = [0, 128, 384, 896, 2048, 4096]
 FIRST_SPLIT = 768
-KEPT = S - 3 * C
+KEPT = S - 4 * C
 WARM_UPS = 2
 HALF = T // 2
 LAST_STORE = 128
@@ -137,7 +137,7 @@ def tile_moe_pre_lin_gelu_kernel(
         def quantise(a, c0, c1, xb, codes=None):
             if codes is None:
                 codes = cpool.tile([P, c1 - c0], U32, name="codes", align_bytes=64)
-            scales = cpool.tile([P, c1 - c0], U8, name="scales", align_bytes=64, bufs=10)
+            scales = cpool.tile([P, c1 - c0], U8, name="scales", align_bytes=64, bufs=9)
             nc.vector.quantize_mx(out=codes[:, :].bitcast(FP8X4), scales=scales[:], in_=xb)
             for m0 in range(c0, c1, MM_N):
                 quantised[(a, m0)] = (codes, scales, m0 - c0)
@@ -176,7 +176,7 @@ def tile_moe_pre_lin_gelu_kernel(
                     quantise(*piece)
             activate(banks)
             a, lo, hi = UNITS[u - 1]
-            banks = [multiply(c0, c0 + C, (0, 1)) for c0 in range(lo, hi, C)] if a == PASSES - 1 else []
+            banks = [multiply(c0, c0 + C, (0, 1)) for c0 in range(lo, min(hi, KEPT), C)] if a == PASSES - 1 else []
             if u == last - 1:
                 codes, scales, at = quantised[(PASSES - 1, lo)]
                 idle = psum.tile([P, BANK], F32, name="acc")
@@ -196,8 +196,11 @@ def tile_moe_pre_lin_gelu_kernel(
         before = interleave_unit(last - 1, g_prev)
         activate(banks)
         final = interleave_unit(last, g_last)
-        late = [(0, c0, c0 + C, kept[3][:, (c0 - KEPT) * PACK : (c0 - KEPT + C) * PACK]) for c0 in range(KEPT, S, C)]
-        late = [late[0], before[0], late[1], final[0], late[2], final[1]]
+        late = [
+            (0, c0, c1, kept[3][:, (c0 - KEPT) * PACK : (c1 - KEPT) * PACK])
+            for c0, c1 in ((KEPT, S - 2 * C), (S - 2 * C, S - C), (S - C, S))
+        ]
+        late = late[:1] + before + late[1:] + final
         width = sum(c1 - c0 for a, c0, c1, xb in late)
         late_codes = keep.tile([P, width], U32, name="win%d_%d" % (PASSES - 1, PACK - 2), align_bytes=64)
         at = 0
@@ -206,9 +209,10 @@ def tile_moe_pre_lin_gelu_kernel(
             at = at + c1 - c0
         activate(
             [
-                multiply(KEPT, KEPT + C, (0, 1)),
-                multiply(KEPT + C, S - C, (1, 0)),
-                multiply(S - C, S - MM_N, (1, 0)),
+                multiply(KEPT, KEPT + C, (1, 0)),
+                multiply(KEPT + C, KEPT + 2 * C, (0, 1)),
+                multiply(KEPT + 2 * C, S - C, (1, 0)),
+                multiply(S - C, S - MM_N, (0, 1)),
                 multiply(S - MM_N, S, (0, 1)),
             ]
         )

@@ -18,25 +18,23 @@ FP4X4 = mybir.dt.float4_e2m1fn_x4
 MULT = mybir.AluOpType.mult
 ADD = mybir.AluOpType.add
 GELU = mybir.ActivationFunctionType.Gelu_apprx_tanh
+COPY = mybir.ActivationFunctionType.Copy
 
 P = 128
 PACK = 4
 PASSES = K // (P * PACK)
 LIST = 16
-WIDE = 2048
-WINDOW = WIDE + 32
-PIECE = 1024
-MM_N = 128
+WINDOW = T + 32
+PIECE = 512
 BANK = 512
+RUN = 4
 
-UNITS = [(0, 0, 2048), (1, 0, 2048), (0, 2048, 4096), (1, 2048, 3328), (1, 3328, 3840),
-         (1, 3840, 4096)]
-GATE_CUTS = [0, 128, 384, 896, 2048, 4096]
+SCALAR_UNITS = [(0, 0, 1024), (0, 1024, 2048), (0, 2048, 3072), (1, 0, 1024), (1, 1024, 2048),
+                (1, 2048, 2560), (1, 2560, 2816), (1, 2816, 2944)]
+VECTOR_UNITS = {0: (0, 3072, 4096), 1: (1, 3584, 4096), 3: (1, 2944, 3584)}
+GATE_CUTS = [3072, 3200, 3456, 4096]
 FIRST_SPLIT = 768
-KEPT = S - 4 * C
-WARM_UPS = 2
-HALF = T // 2
-LAST_STORE = 128
+BACK_CUTS = [0, 128, 320, 576, 896, 1024]
 
 
 def tile_moe_pre_lin_gelu_kernel(
@@ -45,37 +43,37 @@ def tile_moe_pre_lin_gelu_kernel(
     nc = tc.nc
     with ExitStack() as ctx:
         keep = ctx.enter_context(tc.tile_pool(name="keep", bufs=1))
-        gpool = ctx.enter_context(tc.tile_pool(name="gpool", bufs=2))
-        xpool = ctx.enter_context(tc.tile_pool(name="xpool", bufs=3))
-        cpool = ctx.enter_context(tc.tile_pool(name="cpool", bufs=5))
-        psum = ctx.enter_context(tc.psum_pool(name="psum", bufs=8))
+        spool = ctx.enter_context(tc.tile_pool(name="spool", bufs=3))
+        xpool = ctx.enter_context(tc.tile_pool(name="xpool", bufs=4))
+        cpool = ctx.enter_context(tc.tile_pool(name="cpool", bufs=6))
+        psum = ctx.enter_context(tc.psum_pool(name="psum", bufs=1))
 
         offs_sb = keep.tile([P, S // LIST], U16, name="offs_sb")
         pos_sb = [keep.tile([P, T // LIST], U16, name="pos_sb%d" % r) for r in range(TOP)]
         windows = [[keep.tile([P, WINDOW], F32, name="win%d_%d" % (a, t), align_bytes=64) for t in range(PACK)] for a in range(PASSES)]
-        gate_sb = keep.tile([P, S], F32, name="gate_sb")
+        gate_sb = keep.tile([P, S], F32, name="gate_sb", align_bytes=64)
         w_sb = keep.tile([P, E * PASSES * 2 * N], U8, name="w_sb", align_bytes=64)
         ws_sb = keep.tile([P, E * PASSES * N], U8, name="ws_sb", align_bytes=64)
         b_sb = keep.tile([P, E], F32, name="b_sb")
         y = keep.tile([P, S], F32, name="y")
-        zeros = keep.tile([P, HALF], F32, name="zeros")
+        banks = [psum.tile([P, BANK], F32, name="acc%d" % i) for i in range(S // BANK)]
 
         x_rows = xT.rearrange("(a p t) c -> a t p c", a=PASSES, t=PACK)
 
         nc.vector.memset(ws_sb[:].bitcast(I32), 0)
-        nc.vector.memset(zeros[:], 0.0)
 
         nc.scalar.dma_start(windows[0][0][:, 0:FIRST_SPLIT], x_rows[0, 0][:, 0:FIRST_SPLIT])
         nc.sync.dma_start(offs_sb[:], offs)
-        nc.sync.dma_start(gate_sb[:, 0 : GATE_CUTS[1]], gate[0:P, 0 : GATE_CUTS[1]])
+        nc.sync.dma_start(gate_sb[:, GATE_CUTS[0] : GATE_CUTS[1]], gate[0:P, GATE_CUTS[0] : GATE_CUTS[1]])
         nc.sync.dma_start(windows[0][0][:, FIRST_SPLIT:T], x_rows[0, 0][:, FIRST_SPLIT:T])
-        for lo, hi in zip(GATE_CUTS[1:-2], GATE_CUTS[2:-1]):
+        for lo, hi in zip(GATE_CUTS[1:-1], GATE_CUTS[2:]):
             nc.sync.dma_start(gate_sb[:, lo:hi], gate[0:P, lo:hi])
-        for a in range(PASSES):
-            for t in range(PACK):
-                if (a, t) != (0, 0):
-                    nc.sync.dma_start(windows[a][t][:, 0:T], x_rows[a, t])
-        nc.sync.dma_start(gate_sb[:, GATE_CUTS[-2] : S], gate[0:P, GATE_CUTS[-2] : S])
+        for t in range(1, PACK):
+            nc.sync.dma_start(windows[0][t][:, 0:T], x_rows[0, t])
+        nc.sync.dma_start(gate_sb[:, 0:1024], gate[0:P, 0:1024])
+        for t in range(PACK):
+            nc.sync.dma_start(windows[1][t][:, 0:T], x_rows[1, t])
+        nc.sync.dma_start(gate_sb[:, 1024 : GATE_CUTS[0]], gate[0:P, 1024 : GATE_CUTS[0]])
         nc.sync.dma_start(
             w_sb[:].bitcast(I32).rearrange("p (g n) -> p g n", g=E * PASSES),
             w_words.rearrange("e a p n -> p (e a) n").bitcast(I32),
@@ -89,144 +87,109 @@ def tile_moe_pre_lin_gelu_kernel(
         for r, pos in enumerate((pos1, pos2, pos3, pos4)):
             nc.sync.dma_start(pos_sb[r][:], pos)
 
-        quantised = {}
+        def pieces(lo, hi):
+            cuts = [lo] + [c for c in range(0, S, PIECE) if lo < c < hi] + [hi]
+            return list(zip(cuts[:-1], cuts[1:]))
 
-        def pieces(lo, hi, widest):
-            cuts = []
-            while lo < hi:
-                width = widest
-                while lo + width > hi:
-                    width = width // 2
-                cuts.append((lo, lo + width))
-                lo = lo + width
-            return cuts
+        def listed(a, t, lo, hi):
+            return windows[a][t][:].indirect(offs_sb[:, lo // LIST : hi // LIST])
 
-        def gather(u):
-            a, lo, hi = UNITS[u]
-            g = gpool.tile([P, PACK, hi - lo], F32, name="g", align_bytes=64)
+        def scalar_gather(a, lo, hi):
+            g = spool.tile([P, PACK, hi - lo], F32, name="raw", align_bytes=64)
             for t in range(PACK):
-                cuts = GATE_CUTS[:-1] if (u, t) == (0, 0) else [lo, hi]
-                for c0, c1 in zip(cuts[:-1], cuts[1:]):
-                    nc.vector.tensor_tensor(
-                        g[:, t, c0 - lo : c1 - lo],
-                        windows[a][t][:].indirect(offs_sb[:, c0 // LIST : c1 // LIST]),
-                        gate_sb[:, c0:c1],
-                        MULT,
-                    )
+                nc.scalar.activation(g[:, t, :], listed(a, t, lo, hi), COPY)
             return g
 
-        def interleave(move, xb, planes):
-            move(
-                xb.rearrange("p (c i t) -> p c t i", i=4, t=PACK),
-                planes.rearrange("p t (c i) -> p c t i", i=4),
-            )
+        def vector_gather(a, lo, hi):
+            g = keep.tile([P, PACK, hi - lo], F32, name="gated", align_bytes=64)
+            for t in range(PACK):
+                cuts = GATE_CUTS if (a, t) == (0, 0) else [lo, hi]
+                for c0, c1 in zip(cuts[:-1], cuts[1:]):
+                    nc.vector.tensor_tensor(g[:, t, c0 - lo : c1 - lo], listed(a, t, c0, c1), gate_sb[:, c0:c1], MULT)
+            return g
 
-        def interleave_unit(u, g):
-            a, lo, hi = UNITS[u]
-            rounded = []
-            cuts = pieces(lo, KEPT, PIECE) + [(KEPT, hi)] if (a, hi) == (0, S) else pieces(lo, hi, MM_N if u == len(UNITS) - 1 else PIECE)
-            for c0, c1 in cuts:
-                if (a, c0) == (0, KEPT):
-                    xb = keep.tile([P, (c1 - c0) * PACK], BF16, name="xb_kept", align_bytes=64)
-                else:
-                    xb = xpool.tile([P, (c1 - c0) * PACK], BF16, name="xb", align_bytes=64)
-                interleave(nc.scalar.copy, xb[:], g[:, :, c0 - lo : c1 - lo])
-                rounded.append((a, c0, c1, xb[:]))
-            return rounded
+        def side_by_side(xb):
+            return xb.rearrange("p (c i t) -> p c t i", i=RUN, t=PACK)
 
-        def quantise(a, c0, c1, xb, codes=None):
-            if codes is None:
-                codes = cpool.tile([P, c1 - c0], U32, name="codes", align_bytes=64)
-            scales = cpool.tile([P, c1 - c0], U8, name="scales", align_bytes=64, bufs=9)
-            nc.vector.quantize_mx(out=codes[:, :].bitcast(FP8X4), scales=scales[:], in_=xb)
-            for m0 in range(c0, c1, MM_N):
-                quantised[(a, m0)] = (codes, scales, m0 - c0)
+        def by_plane(planes):
+            return planes.rearrange("p t (c i) -> p c t i", i=RUN)
 
-        def multiply(lo, hi, order):
-            acc = psum.tile([P, hi - lo], F32, name="acc")
-            steps = [(a, m0) for a in order for m0 in range(lo, hi, MM_N)]
-            for a, m0 in steps:
-                codes, scales, at = quantised[(a, m0)]
+        todo = [PASSES * BANK] * len(banks)
+        waiting = []
+
+        def finish():
+            a, c0, c1, xb = waiting.pop(0)
+            codes = cpool.tile([P, c1 - c0], U32, name="codes", align_bytes=64)
+            scales = cpool.tile([P, c1 - c0], U8, name="scales", align_bytes=64)
+            nc.vector.quantize_mx(out=codes[:].bitcast(FP8X4), scales=scales[:], in_=xb[:])
+            bank = c0 // BANK
+            width = min(C, c1 - c0)
+            for m0 in range(c0, c1, width):
                 matrix = (m0 // C) * PASSES + a
+                first = todo[bank] == PASSES * BANK
+                todo[bank] = todo[bank] - width
                 nc.tensor.matmul_mx(
-                    out=acc[:, m0 - lo : m0 - lo + MM_N],
+                    out=banks[bank][:, m0 - bank * BANK : m0 - bank * BANK + width],
                     lhsT=w_sb[:, matrix * 2 * N : (matrix + 1) * 2 * N].bitcast(FP4X4),
                     lhsT_scale=ws_sb[:, matrix * N : (matrix + 1) * N],
-                    rhs=codes[:, at : at + MM_N].bitcast(FP8X4),
-                    rhs_scale=scales[:, at : at + MM_N],
-                    start=((a, m0) == steps[0]),
-                    stop=((a, m0) == steps[-1]),
+                    rhs=codes[:, m0 - c0 : m0 - c0 + width].bitcast(FP8X4),
+                    rhs_scale=scales[:, m0 - c0 : m0 - c0 + width],
+                    start=first,
+                    stop=(todo[bank] == 0),
                 )
-            return acc, lo, hi
+            if todo[bank] == 0:
+                for e in range(bank * BANK // C, (bank + 1) * BANK // C):
+                    at = e * C - bank * BANK
+                    nc.scalar.activation(y[:, e * C : (e + 1) * C], banks[bank][:, at : at + C], GELU, bias=b_sb[:, e : e + 1])
 
-        def activate(banks):
-            for acc, lo, hi in banks:
-                e = lo // C
-                nc.scalar.activation(y[:, lo:hi], acc[:], GELU, bias=b_sb[:, e : e + 1])
+        def rounded(a, c0, c1):
+            xb = xpool.tile([P, (c1 - c0) * PACK], BF16, name="xb", align_bytes=64)
+            waiting.append((a, c0, c1, xb))
+            return xb
 
-        last = len(UNITS) - 1
-        g_prev = gather(0)
-        banks = []
-        for u in range(1, last):
-            g_next = gather(u)
-            for piece in interleave_unit(u - 1, g_prev):
-                if piece[:2] == (0, KEPT):
-                    kept = piece
-                else:
-                    quantise(*piece)
-            activate(banks)
-            a, lo, hi = UNITS[u - 1]
-            banks = [multiply(c0, c0 + C, (0, 1)) for c0 in range(lo, min(hi, KEPT), C)] if a == PASSES - 1 else []
-            if u == last - 1:
-                codes, scales, at = quantised[(PASSES - 1, lo)]
-                idle = psum.tile([P, BANK], F32, name="acc")
-                for repeat in range(WARM_UPS):
-                    nc.tensor.matmul_mx(
-                        out=idle[:],
-                        lhsT=w_sb[:, 0 : 2 * N].bitcast(FP4X4),
-                        lhsT_scale=ws_sb[:, 0:N],
-                        rhs=codes[:, 0:BANK].bitcast(FP8X4),
-                        rhs_scale=scales[:, 0:BANK],
-                        start=True,
-                        stop=True,
-                    )
-            g_prev = g_next
+        raw = [scalar_gather(*SCALAR_UNITS[0])]
+        for u, (a, lo, hi) in enumerate(SCALAR_UNITS):
+            if u + 1 < len(SCALAR_UNITS):
+                raw.append(scalar_gather(*SCALAR_UNITS[u + 1]))
+            if u in VECTOR_UNITS:
+                va, vlo, vhi = VECTOR_UNITS[u]
+                g = vector_gather(va, vlo, vhi)
+                if waiting:
+                    finish()
+                for c0, c1 in pieces(vlo, vhi):
+                    xb = rounded(va, c0, c1)
+                    nc.vector.tensor_copy(side_by_side(xb[:]), by_plane(g[:, :, c0 - vlo : c1 - vlo]))
+                    if len(waiting) > 1:
+                        finish()
+            for c0, c1 in pieces(lo, hi):
+                xb = rounded(a, c0, c1)
+                weights = gate_sb[:, c0:c1].rearrange("p (c i) -> p c i", i=RUN).unsqueeze(2)
+                nc.vector.tensor_tensor(
+                    side_by_side(xb[:]),
+                    by_plane(raw[u][:, :, c0 - lo : c1 - lo]),
+                    weights.to_broadcast([P, (c1 - c0) // RUN, PACK, RUN]),
+                    MULT,
+                )
+                if len(waiting) > 1:
+                    finish()
+        finish()
 
-        g_last = gather(last)
-        before = interleave_unit(last - 1, g_prev)
-        activate(banks)
-        final = interleave_unit(last, g_last)
-        late = [
-            (0, c0, c1, kept[3][:, (c0 - KEPT) * PACK : (c1 - KEPT) * PACK])
-            for c0, c1 in ((KEPT, S - 2 * C), (S - 2 * C, S - C), (S - C, S))
-        ]
-        late = late[:1] + before + late[1:] + final
-        width = sum(c1 - c0 for a, c0, c1, xb in late)
-        late_codes = keep.tile([P, width], U32, name="win%d_%d" % (PASSES - 1, PACK - 2), align_bytes=64)
-        at = 0
-        for a, c0, c1, xb in late:
-            quantise(a, c0, c1, xb, codes=late_codes[:, at : at + c1 - c0])
-            at = at + c1 - c0
-        activate(
-            [
-                multiply(KEPT, KEPT + C, (1, 0)),
-                multiply(KEPT + C, KEPT + 2 * C, (0, 1)),
-                multiply(KEPT + 2 * C, S - C, (1, 0)),
-                multiply(S - C, S - MM_N, (0, 1)),
-                multiply(S - MM_N, S, (0, 1)),
-            ]
-        )
+        parts = spool.tile([P, TOP, T], F32, name="raw", align_bytes=64)
+        total = keep.tile([P, T], F32, name="gated", align_bytes=64)
 
-        sums = gpool.tile([P, TOP, T], F32, name="g", align_bytes=64)
+        def picked(r, lo, hi):
+            return y[:].indirect(pos_sb[r][:, lo // LIST : hi // LIST])
 
-        def fetch(r, lo, hi):
-            picked = y[:].indirect(pos_sb[r][:, lo // LIST : hi // LIST])
-            so_far = zeros[:] if r == 0 else sums[:, r - 1, lo:hi]
-            nc.vector.tensor_tensor(sums[:, r, lo:hi], picked, so_far, ADD)
+        def close(lo, hi):
+            nc.vector.tensor_tensor(total[:, lo:hi], parts[:, 2, lo:hi], parts[:, 3, lo:hi], ADD)
+            nc.sync.dma_start(out[:, lo:hi], total[:, lo:hi])
 
-        for r in range(TOP - 1):
-            for lo in range(0, T, HALF):
-                fetch(r, lo, lo + HALF)
-        for lo, hi in pieces(0, T - LAST_STORE, HALF) + [(T - LAST_STORE, T)]:
-            fetch(TOP - 1, lo, hi)
-            nc.sync.dma_start(out[:, lo:hi], sums[:, TOP - 1, lo:hi])
+        ranges = list(zip(BACK_CUTS[:-1], BACK_CUTS[1:]))
+        for i, (lo, hi) in enumerate(ranges):
+            for r in range(2):
+                nc.scalar.activation(parts[:, r, lo:hi], picked(r, lo, hi), COPY)
+            nc.vector.tensor_tensor(parts[:, 2, lo:hi], picked(2, lo, hi), parts[:, 0, lo:hi], ADD)
+            if i > 0:
+                close(*ranges[i - 1])
+            nc.vector.tensor_tensor(parts[:, 3, lo:hi], picked(3, lo, hi), parts[:, 1, lo:hi], ADD)
+        close(*ranges[-1])

@@ -1,6 +1,7 @@
 from contextlib import ExitStack
 
 import concourse.mybir as mybir
+from concourse.masks import make_identity
 
 K, T, E, C, N = 1024, 1024, 16, 256, 128
 S = E * C
@@ -25,16 +26,14 @@ PACK = 4
 PASSES = K // (P * PACK)
 LIST = 16
 WINDOW = T + 32
-PIECE = 512
 BANK = 512
 RUN = 4
 
-SCALAR_UNITS = [(0, 0, 1024), (0, 1024, 2048), (0, 2048, 3072), (1, 0, 1024), (1, 1024, 2048),
-                (1, 2048, 2560), (1, 2560, 2816), (1, 2816, 2944)]
-VECTOR_UNITS = {0: (0, 3072, 4096), 1: (1, 3584, 4096), 3: (1, 2944, 3584)}
-GATE_CUTS = [3072, 3200, 3456, 4096]
+ROUNDS = [(0, 512, 512, 576), (0, 672, 352, 576), (1, 672, 352, 576), (1, 672, 352, 576), (0, 672, 352, 576),
+          (0, 672, 352, 576), (1, 448, 320, 416), (1, 416, 224, 288), (1, 256, 128, 160), (1, 160, 96, 96)]
 FIRST_SPLIT = 768
 BACK_CUTS = [0, 128, 320, 576, 896, 1024]
+WIDTHS = [1024, 512, 384, 256, 128]
 
 
 def tile_moe_pre_lin_gelu_kernel(
@@ -44,36 +43,53 @@ def tile_moe_pre_lin_gelu_kernel(
     with ExitStack() as ctx:
         keep = ctx.enter_context(tc.tile_pool(name="keep", bufs=1))
         spool = ctx.enter_context(tc.tile_pool(name="spool", bufs=3))
-        xpool = ctx.enter_context(tc.tile_pool(name="xpool", bufs=4))
-        cpool = ctx.enter_context(tc.tile_pool(name="cpool", bufs=6))
-        psum = ctx.enter_context(tc.psum_pool(name="psum", bufs=1))
+        vpool = ctx.enter_context(tc.tile_pool(name="vpool", bufs=2))
+        cpool = ctx.enter_context(tc.tile_pool(name="cpool", bufs=3))
+        sums = ctx.enter_context(tc.psum_pool(name="sums", bufs=6))
+        spread = ctx.enter_context(tc.psum_pool(name="spread", bufs=2))
 
         offs_sb = keep.tile([P, S // LIST], U16, name="offs_sb")
         pos_sb = [keep.tile([P, T // LIST], U16, name="pos_sb%d" % r) for r in range(TOP)]
         windows = [[keep.tile([P, WINDOW], F32, name="win%d_%d" % (a, t), align_bytes=64) for t in range(PACK)] for a in range(PASSES)]
         gate_sb = keep.tile([P, S], F32, name="gate_sb", align_bytes=64)
+        gate_rows = keep.tile([P, P], F32, name="gate_rows")
+        gate_cols = keep.tile([P, S // P], F32, name="gate_cols")
+        identity = keep.tile([P, P], F32, name="identity")
         w_sb = keep.tile([P, E * PASSES * 2 * N], U8, name="w_sb", align_bytes=64)
         ws_sb = keep.tile([P, E * PASSES * N], U8, name="ws_sb", align_bytes=64)
         b_sb = keep.tile([P, E], F32, name="b_sb")
         y = keep.tile([P, S], F32, name="y")
-        banks = [psum.tile([P, BANK], F32, name="acc%d" % i) for i in range(S // BANK)]
+
+        starts = []
+        reached = [0] * PASSES
+        for a, n_s, n_v, n_g in ROUNDS:
+            starts.append(reached[a])
+            reached[a] = reached[a] + n_s + n_v
 
         x_rows = xT.rearrange("(a p t) c -> a t p c", a=PASSES, t=PACK)
 
         nc.vector.memset(ws_sb[:].bitcast(I32), 0)
+        nc.gpsimd.memset(gate_rows[:], 0.0)
+        make_identity(nc, identity[:])
+
+        needed = []
+        for lo, hi in sorted(set((lo + n_s + n_v - n_g, lo + n_s + n_v) for lo, (a, n_s, n_v, n_g) in zip(starts, ROUNDS))):
+            if needed and lo <= needed[-1][1]:
+                needed[-1] = (needed[-1][0], max(hi, needed[-1][1]))
+            else:
+                needed.append((lo, hi))
 
         nc.scalar.dma_start(windows[0][0][:, 0:FIRST_SPLIT], x_rows[0, 0][:, 0:FIRST_SPLIT])
         nc.sync.dma_start(offs_sb[:], offs)
-        nc.sync.dma_start(gate_sb[:, GATE_CUTS[0] : GATE_CUTS[1]], gate[0:P, GATE_CUTS[0] : GATE_CUTS[1]])
         nc.sync.dma_start(windows[0][0][:, FIRST_SPLIT:T], x_rows[0, 0][:, FIRST_SPLIT:T])
-        for lo, hi in zip(GATE_CUTS[1:-1], GATE_CUTS[2:]):
-            nc.sync.dma_start(gate_sb[:, lo:hi], gate[0:P, lo:hi])
-        for t in range(1, PACK):
+        nc.sync.dma_start(windows[0][1][:, 0:T], x_rows[0, 1])
+        nc.sync.dma_start(gate_rows[0 : S // P, :], gate[0, :].rearrange("(m n) -> m n", n=P))
+        for t in range(2, PACK):
             nc.sync.dma_start(windows[0][t][:, 0:T], x_rows[0, t])
-        nc.sync.dma_start(gate_sb[:, 0:1024], gate[0:P, 0:1024])
+        for lo, hi in needed[:2]:
+            nc.sync.dma_start(gate_sb[:, lo:hi], gate[0:P, lo:hi])
         for t in range(PACK):
             nc.sync.dma_start(windows[1][t][:, 0:T], x_rows[1, t])
-        nc.sync.dma_start(gate_sb[:, 1024 : GATE_CUTS[0]], gate[0:P, 1024 : GATE_CUTS[0]])
         nc.sync.dma_start(
             w_sb[:].bitcast(I32).rearrange("p (g n) -> p g n", g=E * PASSES),
             w_words.rearrange("e a p n -> p (e a) n").bitcast(I32),
@@ -83,53 +99,60 @@ def tile_moe_pre_lin_gelu_kernel(
                 ws_sb[32 * q : 32 * q + 4, :].bitcast(I32).rearrange("p (g n) -> p g n", g=E * PASSES),
                 w_scales[:, :, 4 * q : 4 * q + 4, :].rearrange("e a q n -> q (e a) n").bitcast(I32),
             )
+        for lo, hi in needed[2:]:
+            nc.sync.dma_start(gate_sb[:, lo:hi], gate[0:P, lo:hi])
         nc.sync.dma_start(b_sb[:], b)
         for r, pos in enumerate((pos1, pos2, pos3, pos4)):
             nc.sync.dma_start(pos_sb[r][:], pos)
 
-        def pieces(lo, hi):
-            cuts = [lo] + [c for c in range(0, S, PIECE) if lo < c < hi] + [hi]
-            return list(zip(cuts[:-1], cuts[1:]))
-
         def listed(a, t, lo, hi):
             return windows[a][t][:].indirect(offs_sb[:, lo // LIST : hi // LIST])
 
-        def scalar_gather(a, lo, hi):
-            g = spool.tile([P, PACK, hi - lo], F32, name="raw", align_bytes=64)
+        def scalar_gather(r):
+            a, n_s, n_v, n_g = ROUNDS[r]
+            raw = spool.tile([P, PACK, n_s], F32, name="raw_s", align_bytes=64)
             for t in range(PACK):
-                nc.scalar.activation(g[:, t, :], listed(a, t, lo, hi), COPY)
-            return g
+                nc.scalar.activation(raw[:, t, :], listed(a, t, starts[r], starts[r] + n_s), COPY)
+            return raw
 
-        def vector_gather(a, lo, hi):
-            g = keep.tile([P, PACK, hi - lo], F32, name="gated", align_bytes=64)
-            for t in range(PACK):
-                cuts = GATE_CUTS if (a, t) == (0, 0) else [lo, hi]
-                for c0, c1 in zip(cuts[:-1], cuts[1:]):
-                    nc.vector.tensor_tensor(g[:, t, c0 - lo : c1 - lo], listed(a, t, c0, c1), gate_sb[:, c0:c1], MULT)
-            return g
+        def vector_gather(r, raw, planes):
+            a, n_s, n_v, n_g = ROUNDS[r]
+            lo = starts[r] + n_s
+            for t in planes:
+                nc.vector.tensor_copy(raw[:, t, :], listed(a, t, lo, lo + n_v))
 
-        def side_by_side(xb):
-            return xb.rearrange("p (c i t) -> p c t i", i=RUN, t=PACK)
+        def times_gate(engine, xb, raw, weights):
+            width = weights.shape[1]
+            engine.tensor_tensor(
+                xb.rearrange("p (c i t) -> p c t i", i=RUN, t=PACK),
+                raw.rearrange("p t (c i) -> p c t i", i=RUN),
+                weights.rearrange("p (c i) -> p c i", i=RUN).unsqueeze(2).to_broadcast([P, width // RUN, PACK, RUN]),
+                MULT,
+            )
 
-        def by_plane(planes):
-            return planes.rearrange("p t (c i) -> p c t i", i=RUN)
+        def spread_gate(r):
+            a, n_s, n_v, n_g = ROUNDS[r]
+            bank = spread.tile([P, BANK], F32, name="gate_ps")
+            for c0 in range(0, n_s + n_v - n_g, P):
+                m = (starts[r] + c0) // P
+                nc.tensor.transpose(bank[:, c0 : c0 + P], gate_cols[:, m : m + 1].to_broadcast([P, P]), identity[:])
+            return bank
 
-        todo = [PASSES * BANK] * len(banks)
-        waiting = []
+        banks = {}
+        todo = [PASSES * BANK] * (S // BANK)
 
-        def finish():
-            a, c0, c1, xb = waiting.pop(0)
-            codes = cpool.tile([P, c1 - c0], U32, name="codes", align_bytes=64)
-            scales = cpool.tile([P, c1 - c0], U8, name="scales", align_bytes=64)
-            nc.vector.quantize_mx(out=codes[:].bitcast(FP8X4), scales=scales[:], in_=xb[:])
-            bank = c0 // BANK
-            width = min(C, c1 - c0)
-            for m0 in range(c0, c1, width):
+        def multiply(a, c0, c1, codes, scales):
+            m0 = c0
+            while m0 < c1:
+                width = min(C - m0 % C, c1 - m0)
+                bank = m0 // BANK
                 matrix = (m0 // C) * PASSES + a
-                first = todo[bank] == PASSES * BANK
+                first = bank not in banks
+                if first:
+                    banks[bank] = sums.tile([P, BANK], F32, name="acc")
                 todo[bank] = todo[bank] - width
                 nc.tensor.matmul_mx(
-                    out=banks[bank][:, m0 - bank * BANK : m0 - bank * BANK + width],
+                    out=banks[bank][:, m0 % BANK : m0 % BANK + width],
                     lhsT=w_sb[:, matrix * 2 * N : (matrix + 1) * 2 * N].bitcast(FP4X4),
                     lhsT_scale=ws_sb[:, matrix * N : (matrix + 1) * N],
                     rhs=codes[:, m0 - c0 : m0 - c0 + width].bitcast(FP8X4),
@@ -137,45 +160,54 @@ def tile_moe_pre_lin_gelu_kernel(
                     start=first,
                     stop=(todo[bank] == 0),
                 )
-            if todo[bank] == 0:
-                for e in range(bank * BANK // C, (bank + 1) * BANK // C):
-                    at = e * C - bank * BANK
-                    nc.scalar.activation(y[:, e * C : (e + 1) * C], banks[bank][:, at : at + C], GELU, bias=b_sb[:, e : e + 1])
+                if todo[bank] == 0:
+                    for e in range(bank * BANK // C, (bank + 1) * BANK // C):
+                        at = e * C % BANK
+                        nc.scalar.activation(y[:, e * C : (e + 1) * C], banks[bank][:, at : at + C], GELU, bias=b_sb[:, e : e + 1])
+                m0 = m0 + width
 
-        def rounded(a, c0, c1):
-            xb = xpool.tile([P, (c1 - c0) * PACK], BF16, name="xb", align_bytes=64)
-            waiting.append((a, c0, c1, xb))
-            return xb
-
-        raw = [scalar_gather(*SCALAR_UNITS[0])]
-        for u, (a, lo, hi) in enumerate(SCALAR_UNITS):
-            if u + 1 < len(SCALAR_UNITS):
-                raw.append(scalar_gather(*SCALAR_UNITS[u + 1]))
-            if u in VECTOR_UNITS:
-                va, vlo, vhi = VECTOR_UNITS[u]
-                g = vector_gather(va, vlo, vhi)
-                if waiting:
-                    finish()
-                for c0, c1 in pieces(vlo, vhi):
-                    xb = rounded(va, c0, c1)
-                    nc.vector.tensor_copy(side_by_side(xb[:]), by_plane(g[:, :, c0 - vlo : c1 - vlo]))
-                    if len(waiting) > 1:
-                        finish()
-            for c0, c1 in pieces(lo, hi):
-                xb = rounded(a, c0, c1)
-                weights = gate_sb[:, c0:c1].rearrange("p (c i) -> p c i", i=RUN).unsqueeze(2)
-                nc.vector.tensor_tensor(
-                    side_by_side(xb[:]),
-                    by_plane(raw[u][:, :, c0 - lo : c1 - lo]),
-                    weights.to_broadcast([P, (c1 - c0) // RUN, PACK, RUN]),
-                    MULT,
+        def quantise(r, xb):
+            a, n_s, n_v, n_g = ROUNDS[r]
+            at = 0
+            while at < n_s + n_v:
+                width = max(w for w in WIDTHS if at + w <= n_s + n_v)
+                codes = cpool.tile([P, width], U32, name="codes", align_bytes=64)
+                scales = cpool.tile([P, width], U8, name="scales", align_bytes=64)
+                nc.vector.quantize_mx(
+                    out=codes[:].bitcast(FP8X4), scales=scales[:], in_=xb[:, at * PACK : (at + width) * PACK]
                 )
-                if len(waiting) > 1:
-                    finish()
-        finish()
+                multiply(a, starts[r] + at, starts[r] + at + width, codes, scales)
+                at = at + width
 
-        parts = spool.tile([P, TOP, T], F32, name="raw", align_bytes=64)
-        total = keep.tile([P, T], F32, name="gated", align_bytes=64)
+        def raw_of_vector(r):
+            return vpool.tile([P, PACK, ROUNDS[r][2]], F32, name="raw_v", align_bytes=64)
+
+        raw_s = scalar_gather(0)
+        raw_v = raw_of_vector(0)
+        vector_gather(0, raw_v, range(PACK))
+        turned = spread.tile([P, P], F32, name="gate_ps")
+        nc.tensor.transpose(turned[:], gate_rows[:], identity[:])
+        nc.vector.tensor_copy(gate_cols[:], turned[:, 0 : S // P])
+        for r, (a, n_s, n_v, n_g) in enumerate(ROUNDS):
+            more = r + 1 < len(ROUNDS)
+            lo, n, n_m = starts[r], n_s + n_v, n_s + n_v - n_g
+            xb = keep.tile([P, n * PACK], BF16, name="xb", align_bytes=64)
+            times_gate(nc.gpsimd, xb[:, n_s * PACK : n * PACK], raw_v[:], gate_sb[:, lo + n_s : lo + n])
+            if n_m < n_s:
+                times_gate(nc.gpsimd, xb[:, n_m * PACK : n_s * PACK], raw_s[:, :, n_m:n_s], gate_sb[:, lo + n_m : lo + n_s])
+            gate_ps = spread_gate(r)
+            if more:
+                next_s = scalar_gather(r + 1)
+                next_v = raw_of_vector(r + 1)
+                vector_gather(r + 1, next_v, range(PACK - 1))
+            times_gate(nc.vector, xb[:, 0 : n_m * PACK], raw_s[:, :, 0:n_m], gate_ps[:, 0:n_m])
+            if more:
+                vector_gather(r + 1, next_v, [PACK - 1])
+                raw_s, raw_v = next_s, next_v
+            quantise(r, xb)
+
+        parts = keep.tile([P, TOP, T], F32, name="gate_sb", align_bytes=64)
+        total = keep.tile([P, T], F32, name="win0_0", align_bytes=64)
 
         def picked(r, lo, hi):
             return y[:].indirect(pos_sb[r][:, lo // LIST : hi // LIST])

@@ -28,9 +28,10 @@ LIST = 16
 WINDOW = T + 32
 BANK = 512
 RUN = 4
+RUN_G = 2
 
-ROUNDS = [(0, 512, 512, 576), (0, 672, 352, 576), (1, 672, 352, 576), (1, 672, 352, 576), (0, 672, 352, 576),
-          (0, 672, 352, 576), (1, 448, 320, 416), (1, 416, 224, 288), (1, 256, 128, 160), (1, 160, 96, 96)]
+ROUNDS = [(0, 512, 512, 512), (0, 704, 320, 512), (1, 704, 320, 512), (1, 704, 320, 512), (0, 672, 352, 512),
+          (0, 672, 352, 512), (1, 448, 320, 384), (1, 416, 224, 256), (1, 256, 128, 128), (1, 160, 96, 96)]
 FIRST_SPLIT = 768
 BACK_CUTS = [0, 128, 320, 576, 896, 1024]
 WIDTHS = [1024, 512, 384, 256, 128]
@@ -42,17 +43,20 @@ def tile_moe_pre_lin_gelu_kernel(
     nc = tc.nc
     with ExitStack() as ctx:
         keep = ctx.enter_context(tc.tile_pool(name="keep", bufs=1))
-        spool = ctx.enter_context(tc.tile_pool(name="spool", bufs=3))
-        vpool = ctx.enter_context(tc.tile_pool(name="vpool", bufs=2))
+        rawpool = ctx.enter_context(tc.tile_pool(name="rawpool", bufs=1))
         cpool = ctx.enter_context(tc.tile_pool(name="cpool", bufs=3))
-        sums = ctx.enter_context(tc.psum_pool(name="sums", bufs=6))
-        spread = ctx.enter_context(tc.psum_pool(name="spread", bufs=2))
+        sums = ctx.enter_context(tc.psum_pool(name="sums", bufs=5))
+        spread = ctx.enter_context(tc.psum_pool(name="spread", bufs=3))
 
         offs_sb = keep.tile([P, S // LIST], U16, name="offs_sb")
         pos_sb = [keep.tile([P, T // LIST], U16, name="pos_sb%d" % r) for r in range(TOP)]
         windows = [[keep.tile([P, WINDOW], F32, name="win%d_%d" % (a, t), align_bytes=64) for t in range(PACK)] for a in range(PASSES)]
         gate_sb = keep.tile([P, S], F32, name="gate_sb", align_bytes=64)
-        gate_rows = keep.tile([P, P], F32, name="gate_rows")
+        size_s = 4 * PACK * max(n_s for a, n_s, n_v, n_g in ROUNDS)
+        size_v = 4 * PACK * max(n_v for a, n_s, n_v, n_g in ROUNDS)
+        place_s = [0, size_s, 2 * size_s + 2 * size_v]
+        place_v = [2 * size_s + size_v, 2 * size_s]
+        gate_rows = rawpool.tile([P, P], F32, name="gate_rows", offset=place_v[1] - 2 * P)
         gate_cols = keep.tile([P, S // P], F32, name="gate_cols")
         identity = keep.tile([P, P], F32, name="identity")
         w_sb = keep.tile([P, E * PASSES * 2 * N], U8, name="w_sb", align_bytes=64)
@@ -80,12 +84,15 @@ def tile_moe_pre_lin_gelu_kernel(
                 needed.append((lo, hi))
 
         nc.scalar.dma_start(windows[0][0][:, 0:FIRST_SPLIT], x_rows[0, 0][:, 0:FIRST_SPLIT])
+        idle = keep.tile([P, 2], F32, name="idle")
+        nc.vector.memset(idle[:, 0:1], 0.0)
+        nc.scalar.activation(idle[:, 1:2], idle[:, 0:1], GELU)
         nc.sync.dma_start(offs_sb[:], offs)
         nc.sync.dma_start(windows[0][0][:, FIRST_SPLIT:T], x_rows[0, 0][:, FIRST_SPLIT:T])
         nc.sync.dma_start(windows[0][1][:, 0:T], x_rows[0, 1])
-        nc.sync.dma_start(gate_rows[0 : S // P, :], gate[0, :].rearrange("(m n) -> m n", n=P))
         for t in range(2, PACK):
             nc.sync.dma_start(windows[0][t][:, 0:T], x_rows[0, t])
+        nc.sync.dma_start(gate_rows[0 : S // P, :], gate[0, :].rearrange("(m n) -> m n", n=P))
         for lo, hi in needed[:2]:
             nc.sync.dma_start(gate_sb[:, lo:hi], gate[0:P, lo:hi])
         for t in range(PACK):
@@ -110,7 +117,7 @@ def tile_moe_pre_lin_gelu_kernel(
 
         def scalar_gather(r):
             a, n_s, n_v, n_g = ROUNDS[r]
-            raw = spool.tile([P, PACK, n_s], F32, name="raw_s", align_bytes=64)
+            raw = rawpool.tile([P, PACK, n_s], F32, name="raw_s%d" % r, offset=place_s[r % 3])
             for t in range(PACK):
                 nc.scalar.activation(raw[:, t, :], listed(a, t, starts[r], starts[r] + n_s), COPY)
             return raw
@@ -121,21 +128,20 @@ def tile_moe_pre_lin_gelu_kernel(
             for t in planes:
                 nc.vector.tensor_copy(raw[:, t, :], listed(a, t, lo, lo + n_v))
 
-        def times_gate(engine, xb, raw, weights):
+        def times_gate(engine, run, xb, raw, weights):
             width = weights.shape[1]
             engine.tensor_tensor(
-                xb.rearrange("p (c i t) -> p c t i", i=RUN, t=PACK),
-                raw.rearrange("p t (c i) -> p c t i", i=RUN),
-                weights.rearrange("p (c i) -> p c i", i=RUN).unsqueeze(2).to_broadcast([P, width // RUN, PACK, RUN]),
+                xb.rearrange("p (c i t) -> p c t i", i=run, t=PACK),
+                raw.rearrange("p t (c i) -> p c t i", i=run),
+                weights.rearrange("p (c i) -> p c i", i=run).unsqueeze(2).to_broadcast([P, width // run, PACK, run]),
                 MULT,
             )
 
-        def spread_gate(r):
-            a, n_s, n_v, n_g = ROUNDS[r]
+        def spread_gate(lo, hi):
             bank = spread.tile([P, BANK], F32, name="gate_ps")
-            for c0 in range(0, n_s + n_v - n_g, P):
-                m = (starts[r] + c0) // P
-                nc.tensor.transpose(bank[:, c0 : c0 + P], gate_cols[:, m : m + 1].to_broadcast([P, P]), identity[:])
+            for c0 in range(lo, hi, P):
+                m = c0 // P
+                nc.tensor.transpose(bank[:, c0 - lo : c0 - lo + P], gate_cols[:, m : m + 1].to_broadcast([P, P]), identity[:])
             return bank
 
         banks = {}
@@ -180,7 +186,7 @@ def tile_moe_pre_lin_gelu_kernel(
                 at = at + width
 
         def raw_of_vector(r):
-            return vpool.tile([P, PACK, ROUNDS[r][2]], F32, name="raw_v", align_bytes=64)
+            return rawpool.tile([P, PACK, ROUNDS[r][2]], F32, name="raw_v%d" % r, offset=place_v[r % 2])
 
         raw_s = scalar_gather(0)
         raw_v = raw_of_vector(0)
@@ -192,15 +198,17 @@ def tile_moe_pre_lin_gelu_kernel(
             more = r + 1 < len(ROUNDS)
             lo, n, n_m = starts[r], n_s + n_v, n_s + n_v - n_g
             xb = keep.tile([P, n * PACK], BF16, name="xb", align_bytes=64)
-            times_gate(nc.gpsimd, xb[:, n_s * PACK : n * PACK], raw_v[:], gate_sb[:, lo + n_s : lo + n])
+            times_gate(nc.gpsimd, RUN_G, xb[:, n_s * PACK : n * PACK], raw_v[:], gate_sb[:, lo + n_s : lo + n])
             if n_m < n_s:
-                times_gate(nc.gpsimd, xb[:, n_m * PACK : n_s * PACK], raw_s[:, :, n_m:n_s], gate_sb[:, lo + n_m : lo + n_s])
-            gate_ps = spread_gate(r)
+                times_gate(nc.gpsimd, RUN_G, xb[:, n_m * PACK : n_s * PACK], raw_s[:, :, n_m:n_s], gate_sb[:, lo + n_m : lo + n_s])
+            shares = [(c0, min(c0 + BANK, n_m)) for c0 in range(0, n_m, BANK)]
+            gate_ps = [spread_gate(lo + c0, lo + c1) for c0, c1 in shares]
             if more:
                 next_s = scalar_gather(r + 1)
                 next_v = raw_of_vector(r + 1)
                 vector_gather(r + 1, next_v, range(PACK - 1))
-            times_gate(nc.vector, xb[:, 0 : n_m * PACK], raw_s[:, :, 0:n_m], gate_ps[:, 0:n_m])
+            for (c0, c1), bank in zip(shares, gate_ps):
+                times_gate(nc.vector, RUN, xb[:, c0 * PACK : c1 * PACK], raw_s[:, :, c0:c1], bank[:, 0 : c1 - c0])
             if more:
                 vector_gather(r + 1, next_v, [PACK - 1])
                 raw_s, raw_v = next_s, next_v

@@ -30,9 +30,10 @@ BANK = 512
 RUN = 4
 RUN_G = 2
 
-ROUNDS = [(0, 512, 512, 512), (0, 704, 320, 512), (1, 704, 320, 512), (1, 704, 320, 512), (0, 672, 352, 512),
-          (0, 672, 352, 512), (1, 448, 320, 384), (1, 416, 224, 256), (1, 256, 128, 128), (1, 160, 96, 96)]
+ROUNDS = [(0, 512, 512, 512), (1, 672, 352, 512), (0, 672, 352, 512), (1, 672, 352, 512), (0, 672, 352, 512),
+          (1, 672, 352, 512), (0, 672, 352, 512), (1, 416, 96, 256), (1, 256, 128, 128), (1, 128, 0, 0)]
 FIRST_SPLIT = 768
+GROUP_CUTS = list(range(0, S - BANK + 1, BANK)) + [S - C, S - P, S]
 BACK_CUTS = [0, 128, 320, 576, 896, 1024]
 WIDTHS = [1024, 512, 384, 256, 128]
 
@@ -44,9 +45,9 @@ def tile_moe_pre_lin_gelu_kernel(
     with ExitStack() as ctx:
         keep = ctx.enter_context(tc.tile_pool(name="keep", bufs=1))
         rawpool = ctx.enter_context(tc.tile_pool(name="rawpool", bufs=1))
-        cpool = ctx.enter_context(tc.tile_pool(name="cpool", bufs=3))
-        sums = ctx.enter_context(tc.psum_pool(name="sums", bufs=5))
-        spread = ctx.enter_context(tc.psum_pool(name="spread", bufs=3))
+        cpool = ctx.enter_context(tc.tile_pool(name="cpool", bufs=6))
+        sums = ctx.enter_context(tc.psum_pool(name="sums", bufs=6))
+        spread = ctx.enter_context(tc.psum_pool(name="spread", bufs=2))
 
         offs_sb = keep.tile([P, S // LIST], U16, name="offs_sb")
         pos_sb = [keep.tile([P, T // LIST], U16, name="pos_sb%d" % r) for r in range(TOP)]
@@ -54,9 +55,10 @@ def tile_moe_pre_lin_gelu_kernel(
         gate_sb = keep.tile([P, S], F32, name="gate_sb", align_bytes=64)
         size_s = 4 * PACK * max(n_s for a, n_s, n_v, n_g in ROUNDS)
         size_v = 4 * PACK * max(n_v for a, n_s, n_v, n_g in ROUNDS)
-        place_s = [0, size_s, 2 * size_s + 2 * size_v]
-        place_v = [2 * size_s + size_v, 2 * size_s]
-        gate_rows = rawpool.tile([P, P], F32, name="gate_rows", offset=place_v[1] - 2 * P)
+        place_s = [i * size_s for i in range(3)]
+        place_v = [3 * size_s + i * size_v for i in range(2)]
+        gate_first = rawpool.tile([P, ROUNDS[0][3]], F32, name="gate_first", offset=place_s[2])
+        gate_rows = keep.tile([P, P], F32, name="gate_rows")
         gate_cols = keep.tile([P, S // P], F32, name="gate_cols")
         identity = keep.tile([P, P], F32, name="identity")
         w_sb = keep.tile([P, E * PASSES * 2 * N], U8, name="w_sb", align_bytes=64)
@@ -77,7 +79,7 @@ def tile_moe_pre_lin_gelu_kernel(
         make_identity(nc, identity[:])
 
         needed = []
-        for lo, hi in sorted(set((lo + n_s + n_v - n_g, lo + n_s + n_v) for lo, (a, n_s, n_v, n_g) in zip(starts, ROUNDS))):
+        for lo, hi in sorted(set((lo + n_s + n_v - n_g, lo + n_s + n_v) for lo, (a, n_s, n_v, n_g) in zip(starts[1:], ROUNDS[1:]) if n_g)):
             if needed and lo <= needed[-1][1]:
                 needed[-1] = (needed[-1][0], max(hi, needed[-1][1]))
             else:
@@ -90,13 +92,15 @@ def tile_moe_pre_lin_gelu_kernel(
         nc.sync.dma_start(offs_sb[:], offs)
         nc.sync.dma_start(windows[0][0][:, FIRST_SPLIT:T], x_rows[0, 0][:, FIRST_SPLIT:T])
         nc.sync.dma_start(windows[0][1][:, 0:T], x_rows[0, 1])
+        nc.sync.dma_start(gate_rows[0 : S // P, :], gate[0, :].rearrange("(m n) -> m n", n=P))
         for t in range(2, PACK):
             nc.sync.dma_start(windows[0][t][:, 0:T], x_rows[0, t])
-        nc.sync.dma_start(gate_rows[0 : S // P, :], gate[0, :].rearrange("(m n) -> m n", n=P))
-        for lo, hi in needed[:2]:
-            nc.sync.dma_start(gate_sb[:, lo:hi], gate[0:P, lo:hi])
+        first_end = ROUNDS[0][1] + ROUNDS[0][2]
+        nc.sync.dma_start(gate_first[:], gate[0:P, first_end - ROUNDS[0][3] : first_end])
         for t in range(PACK):
             nc.sync.dma_start(windows[1][t][:, 0:T], x_rows[1, t])
+        for lo, hi in needed[:2]:
+            nc.sync.dma_start(gate_sb[:, lo:hi], gate[0:P, lo:hi])
         nc.sync.dma_start(
             w_sb[:].bitcast(I32).rearrange("p (g n) -> p g n", g=E * PASSES),
             w_words.rearrange("e a p n -> p (e a) n").bitcast(I32),
@@ -145,74 +149,85 @@ def tile_moe_pre_lin_gelu_kernel(
             return bank
 
         banks = {}
-        todo = [PASSES * BANK] * (S // BANK)
+        todo = {}
 
         def multiply(a, c0, c1, codes, scales):
             m0 = c0
             while m0 < c1:
-                width = min(C - m0 % C, c1 - m0)
-                bank = m0 // BANK
+                lo, hi = [(lo, hi) for lo, hi in zip(GROUP_CUTS[:-1], GROUP_CUTS[1:]) if lo <= m0 < hi][0]
+                width = min(C - m0 % C, c1 - m0, hi - m0)
                 matrix = (m0 // C) * PASSES + a
-                first = bank not in banks
+                first = lo not in banks
                 if first:
-                    banks[bank] = sums.tile([P, BANK], F32, name="acc")
-                todo[bank] = todo[bank] - width
+                    banks[lo] = sums.tile([P, hi - lo], F32, name="acc")
+                    todo[lo] = PASSES * (hi - lo)
+                todo[lo] = todo[lo] - width
                 nc.tensor.matmul_mx(
-                    out=banks[bank][:, m0 % BANK : m0 % BANK + width],
+                    out=banks[lo][:, m0 - lo : m0 - lo + width],
                     lhsT=w_sb[:, matrix * 2 * N : (matrix + 1) * 2 * N].bitcast(FP4X4),
                     lhsT_scale=ws_sb[:, matrix * N : (matrix + 1) * N],
                     rhs=codes[:, m0 - c0 : m0 - c0 + width].bitcast(FP8X4),
                     rhs_scale=scales[:, m0 - c0 : m0 - c0 + width],
                     start=first,
-                    stop=(todo[bank] == 0),
+                    stop=(todo[lo] == 0),
                 )
-                if todo[bank] == 0:
-                    for e in range(bank * BANK // C, (bank + 1) * BANK // C):
-                        at = e * C % BANK
-                        nc.scalar.activation(y[:, e * C : (e + 1) * C], banks[bank][:, at : at + C], GELU, bias=b_sb[:, e : e + 1])
+                if todo[lo] == 0:
+                    for e0 in range(lo, hi, C):
+                        e1 = min(e0 + C, hi)
+                        bias = b_sb[:, e0 // C : e0 // C + 1]
+                        nc.scalar.activation(y[:, e0:e1], banks[lo][:, e0 - lo : e1 - lo], GELU, bias=bias)
                 m0 = m0 + width
 
-        def quantise(r, xb):
-            a, n_s, n_v, n_g = ROUNDS[r]
+        def quantise(a, lo, hi, xb):
             at = 0
-            while at < n_s + n_v:
-                width = max(w for w in WIDTHS if at + w <= n_s + n_v)
+            while at < hi - lo:
+                width = max(w for w in WIDTHS if at + w <= hi - lo)
                 codes = cpool.tile([P, width], U32, name="codes", align_bytes=64)
                 scales = cpool.tile([P, width], U8, name="scales", align_bytes=64)
                 nc.vector.quantize_mx(
                     out=codes[:].bitcast(FP8X4), scales=scales[:], in_=xb[:, at * PACK : (at + width) * PACK]
                 )
-                multiply(a, starts[r] + at, starts[r] + at + width, codes, scales)
+                multiply(a, lo + at, lo + at + width, codes, scales)
                 at = at + width
 
         def raw_of_vector(r):
             return rawpool.tile([P, PACK, ROUNDS[r][2]], F32, name="raw_v%d" % r, offset=place_v[r % 2])
 
-        raw_s = scalar_gather(0)
-        raw_v = raw_of_vector(0)
-        vector_gather(0, raw_v, range(PACK))
         turned = spread.tile([P, P], F32, name="gate_ps")
         nc.tensor.transpose(turned[:], gate_rows[:], identity[:])
         nc.vector.tensor_copy(gate_cols[:], turned[:, 0 : S // P])
+        raw_s = scalar_gather(0)
+        raw_v = raw_of_vector(0)
+        vector_gather(0, raw_v, range(PACK))
+        spread_from = None
         for r, (a, n_s, n_v, n_g) in enumerate(ROUNDS):
             more = r + 1 < len(ROUNDS)
+            helps = more and ROUNDS[r + 1][2] > 0
             lo, n, n_m = starts[r], n_s + n_v, n_s + n_v - n_g
-            xb = keep.tile([P, n * PACK], BF16, name="xb", align_bytes=64)
-            times_gate(nc.gpsimd, RUN_G, xb[:, n_s * PACK : n * PACK], raw_v[:], gate_sb[:, lo + n_s : lo + n])
+            xb = keep.tile([P, n_m * PACK], BF16, name="xb%d" % (r % 2), align_bytes=64)
+            if n_g:
+                xg = keep.tile([P, n_g * PACK], BF16, name="xb%d" % ((r + 1) % 2), align_bytes=64)
+                weights = gate_first[:] if r == 0 else gate_sb[:, lo + n_m : lo + n]
             if n_m < n_s:
-                times_gate(nc.gpsimd, RUN_G, xb[:, n_m * PACK : n_s * PACK], raw_s[:, :, n_m:n_s], gate_sb[:, lo + n_m : lo + n_s])
-            shares = [(c0, min(c0 + BANK, n_m)) for c0 in range(0, n_m, BANK)]
-            gate_ps = [spread_gate(lo + c0, lo + c1) for c0, c1 in shares]
+                times_gate(nc.gpsimd, RUN_G, xg[:, 0 : (n_s - n_m) * PACK], raw_s[:, :, n_m:n_s], weights[:, 0 : n_s - n_m])
+            if n_v:
+                times_gate(nc.gpsimd, RUN_G, xg[:, (n_s - n_m) * PACK : n_g * PACK], raw_v[:], weights[:, n_s - n_m : n_g])
+            if spread_from != lo:
+                gate_ps = spread_gate(lo, lo + n_m)
+                spread_from = lo
             if more:
                 next_s = scalar_gather(r + 1)
+            if helps:
                 next_v = raw_of_vector(r + 1)
                 vector_gather(r + 1, next_v, range(PACK - 1))
-            for (c0, c1), bank in zip(shares, gate_ps):
-                times_gate(nc.vector, RUN, xb[:, c0 * PACK : c1 * PACK], raw_s[:, :, c0:c1], bank[:, 0 : c1 - c0])
-            if more:
+            times_gate(nc.vector, RUN, xb[:], raw_s[:, :, 0:n_m], gate_ps[:, 0:n_m])
+            if helps:
                 vector_gather(r + 1, next_v, [PACK - 1])
+            if more:
                 raw_s, raw_v = next_s, next_v
-            quantise(r, xb)
+            quantise(a, lo, lo + n_m, xb)
+            if n_g:
+                quantise(a, lo + n_m, lo + n, xg)
 
         parts = keep.tile([P, TOP, T], F32, name="gate_sb", align_bytes=64)
         total = keep.tile([P, T], F32, name="win0_0", align_bytes=64)

@@ -30,11 +30,12 @@ BANK = 512
 RUN = 4
 RUN_G = 2
 
-ROUNDS = [(0, 512, 512, 512), (1, 672, 352, 512), (0, 672, 352, 512), (1, 672, 352, 512), (0, 672, 352, 512),
-          (1, 672, 352, 512), (0, 672, 352, 512), (1, 416, 96, 256), (1, 256, 128, 128), (1, 128, 0, 0)]
+ROUNDS = [(0, 512, 512, 512), (0, 672, 352, 448), (1, 672, 352, 448), (1, 672, 352, 448), (0, 672, 352, 448),
+          (1, 672, 352, 448), (0, 704, 320, 320), (1, 384, 128, 128)]
+TAIL_CUTS = [S - BANK, S - C, S - P, S]
 FIRST_SPLIT = 768
 GROUP_CUTS = list(range(0, S - BANK + 1, BANK)) + [S - C, S - P, S]
-BACK_CUTS = [0, 128, 320, 576, 896, 1024]
+BACK_CUTS = [0, 256, 640, 896, 1024]
 WIDTHS = [1024, 512, 384, 256, 128]
 
 
@@ -55,10 +56,9 @@ def tile_moe_pre_lin_gelu_kernel(
         gate_sb = keep.tile([P, S], F32, name="gate_sb", align_bytes=64)
         size_s = 4 * PACK * max(n_s for a, n_s, n_v, n_g in ROUNDS)
         size_v = 4 * PACK * max(n_v for a, n_s, n_v, n_g in ROUNDS)
-        place_s = [i * size_s for i in range(3)]
-        place_v = [3 * size_s + i * size_v for i in range(2)]
-        gate_first = rawpool.tile([P, ROUNDS[0][3]], F32, name="gate_first", offset=place_s[2])
-        gate_rows = keep.tile([P, P], F32, name="gate_rows")
+        place_s = [0, size_s, 2 * size_s + 2 * size_v]
+        place_v = [2 * size_s + size_v, 2 * size_s]
+        gate_rows = rawpool.tile([P, P], F32, name="gate_rows", offset=place_v[1] - 2 * P)
         gate_cols = keep.tile([P, S // P], F32, name="gate_cols")
         identity = keep.tile([P, P], F32, name="identity")
         w_sb = keep.tile([P, E * PASSES * 2 * N], U8, name="w_sb", align_bytes=64)
@@ -78,8 +78,12 @@ def tile_moe_pre_lin_gelu_kernel(
         nc.gpsimd.memset(gate_rows[:], 0.0)
         make_identity(nc, identity[:])
 
+        def first_share(r):
+            a, n_s, n_v, n_g = ROUNDS[r]
+            return min((n_s + n_v - n_g) // P * P, BANK)
+
         needed = []
-        for lo, hi in sorted(set((lo + n_s + n_v - n_g, lo + n_s + n_v) for lo, (a, n_s, n_v, n_g) in zip(starts[1:], ROUNDS[1:]) if n_g)):
+        for lo, hi in sorted(set((starts[r] + first_share(r), starts[r] + n_s + n_v) for r, (a, n_s, n_v, n_g) in enumerate(ROUNDS))):
             if needed and lo <= needed[-1][1]:
                 needed[-1] = (needed[-1][0], max(hi, needed[-1][1]))
             else:
@@ -92,15 +96,13 @@ def tile_moe_pre_lin_gelu_kernel(
         nc.sync.dma_start(offs_sb[:], offs)
         nc.sync.dma_start(windows[0][0][:, FIRST_SPLIT:T], x_rows[0, 0][:, FIRST_SPLIT:T])
         nc.sync.dma_start(windows[0][1][:, 0:T], x_rows[0, 1])
-        nc.sync.dma_start(gate_rows[0 : S // P, :], gate[0, :].rearrange("(m n) -> m n", n=P))
         for t in range(2, PACK):
             nc.sync.dma_start(windows[0][t][:, 0:T], x_rows[0, t])
-        first_end = ROUNDS[0][1] + ROUNDS[0][2]
-        nc.sync.dma_start(gate_first[:], gate[0:P, first_end - ROUNDS[0][3] : first_end])
-        for t in range(PACK):
-            nc.sync.dma_start(windows[1][t][:, 0:T], x_rows[1, t])
+        nc.sync.dma_start(gate_rows[0 : S // P, :], gate[0, :].rearrange("(m n) -> m n", n=P))
         for lo, hi in needed[:2]:
             nc.sync.dma_start(gate_sb[:, lo:hi], gate[0:P, lo:hi])
+        for t in range(PACK):
+            nc.sync.dma_start(windows[1][t][:, 0:T], x_rows[1, t])
         nc.sync.dma_start(
             w_sb[:].bitcast(I32).rearrange("p (g n) -> p g n", g=E * PASSES),
             w_words.rearrange("e a p n -> p (e a) n").bitcast(I32),
@@ -119,11 +121,10 @@ def tile_moe_pre_lin_gelu_kernel(
         def listed(a, t, lo, hi):
             return windows[a][t][:].indirect(offs_sb[:, lo // LIST : hi // LIST])
 
-        def scalar_gather(r):
-            a, n_s, n_v, n_g = ROUNDS[r]
-            raw = rawpool.tile([P, PACK, n_s], F32, name="raw_s%d" % r, offset=place_s[r % 3])
+        def scalar_gather(r, a, lo, hi):
+            raw = rawpool.tile([P, PACK, hi - lo], F32, name="raw_s%d" % r, offset=place_s[r % 3])
             for t in range(PACK):
-                nc.scalar.activation(raw[:, t, :], listed(a, t, starts[r], starts[r] + n_s), COPY)
+                nc.scalar.activation(raw[:, t, :], listed(a, t, lo, hi), COPY)
             return raw
 
         def vector_gather(r, raw, planes):
@@ -193,58 +194,83 @@ def tile_moe_pre_lin_gelu_kernel(
         def raw_of_vector(r):
             return rawpool.tile([P, PACK, ROUNDS[r][2]], F32, name="raw_v%d" % r, offset=place_v[r % 2])
 
+        raw_s = scalar_gather(0, 0, 0, ROUNDS[0][1])
+        raw_v = raw_of_vector(0)
+        vector_gather(0, raw_v, range(PACK))
         turned = spread.tile([P, P], F32, name="gate_ps")
         nc.tensor.transpose(turned[:], gate_rows[:], identity[:])
         nc.vector.tensor_copy(gate_cols[:], turned[:, 0 : S // P])
-        raw_s = scalar_gather(0)
-        raw_v = raw_of_vector(0)
-        vector_gather(0, raw_v, range(PACK))
-        spread_from = None
+        spreads = {}
         for r, (a, n_s, n_v, n_g) in enumerate(ROUNDS):
             more = r + 1 < len(ROUNDS)
-            helps = more and ROUNDS[r + 1][2] > 0
             lo, n, n_m = starts[r], n_s + n_v, n_s + n_v - n_g
-            xb = keep.tile([P, n_m * PACK], BF16, name="xb%d" % (r % 2), align_bytes=64)
-            if n_g:
-                xg = keep.tile([P, n_g * PACK], BF16, name="xb%d" % ((r + 1) % 2), align_bytes=64)
-                weights = gate_first[:] if r == 0 else gate_sb[:, lo + n_m : lo + n]
+            half = first_share(r)
+            first = keep.tile([P, half * PACK], BF16, name="xb%d" % (r % 2), align_bytes=64)
+            second = keep.tile([P, (n - half) * PACK], BF16, name="xb%d" % ((r + 1) % 2), align_bytes=64)
             if n_m < n_s:
-                times_gate(nc.gpsimd, RUN_G, xg[:, 0 : (n_s - n_m) * PACK], raw_s[:, :, n_m:n_s], weights[:, 0 : n_s - n_m])
-            if n_v:
-                times_gate(nc.gpsimd, RUN_G, xg[:, (n_s - n_m) * PACK : n_g * PACK], raw_v[:], weights[:, n_s - n_m : n_g])
-            if spread_from != lo:
-                gate_ps = spread_gate(lo, lo + n_m)
-                spread_from = lo
+                at = n_m - half
+                times_gate(nc.gpsimd, RUN_G, second[:, at * PACK : (n_s - half) * PACK], raw_s[:, :, n_m:n_s], gate_sb[:, lo + n_m : lo + n_s])
+            times_gate(nc.gpsimd, RUN_G, second[:, (n_s - half) * PACK : (n - half) * PACK], raw_v[:], gate_sb[:, lo + n_s : lo + n])
+            if lo not in spreads:
+                spreads[lo] = spread_gate(lo, lo + half)
             if more:
-                next_s = scalar_gather(r + 1)
-            if helps:
+                next_s = scalar_gather(r + 1, ROUNDS[r + 1][0], starts[r + 1], starts[r + 1] + ROUNDS[r + 1][1])
                 next_v = raw_of_vector(r + 1)
                 vector_gather(r + 1, next_v, range(PACK - 1))
-            times_gate(nc.vector, RUN, xb[:], raw_s[:, :, 0:n_m], gate_ps[:, 0:n_m])
-            if helps:
+            times_gate(nc.vector, RUN, first[:], raw_s[:, :, 0:half], spreads[lo][:, 0:half])
+            if more:
                 vector_gather(r + 1, next_v, [PACK - 1])
+            if half < n_m:
+                times_gate(nc.vector, RUN, second[:, 0 : (n_m - half) * PACK], raw_s[:, :, half:n_m], gate_sb[:, lo + half : lo + n_m])
             if more:
                 raw_s, raw_v = next_s, next_v
-            quantise(a, lo, lo + n_m, xb)
-            if n_g:
-                quantise(a, lo + n_m, lo + n, xg)
+            quantise(a, lo, lo + half, first)
+            quantise(a, lo + half, lo + n, second)
 
-        parts = keep.tile([P, TOP, T], F32, name="gate_sb", align_bytes=64)
+        lo = TAIL_CUTS[0]
+        xb = keep.tile([P, (S - lo) * PACK], BF16, name="xb%d" % (len(ROUNDS) % 2), align_bytes=64)
+        gate_last = spread_gate(lo, S)
+        ranges = list(zip(TAIL_CUTS[:-1], TAIL_CUTS[1:]))
+        for i, (c0, c1) in enumerate(ranges):
+            raw_s = scalar_gather(len(ROUNDS) + i, PASSES - 1, c0, c1)
+            times_gate(nc.vector, RUN, xb[:, (c0 - lo) * PACK : (c1 - lo) * PACK], raw_s[:], gate_last[:, c0 - lo : c1 - lo])
+            if i > 0:
+                d0, d1 = ranges[i - 1]
+                quantise(PASSES - 1, d0, d1, xb[:, (d0 - lo) * PACK : (d1 - lo) * PACK])
+        quantise(PASSES - 1, c0, c1, xb[:, (c0 - lo) * PACK : (c1 - lo) * PACK])
+
+        parts = keep.tile([P, TOP - 1, T], F32, name="gate_sb", align_bytes=64)
+        joined = keep.tile([P, 2, T], F32, name="joined", align_bytes=64)
         total = keep.tile([P, T], F32, name="win0_0", align_bytes=64)
 
         def picked(r, lo, hi):
             return y[:].indirect(pos_sb[r][:, lo // LIST : hi // LIST])
 
-        def close(lo, hi):
-            nc.vector.tensor_tensor(total[:, lo:hi], parts[:, 2, lo:hi], parts[:, 3, lo:hi], ADD)
+        def fetch(r, lo, hi):
+            nc.scalar.activation(parts[:, r, lo:hi], picked(r, lo, hi), COPY)
+
+        def fetch_onto(r, onto, lo, hi):
+            nc.vector.tensor_tensor(joined[:, r - 2, lo:hi], picked(r, lo, hi), parts[:, onto, lo:hi], ADD)
+
+        def close(left, right, lo, hi):
+            nc.vector.tensor_tensor(total[:, lo:hi], left[:, lo:hi], right[:, lo:hi], ADD)
             nc.sync.dma_start(out[:, lo:hi], total[:, lo:hi])
 
-        ranges = list(zip(BACK_CUTS[:-1], BACK_CUTS[1:]))
-        for i, (lo, hi) in enumerate(ranges):
-            for r in range(2):
-                nc.scalar.activation(parts[:, r, lo:hi], picked(r, lo, hi), COPY)
-            nc.vector.tensor_tensor(parts[:, 2, lo:hi], picked(2, lo, hi), parts[:, 0, lo:hi], ADD)
-            if i > 0:
-                close(*ranges[i - 1])
-            nc.vector.tensor_tensor(parts[:, 3, lo:hi], picked(3, lo, hi), parts[:, 1, lo:hi], ADD)
-        close(*ranges[-1])
+        t0, t1, t2, t3, t4 = BACK_CUTS
+        for lo, hi in ((t0, t1), (t1, t2), (t2, t4)):
+            fetch(0, lo, hi)
+            fetch(1, lo, hi)
+        fetch(2, t2, t3)
+        fetch(2, t3, t4)
+        nc.vector.tensor_copy(parts[:, 2, t0:t1], picked(2, t0, t1))
+        fetch_onto(3, 0, t0, t1)
+        nc.vector.tensor_tensor(joined[:, 0, t0:t1], parts[:, 2, t0:t1], parts[:, 1, t0:t1], ADD)
+        close(joined[:, 0, :], joined[:, 1, :], t0, t1)
+        fetch_onto(2, 0, t1, t2)
+        fetch_onto(3, 1, t1, t2)
+        fetch_onto(3, 0, t2, t4)
+        close(joined[:, 0, :], joined[:, 1, :], t1, t2)
+        for lo, hi in ((t2, t3), (t3, t4)):
+            nc.vector.tensor_tensor(joined[:, 0, lo:hi], joined[:, 1, lo:hi], parts[:, 1, lo:hi], ADD)
+        for lo, hi in ((t2, t3), (t3, t4)):
+            close(joined[:, 0, :], parts[:, 2, :], lo, hi)

@@ -205,8 +205,8 @@ def tile_moe_pre_lin_gelu_kernel(
             more = r + 1 < len(ROUNDS)
             lo, n, n_m = starts[r], n_s + n_v, n_s + n_v - n_g
             half = first_share(r)
-            first = keep.tile([P, half * PACK], BF16, name="xb%d" % (r % 2), align_bytes=64)
-            second = keep.tile([P, (n - half) * PACK], BF16, name="xb%d" % ((r + 1) % 2), align_bytes=64)
+            xb = keep.tile([P, n * PACK], BF16, name="xb", align_bytes=64)
+            first, second = xb[:, 0 : half * PACK], xb[:, half * PACK : n * PACK]
             if n_m < n_s:
                 at = n_m - half
                 times_gate(nc.gpsimd, RUN_G, second[:, at * PACK : (n_s - half) * PACK], raw_s[:, :, n_m:n_s], gate_sb[:, lo + n_m : lo + n_s])
@@ -217,7 +217,7 @@ def tile_moe_pre_lin_gelu_kernel(
                 next_s = scalar_gather(r + 1, ROUNDS[r + 1][0], starts[r + 1], starts[r + 1] + ROUNDS[r + 1][1])
                 next_v = raw_of_vector(r + 1)
                 vector_gather(r + 1, next_v, range(PACK - 1))
-            times_gate(nc.vector, RUN, first[:], raw_s[:, :, 0:half], spreads[lo][:, 0:half])
+            times_gate(nc.vector, RUN, first, raw_s[:, :, 0:half], spreads[lo][:, 0:half])
             if more:
                 vector_gather(r + 1, next_v, [PACK - 1])
             if half < n_m:
@@ -228,7 +228,7 @@ def tile_moe_pre_lin_gelu_kernel(
             quantise(a, lo + half, lo + n, second)
 
         lo = TAIL_CUTS[0]
-        xb = keep.tile([P, (S - lo) * PACK], BF16, name="xb%d" % (len(ROUNDS) % 2), align_bytes=64)
+        xb = keep.tile([P, (S - lo) * PACK], BF16, name="xb", align_bytes=64)
         gate_last = spread_gate(lo, S)
         ranges = list(zip(TAIL_CUTS[:-1], TAIL_CUTS[1:]))
         for i, (c0, c1) in enumerate(ranges):

@@ -30,8 +30,8 @@ BANK = 512
 RUN = 4
 RUN_G = 2
 
-ROUNDS = [(0, 512, 512, 512), (0, 672, 352, 448), (1, 672, 352, 448), (1, 672, 352, 448), (0, 672, 352, 448),
-          (1, 672, 352, 448), (0, 704, 320, 320), (1, 384, 128, 128)]
+ROUNDS = [(0, 512, 512, 512), (0, 608, 416, 512), (1, 608, 416, 512), (1, 608, 416, 512), (0, 608, 416, 512),
+          (1, 608, 416, 512), (0, 704, 320, 320), (1, 384, 128, 128)]
 TAIL_CUTS = [S - BANK, S - C, S - P, S]
 FIRST_SPLIT = 768
 GROUP_CUTS = list(range(0, S - BANK + 1, BANK)) + [S - C, S - P, S]

@@ -29,9 +29,10 @@ WINDOW = T + 32
 BANK = 512
 RUN = 4
 RUN_G = 2
+STEP = 64
 
-ROUNDS = [(0, 512, 512, 512), (0, 608, 416, 512), (1, 608, 416, 512), (1, 608, 416, 512), (0, 608, 416, 512),
-          (1, 608, 416, 512), (0, 704, 320, 320), (1, 384, 128, 128)]
+ROUNDS = [(0, 512, 512, 512), (0, 672, 352, 512), (1, 672, 352, 512), (1, 672, 352, 512), (0, 672, 352, 512),
+          (1, 672, 352, 512), (0, 704, 320, 320), (1, 384, 128, 128)]
 TAIL_CUTS = [S - BANK, S - C, S - P, S]
 FIRST_SPLIT = 768
 GROUP_CUTS = list(range(0, S - BANK + 1, BANK)) + [S - C, S - P, S]
@@ -56,9 +57,20 @@ def tile_moe_pre_lin_gelu_kernel(
         gate_sb = keep.tile([P, S], F32, name="gate_sb", align_bytes=64)
         size_s = 4 * PACK * max(n_s for a, n_s, n_v, n_g in ROUNDS)
         size_v = 4 * PACK * max(n_v for a, n_s, n_v, n_g in ROUNDS)
-        place_s = [0, size_s, 2 * size_s + 2 * size_v]
-        place_v = [2 * size_s + size_v, 2 * size_s]
-        gate_rows = rawpool.tile([P, P], F32, name="gate_rows", offset=place_v[1] - 2 * P)
+        rounds = len(ROUNDS)
+        size_x = 2 * PACK * max(n_s + n_v for a, n_s, n_v, n_g in ROUNDS)
+        base_x = 2 * size_s + size_v
+        place_x = [base_x + STEP * (r // 2 if r % 2 == 0 else rounds - r // 2) for r in range(rounds + 1)]
+        end_x = [place_x[r] + 2 * PACK * (n_s + n_v) for r, (a, n_s, n_v, n_g) in enumerate(ROUNDS)]
+        beyond = base_x + STEP * rounds + size_x
+        place_v = []
+        for r, (a, n_s, n_v, n_g) in enumerate(ROUNDS):
+            if r % 2 == 0:
+                place_v.append(place_x[r] - 4 * PACK * n_v)
+            else:
+                place_v.append(beyond + size_v - 4 * PACK * n_v if r == 1 else end_x[r - 2] - STEP)
+        place_s = [0, beyond + size_v, size_s]
+        gate_rows = rawpool.tile([P, P], F32, name="gate_rows", offset=place_s[1] - 2 * P)
         gate_cols = keep.tile([P, S // P], F32, name="gate_cols")
         identity = keep.tile([P, P], F32, name="identity")
         w_sb = keep.tile([P, E * PASSES * 2 * N], U8, name="w_sb", align_bytes=64)
@@ -192,7 +204,7 @@ def tile_moe_pre_lin_gelu_kernel(
                 at = at + width
 
         def raw_of_vector(r):
-            return rawpool.tile([P, PACK, ROUNDS[r][2]], F32, name="raw_v%d" % r, offset=place_v[r % 2])
+            return rawpool.tile([P, PACK, ROUNDS[r][2]], F32, name="raw_v%d" % r, offset=place_v[r])
 
         raw_s = scalar_gather(0, 0, 0, ROUNDS[0][1])
         raw_v = raw_of_vector(0)
@@ -205,7 +217,7 @@ def tile_moe_pre_lin_gelu_kernel(
             more = r + 1 < len(ROUNDS)
             lo, n, n_m = starts[r], n_s + n_v, n_s + n_v - n_g
             half = first_share(r)
-            xb = keep.tile([P, n * PACK], BF16, name="xb", align_bytes=64)
+            xb = rawpool.tile([P, n * PACK], BF16, name="xb%d" % r, offset=place_x[r], align_bytes=64)
             first, second = xb[:, 0 : half * PACK], xb[:, half * PACK : n * PACK]
             if n_m < n_s:
                 at = n_m - half
@@ -228,7 +240,7 @@ def tile_moe_pre_lin_gelu_kernel(
             quantise(a, lo + half, lo + n, second)
 
         lo = TAIL_CUTS[0]
-        xb = keep.tile([P, (S - lo) * PACK], BF16, name="xb", align_bytes=64)
+        xb = rawpool.tile([P, (S - lo) * PACK], BF16, name="xb_last", offset=place_x[rounds], align_bytes=64)
         gate_last = spread_gate(lo, S)
         ranges = list(zip(TAIL_CUTS[:-1], TAIL_CUTS[1:]))
         for i, (c0, c1) in enumerate(ranges):

@@ -32,11 +32,11 @@ RUN_G = 2
 STEP = 64
 
 ROUNDS = [(0, 512, 512, 512), (0, 672, 352, 512), (1, 672, 352, 512), (1, 672, 352, 512), (0, 672, 352, 512),
-          (1, 672, 352, 512), (0, 704, 320, 320), (1, 384, 128, 128)]
+          (1, 672, 352, 512), (0, 768, 256, 256), (1, 512, 0, 128)]
 TAIL_CUTS = [S - BANK, S - C, S - P, S]
 FIRST_SPLIT = 768
 GROUP_CUTS = list(range(0, S - BANK + 1, BANK)) + [S - C, S - P, S]
-BACK_CUTS = [0, 256, 640, 896, 1024]
+BACK_CUTS = [0, 384, 640, 896, 1024]
 WIDTHS = [1024, 512, 384, 256, 128]
 
 
@@ -58,19 +58,20 @@ def tile_moe_pre_lin_gelu_kernel(
         size_s = 4 * PACK * max(n_s for a, n_s, n_v, n_g in ROUNDS)
         size_v = 4 * PACK * max(n_v for a, n_s, n_v, n_g in ROUNDS)
         rounds = len(ROUNDS)
-        size_x = 2 * PACK * max(n_s + n_v for a, n_s, n_v, n_g in ROUNDS)
-        base_x = 2 * size_s + size_v
-        place_x = [base_x + STEP * (r // 2 if r % 2 == 0 else rounds - r // 2) for r in range(rounds + 1)]
-        end_x = [place_x[r] + 2 * PACK * (n_s + n_v) for r, (a, n_s, n_v, n_g) in enumerate(ROUNDS)]
-        beyond = base_x + STEP * rounds + size_x
+        left = 2 * size_s + size_v
+        right = left + 2 * 2 * PACK * max(n_s + n_v - n_g for a, n_s, n_v, n_g in ROUNDS) + STEP * (rounds + 1)
+        left_start = [left + STEP * (r // 2) for r in range(rounds + 1)]
+        right_end = [right - STEP * ((r + 1) // 2) for r in range(rounds + 1)]
         place_v = []
         for r, (a, n_s, n_v, n_g) in enumerate(ROUNDS):
-            if r % 2 == 0:
-                place_v.append(place_x[r] - 4 * PACK * n_v)
-            else:
-                place_v.append(beyond + size_v - 4 * PACK * n_v if r == 1 else end_x[r - 2] - STEP)
-        place_s = [0, beyond + size_v, size_s]
-        gate_rows = rawpool.tile([P, P], F32, name="gate_rows", offset=place_s[1] - 2 * P)
+            place_v.append(right_end[r] if r % 2 == 0 else left_start[r] - 4 * PACK * n_v)
+        place_s = [0, place_v[1] - 4 * PACK * ROUNDS[1][1], right + size_v]
+        gate_rows = rawpool.tile([P, P], F32, name="gate_rows", offset=place_v[1] - 2 * P)
+
+        def rounded_tile(r, slots, on_left):
+            place = left_start[r] if on_left else right_end[r] - 2 * PACK * slots
+            return rawpool.tile([P, slots * PACK], BF16, name="xb%d_%d" % (r, on_left), offset=place, align_bytes=64)
+
         gate_cols = keep.tile([P, S // P], F32, name="gate_cols")
         identity = keep.tile([P, P], F32, name="identity")
         w_sb = keep.tile([P, E * PASSES * 2 * N], U8, name="w_sb", align_bytes=64)
@@ -90,12 +91,8 @@ def tile_moe_pre_lin_gelu_kernel(
         nc.gpsimd.memset(gate_rows[:], 0.0)
         make_identity(nc, identity[:])
 
-        def first_share(r):
-            a, n_s, n_v, n_g = ROUNDS[r]
-            return min((n_s + n_v - n_g) // P * P, BANK)
-
         needed = []
-        for lo, hi in sorted(set((starts[r] + first_share(r), starts[r] + n_s + n_v) for r, (a, n_s, n_v, n_g) in enumerate(ROUNDS))):
+        for lo, hi in sorted(set((starts[r] + n_s + n_v - n_g, starts[r] + n_s + n_v) for r, (a, n_s, n_v, n_g) in enumerate(ROUNDS))):
             if needed and lo <= needed[-1][1]:
                 needed[-1] = (needed[-1][0], max(hi, needed[-1][1]))
             else:
@@ -215,37 +212,42 @@ def tile_moe_pre_lin_gelu_kernel(
         spreads = {}
         for r, (a, n_s, n_v, n_g) in enumerate(ROUNDS):
             more = r + 1 < len(ROUNDS)
+            helps = more and ROUNDS[r + 1][2] > 0
             lo, n, n_m = starts[r], n_s + n_v, n_s + n_v - n_g
-            half = first_share(r)
-            xb = rawpool.tile([P, n * PACK], BF16, name="xb%d" % r, offset=place_x[r], align_bytes=64)
-            first, second = xb[:, 0 : half * PACK], xb[:, half * PACK : n * PACK]
+            first = rounded_tile(r, n_m, r % 2 == 0)
+            second = rounded_tile(r, n_g, r % 2 == 1)
             if n_m < n_s:
-                at = n_m - half
-                times_gate(nc.gpsimd, RUN_G, second[:, at * PACK : (n_s - half) * PACK], raw_s[:, :, n_m:n_s], gate_sb[:, lo + n_m : lo + n_s])
-            times_gate(nc.gpsimd, RUN_G, second[:, (n_s - half) * PACK : (n - half) * PACK], raw_v[:], gate_sb[:, lo + n_s : lo + n])
-            if lo not in spreads:
-                spreads[lo] = spread_gate(lo, lo + half)
+                times_gate(nc.gpsimd, RUN_G, second[:, 0 : (n_s - n_m) * PACK], raw_s[:, :, n_m:n_s], gate_sb[:, lo + n_m : lo + n_s])
+            if n_v:
+                times_gate(nc.gpsimd, RUN_G, second[:, (n_s - n_m) * PACK : n_g * PACK], raw_v[:], gate_sb[:, lo + n_s : lo + n])
+            shares = [(c0, min(c0 + BANK, n_m)) for c0 in range(0, n_m, BANK)]
+            for c0, c1 in shares:
+                if lo + c0 not in spreads:
+                    spreads[lo + c0] = spread_gate(lo + c0, lo + c0 + BANK)
             if more:
                 next_s = scalar_gather(r + 1, ROUNDS[r + 1][0], starts[r + 1], starts[r + 1] + ROUNDS[r + 1][1])
+            if helps:
                 next_v = raw_of_vector(r + 1)
                 vector_gather(r + 1, next_v, range(PACK - 1))
-            times_gate(nc.vector, RUN, first, raw_s[:, :, 0:half], spreads[lo][:, 0:half])
-            if more:
+            for c0, c1 in shares:
+                times_gate(nc.vector, RUN, first[:, c0 * PACK : c1 * PACK], raw_s[:, :, c0:c1], spreads[lo + c0][:, 0 : c1 - c0])
+            if helps:
                 vector_gather(r + 1, next_v, [PACK - 1])
-            if half < n_m:
-                times_gate(nc.vector, RUN, second[:, 0 : (n_m - half) * PACK], raw_s[:, :, half:n_m], gate_sb[:, lo + half : lo + n_m])
             if more:
                 raw_s, raw_v = next_s, next_v
-            quantise(a, lo, lo + half, first)
-            quantise(a, lo + half, lo + n, second)
+            quantise(a, lo, lo + n_m, first)
+            quantise(a, lo + n_m, lo + n, second)
 
         lo = TAIL_CUTS[0]
-        xb = rawpool.tile([P, (S - lo) * PACK], BF16, name="xb_last", offset=place_x[rounds], align_bytes=64)
-        gate_last = spread_gate(lo, S)
+        xb = rounded_tile(rounds, S - lo, rounds % 2 == 0)
+        gate_last = spreads[lo]
         ranges = list(zip(TAIL_CUTS[:-1], TAIL_CUTS[1:]))
+        raw_s = rawpool.tile([P, PACK, S - lo], F32, name="raw_last", offset=place_s[rounds % 3])
+        for c0 in range(lo, S, C):
+            for t in range(PACK):
+                nc.scalar.activation(raw_s[:, t, c0 - lo : c0 - lo + C], listed(PASSES - 1, t, c0, c0 + C), COPY)
         for i, (c0, c1) in enumerate(ranges):
-            raw_s = scalar_gather(len(ROUNDS) + i, PASSES - 1, c0, c1)
-            times_gate(nc.vector, RUN, xb[:, (c0 - lo) * PACK : (c1 - lo) * PACK], raw_s[:], gate_last[:, c0 - lo : c1 - lo])
+            times_gate(nc.vector, RUN, xb[:, (c0 - lo) * PACK : (c1 - lo) * PACK], raw_s[:, :, c0 - lo : c1 - lo], gate_last[:, c0 - lo : c1 - lo])
             if i > 0:
                 d0, d1 = ranges[i - 1]
                 quantise(PASSES - 1, d0, d1, xb[:, (d0 - lo) * PACK : (d1 - lo) * PACK])
@@ -268,21 +270,26 @@ def tile_moe_pre_lin_gelu_kernel(
             nc.vector.tensor_tensor(total[:, lo:hi], left[:, lo:hi], right[:, lo:hi], ADD)
             nc.sync.dma_start(out[:, lo:hi], total[:, lo:hi])
 
+        def join(lo, hi, left):
+            nc.vector.tensor_tensor(joined[:, 0, lo:hi], left[:, lo:hi], parts[:, 1, lo:hi], ADD)
+
         t0, t1, t2, t3, t4 = BACK_CUTS
-        for lo, hi in ((t0, t1), (t1, t2), (t2, t4)):
-            fetch(0, lo, hi)
-            fetch(1, lo, hi)
+        fetch(0, t1, t2)
+        fetch(1, t1, t2)
+        for r in range(2):
+            fetch(r, t0, t1)
+            fetch(r, t2, t4)
         fetch(2, t2, t3)
         fetch(2, t3, t4)
         nc.vector.tensor_copy(parts[:, 2, t0:t1], picked(2, t0, t1))
-        fetch_onto(3, 0, t0, t1)
-        nc.vector.tensor_tensor(joined[:, 0, t0:t1], parts[:, 2, t0:t1], parts[:, 1, t0:t1], ADD)
-        close(joined[:, 0, :], joined[:, 1, :], t0, t1)
         fetch_onto(2, 0, t1, t2)
         fetch_onto(3, 1, t1, t2)
-        fetch_onto(3, 0, t2, t4)
+        fetch_onto(3, 0, t0, t1)
         close(joined[:, 0, :], joined[:, 1, :], t1, t2)
-        for lo, hi in ((t2, t3), (t3, t4)):
-            nc.vector.tensor_tensor(joined[:, 0, lo:hi], joined[:, 1, lo:hi], parts[:, 1, lo:hi], ADD)
+        fetch_onto(3, 0, t2, t4)
+        join(t0, t1, parts[:, 2, :])
+        join(t2, t3, joined[:, 1, :])
+        close(joined[:, 0, :], joined[:, 1, :], t0, t1)
+        join(t3, t4, joined[:, 1, :])
         for lo, hi in ((t2, t3), (t3, t4)):
             close(joined[:, 0, :], parts[:, 2, :], lo, hi)

@@ -31,8 +31,8 @@ RUN = 4
 RUN_G = 2
 STEP = 64
 
-ROUNDS = [(0, 512, 512, 512), (0, 672, 352, 512), (1, 672, 352, 512), (1, 672, 352, 512), (0, 672, 352, 512),
-          (1, 672, 352, 512), (0, 768, 256, 256), (1, 512, 0, 128)]
+ROUNDS = [(0, 512, 512, 512), (0, 640, 384, 640), (1, 640, 384, 640), (1, 640, 384, 640), (0, 640, 384, 640),
+          (1, 640, 384, 512), (0, 768, 256, 256), (1, 512, 0, 128)]
 TAIL_CUTS = [S - BANK, S - C, S - P, S]
 FIRST_SPLIT = 768
 GROUP_CUTS = list(range(0, S - BANK + 1, BANK)) + [S - C, S - P, S]
@@ -210,6 +210,9 @@ def tile_moe_pre_lin_gelu_kernel(
         nc.tensor.transpose(turned[:], gate_rows[:], identity[:])
         nc.vector.tensor_copy(gate_cols[:], turned[:, 0 : S // P])
         spreads = {}
+        spread_end = {TAIL_CUTS[0]: S}
+        for lo, (a, n_s, n_v, n_g) in zip(starts, ROUNDS):
+            spread_end[lo] = max(spread_end.get(lo, lo), lo + min(BANK, n_s + n_v - n_g))
         for r, (a, n_s, n_v, n_g) in enumerate(ROUNDS):
             more = r + 1 < len(ROUNDS)
             helps = more and ROUNDS[r + 1][2] > 0
@@ -223,7 +226,7 @@ def tile_moe_pre_lin_gelu_kernel(
             shares = [(c0, min(c0 + BANK, n_m)) for c0 in range(0, n_m, BANK)]
             for c0, c1 in shares:
                 if lo + c0 not in spreads:
-                    spreads[lo + c0] = spread_gate(lo + c0, lo + c0 + BANK)
+                    spreads[lo + c0] = spread_gate(lo + c0, spread_end[lo + c0])
             if more:
                 next_s = scalar_gather(r + 1, ROUNDS[r + 1][0], starts[r + 1], starts[r + 1] + ROUNDS[r + 1][1])
             if helps:

@@ -29,15 +29,15 @@ WINDOW = T + 32
 BANK = 512
 RUN = 4
 RUN_G = 2
-STEP = 64
 
-ROUNDS = [(0, 512, 512, 512), (0, 640, 384, 640), (1, 640, 384, 640), (1, 640, 384, 640), (0, 640, 384, 640),
-          (1, 640, 384, 512), (0, 768, 256, 256), (1, 512, 0, 128)]
-TAIL_CUTS = [S - BANK, S - C, S - P, S]
+STEP = 64
+SPAN = 1024
+ORDER = [(0, 0), (0, 1), (1, 0), (1, 1), (0, 2), (1, 2), (0, 3), (1, 3)]
+GATHERED = [512,416,352,352,352,352,352,352]
+MULTIPLIED = [384,432,432,432,432,432,432,704]
 FIRST_SPLIT = 768
 GROUP_CUTS = list(range(0, S - BANK + 1, BANK)) + [S - C, S - P, S]
 BACK_CUTS = [0, 384, 640, 896, 1024]
-WIDTHS = [1024, 512, 384, 256, 128]
 
 
 def tile_moe_pre_lin_gelu_kernel(
@@ -46,8 +46,8 @@ def tile_moe_pre_lin_gelu_kernel(
     nc = tc.nc
     with ExitStack() as ctx:
         keep = ctx.enter_context(tc.tile_pool(name="keep", bufs=1))
-        rawpool = ctx.enter_context(tc.tile_pool(name="rawpool", bufs=1))
-        cpool = ctx.enter_context(tc.tile_pool(name="cpool", bufs=6))
+        lanes = ctx.enter_context(tc.tile_pool(name="lanes", bufs=1))
+        cpool = ctx.enter_context(tc.tile_pool(name="cpool", bufs=4))
         sums = ctx.enter_context(tc.psum_pool(name="sums", bufs=6))
         spread = ctx.enter_context(tc.psum_pool(name="spread", bufs=2))
 
@@ -55,35 +55,24 @@ def tile_moe_pre_lin_gelu_kernel(
         pos_sb = [keep.tile([P, T // LIST], U16, name="pos_sb%d" % r) for r in range(TOP)]
         windows = [[keep.tile([P, WINDOW], F32, name="win%d_%d" % (a, t), align_bytes=64) for t in range(PACK)] for a in range(PASSES)]
         gate_sb = keep.tile([P, S], F32, name="gate_sb", align_bytes=64)
-        size_s = 4 * PACK * max(n_s for a, n_s, n_v, n_g in ROUNDS)
-        size_v = 4 * PACK * max(n_v for a, n_s, n_v, n_g in ROUNDS)
-        rounds = len(ROUNDS)
-        left = 2 * size_s + size_v
-        right = left + 2 * 2 * PACK * max(n_s + n_v - n_g for a, n_s, n_v, n_g in ROUNDS) + STEP * (rounds + 1)
-        left_start = [left + STEP * (r // 2) for r in range(rounds + 1)]
-        right_end = [right - STEP * ((r + 1) // 2) for r in range(rounds + 1)]
-        place_v = []
-        for r, (a, n_s, n_v, n_g) in enumerate(ROUNDS):
-            place_v.append(right_end[r] if r % 2 == 0 else left_start[r] - 4 * PACK * n_v)
-        place_s = [0, place_v[1] - 4 * PACK * ROUNDS[1][1], right + size_v]
-        gate_rows = rawpool.tile([P, P], F32, name="gate_rows", offset=place_v[1] - 2 * P)
+        rounds = len(ORDER)
+        last = rounds - 1
+        raw_bytes = 4 * PACK * SPAN
+        half = raw_bytes // 2
+        lane_bytes = (rounds // 2 - 1) * (half + STEP) + raw_bytes
 
-        def rounded_tile(r, slots, on_left):
-            place = left_start[r] if on_left else right_end[r] - 2 * PACK * slots
-            return rawpool.tile([P, slots * PACK], BF16, name="xb%d_%d" % (r, on_left), offset=place, align_bytes=64)
+        def raw_place(r):
+            return (r % 2) * lane_bytes + (r // 2) * (half + STEP)
 
+        def rounded_place(r):
+            return raw_place(r - 1) if r > 0 else 2 * lane_bytes
+
+        gate_rows = lanes.tile([P, P], F32, name="gate_rows", offset=raw_place(1))
         gate_cols = keep.tile([P, S // P], F32, name="gate_cols")
         identity = keep.tile([P, P], F32, name="identity")
         w_sb = keep.tile([P, E * PASSES * 2 * N], U8, name="w_sb", align_bytes=64)
         ws_sb = keep.tile([P, E * PASSES * N], U8, name="ws_sb", align_bytes=64)
-        b_sb = keep.tile([P, E], F32, name="b_sb")
         y = keep.tile([P, S], F32, name="y")
-
-        starts = []
-        reached = [0] * PASSES
-        for a, n_s, n_v, n_g in ROUNDS:
-            starts.append(reached[a])
-            reached[a] = reached[a] + n_s + n_v
 
         x_rows = xT.rearrange("(a p t) c -> a t p c", a=PASSES, t=PACK)
 
@@ -92,11 +81,8 @@ def tile_moe_pre_lin_gelu_kernel(
         make_identity(nc, identity[:])
 
         needed = []
-        for lo, hi in sorted(set((starts[r] + n_s + n_v - n_g, starts[r] + n_s + n_v) for r, (a, n_s, n_v, n_g) in enumerate(ROUNDS))):
-            if needed and lo <= needed[-1][1]:
-                needed[-1] = (needed[-1][0], max(hi, needed[-1][1]))
-            else:
-                needed.append((lo, hi))
+        for j in range(S // SPAN):
+            needed.append((j * SPAN + min(n for n, (a, i) in zip(MULTIPLIED, ORDER) if i == j), (j + 1) * SPAN))
 
         nc.scalar.dma_start(windows[0][0][:, 0:FIRST_SPLIT], x_rows[0, 0][:, 0:FIRST_SPLIT])
         idle = keep.tile([P, 2], F32, name="idle")
@@ -104,8 +90,7 @@ def tile_moe_pre_lin_gelu_kernel(
         nc.scalar.activation(idle[:, 1:2], idle[:, 0:1], GELU)
         nc.sync.dma_start(offs_sb[:], offs)
         nc.sync.dma_start(windows[0][0][:, FIRST_SPLIT:T], x_rows[0, 0][:, FIRST_SPLIT:T])
-        nc.sync.dma_start(windows[0][1][:, 0:T], x_rows[0, 1])
-        for t in range(2, PACK):
+        for t in range(1, PACK):
             nc.sync.dma_start(windows[0][t][:, 0:T], x_rows[0, t])
         nc.sync.dma_start(gate_rows[0 : S // P, :], gate[0, :].rearrange("(m n) -> m n", n=P))
         for lo, hi in needed[:2]:
@@ -123,24 +108,25 @@ def tile_moe_pre_lin_gelu_kernel(
             )
         for lo, hi in needed[2:]:
             nc.sync.dma_start(gate_sb[:, lo:hi], gate[0:P, lo:hi])
-        nc.sync.dma_start(b_sb[:], b)
         for r, pos in enumerate((pos1, pos2, pos3, pos4)):
             nc.sync.dma_start(pos_sb[r][:], pos)
 
         def listed(a, t, lo, hi):
             return windows[a][t][:].indirect(offs_sb[:, lo // LIST : hi // LIST])
 
-        def scalar_gather(r, a, lo, hi):
-            raw = rawpool.tile([P, PACK, hi - lo], F32, name="raw_s%d" % r, offset=place_s[r % 3])
+        def scalar_gather(r):
+            a, j = ORDER[r]
+            raw = lanes.tile([P, PACK, SPAN], F32, name="raw%d" % r, offset=raw_place(r))
+            n = SPAN - GATHERED[r]
             for t in range(PACK):
-                nc.scalar.activation(raw[:, t, :], listed(a, t, lo, hi), COPY)
+                nc.scalar.activation(raw[:, t, 0:n], listed(a, t, j * SPAN, j * SPAN + n), COPY)
             return raw
 
-        def vector_gather(r, raw, planes):
-            a, n_s, n_v, n_g = ROUNDS[r]
-            lo = starts[r] + n_s
-            for t in planes:
-                nc.vector.tensor_copy(raw[:, t, :], listed(a, t, lo, lo + n_v))
+        def vector_gather(r, raw):
+            a, j = ORDER[r]
+            n = SPAN - GATHERED[r]
+            for t in range(PACK):
+                nc.vector.tensor_copy(raw[:, t, n:SPAN], listed(a, t, j * SPAN + n, (j + 1) * SPAN))
 
         def times_gate(engine, run, xb, raw, weights):
             width = weights.shape[1]
@@ -151,15 +137,21 @@ def tile_moe_pre_lin_gelu_kernel(
                 MULT,
             )
 
-        def spread_gate(lo, hi):
-            bank = spread.tile([P, BANK], F32, name="gate_ps")
-            for c0 in range(lo, hi, P):
-                m = c0 // P
-                nc.tensor.transpose(bank[:, c0 - lo : c0 - lo + P], gate_cols[:, m : m + 1].to_broadcast([P, P]), identity[:])
-            return bank
+        spreads = {}
+
+        def spread_gate(lo):
+            if lo not in spreads:
+                hi = max(j * SPAN + n for n, (a, j) in zip(MULTIPLIED, ORDER) if j == lo // SPAN)
+                bank = spread.tile([P, BANK], F32, name="gate_ps")
+                for c0 in range(lo, min(hi, lo + BANK), P):
+                    m = c0 // P
+                    nc.tensor.transpose(bank[:, c0 - lo : c0 - lo + P], gate_cols[:, m : m + 1].to_broadcast([P, P]), identity[:])
+                spreads[lo] = bank
+            return spreads[lo]
 
         banks = {}
         todo = {}
+        closed = []
 
         def multiply(a, c0, c1, codes, scales):
             m0 = c0
@@ -182,79 +174,59 @@ def tile_moe_pre_lin_gelu_kernel(
                     stop=(todo[lo] == 0),
                 )
                 if todo[lo] == 0:
-                    for e0 in range(lo, hi, C):
-                        e1 = min(e0 + C, hi)
-                        bias = b_sb[:, e0 // C : e0 // C + 1]
-                        nc.scalar.activation(y[:, e0:e1], banks[lo][:, e0 - lo : e1 - lo], GELU, bias=bias)
+                    closed.append((lo, hi))
                 m0 = m0 + width
 
-        def quantise(a, lo, hi, xb):
-            at = 0
-            while at < hi - lo:
-                width = max(w for w in WIDTHS if at + w <= hi - lo)
-                codes = cpool.tile([P, width], U32, name="codes", align_bytes=64)
-                scales = cpool.tile([P, width], U8, name="scales", align_bytes=64)
-                nc.vector.quantize_mx(
-                    out=codes[:].bitcast(FP8X4), scales=scales[:], in_=xb[:, at * PACK : (at + width) * PACK]
-                )
-                multiply(a, lo + at, lo + at + width, codes, scales)
-                at = at + width
+        def activate(b_sb):
+            for lo, hi in closed:
+                for e0 in range(lo, hi, C):
+                    e1 = min(e0 + C, hi)
+                    bias = b_sb[:, e0 // C : e0 // C + 1]
+                    nc.scalar.activation(y[:, e0:e1], banks[lo][:, e0 - lo : e1 - lo], GELU, bias=bias)
+            closed.clear()
 
-        def raw_of_vector(r):
-            return rawpool.tile([P, PACK, ROUNDS[r][2]], F32, name="raw_v%d" % r, offset=place_v[r])
+        def quantise(r, c0, c1, xb):
+            a, j = ORDER[r]
+            codes = cpool.tile([P, c1 - c0], U32, name="codes", align_bytes=64)
+            scales = cpool.tile([P, c1 - c0], U8, name="scales", align_bytes=64)
+            nc.vector.quantize_mx(out=codes[:].bitcast(FP8X4), scales=scales[:], in_=xb)
+            multiply(a, j * SPAN + c0, j * SPAN + c1, codes, scales)
 
-        raw_s = scalar_gather(0, 0, 0, ROUNDS[0][1])
-        raw_v = raw_of_vector(0)
-        vector_gather(0, raw_v, range(PACK))
+        raw = scalar_gather(0)
+        vector_gather(0, raw)
         turned = spread.tile([P, P], F32, name="gate_ps")
         nc.tensor.transpose(turned[:], gate_rows[:], identity[:])
         nc.vector.tensor_copy(gate_cols[:], turned[:, 0 : S // P])
-        spreads = {}
-        spread_end = {TAIL_CUTS[0]: S}
-        for lo, (a, n_s, n_v, n_g) in zip(starts, ROUNDS):
-            spread_end[lo] = max(spread_end.get(lo, lo), lo + min(BANK, n_s + n_v - n_g))
-        for r, (a, n_s, n_v, n_g) in enumerate(ROUNDS):
-            more = r + 1 < len(ROUNDS)
-            helps = more and ROUNDS[r + 1][2] > 0
-            lo, n, n_m = starts[r], n_s + n_v, n_s + n_v - n_g
-            first = rounded_tile(r, n_m, r % 2 == 0)
-            second = rounded_tile(r, n_g, r % 2 == 1)
-            if n_m < n_s:
-                times_gate(nc.gpsimd, RUN_G, second[:, 0 : (n_s - n_m) * PACK], raw_s[:, :, n_m:n_s], gate_sb[:, lo + n_m : lo + n_s])
-            if n_v:
-                times_gate(nc.gpsimd, RUN_G, second[:, (n_s - n_m) * PACK : n_g * PACK], raw_v[:], gate_sb[:, lo + n_s : lo + n])
-            shares = [(c0, min(c0 + BANK, n_m)) for c0 in range(0, n_m, BANK)]
-            for c0, c1 in shares:
-                if lo + c0 not in spreads:
-                    spreads[lo + c0] = spread_gate(lo + c0, spread_end[lo + c0])
-            if more:
-                next_s = scalar_gather(r + 1, ROUNDS[r + 1][0], starts[r + 1], starts[r + 1] + ROUNDS[r + 1][1])
-            if helps:
-                next_v = raw_of_vector(r + 1)
-                vector_gather(r + 1, next_v, range(PACK - 1))
-            for c0, c1 in shares:
-                times_gate(nc.vector, RUN, first[:, c0 * PACK : c1 * PACK], raw_s[:, :, c0:c1], spreads[lo + c0][:, 0 : c1 - c0])
-            if helps:
-                vector_gather(r + 1, next_v, [PACK - 1])
-            if more:
-                raw_s, raw_v = next_s, next_v
-            quantise(a, lo, lo + n_m, first)
-            quantise(a, lo + n_m, lo + n, second)
+        before = None
+        for r in range(last):
+            lo, n = ORDER[r][1] * SPAN, MULTIPLIED[r]
+            xb = lanes.tile([P, SPAN * PACK], BF16, name="xb%d" % r, offset=rounded_place(r), align_bytes=64)
+            times_gate(nc.gpsimd, RUN_G, xb[:, n * PACK :], raw[:, :, n:SPAN], gate_sb[:, lo + n : lo + SPAN])
+            ahead = scalar_gather(r + 1)
+            if r == 0:
+                vector_gather(r + 1, ahead)
+            times_gate(nc.vector, RUN, xb[:, 0 : n * PACK], raw[:, :, 0:n], spread_gate(lo)[:, 0:n])
+            if r > 0:
+                vector_gather(r + 1, ahead)
+                quantise(r - 1, 0, SPAN, before[:])
+            raw, before = ahead, xb
 
-        lo = TAIL_CUTS[0]
-        xb = rounded_tile(rounds, S - lo, rounds % 2 == 0)
-        gate_last = spreads[lo]
-        ranges = list(zip(TAIL_CUTS[:-1], TAIL_CUTS[1:]))
-        raw_s = rawpool.tile([P, PACK, S - lo], F32, name="raw_last", offset=place_s[rounds % 3])
-        for c0 in range(lo, S, C):
-            for t in range(PACK):
-                nc.scalar.activation(raw_s[:, t, c0 - lo : c0 - lo + C], listed(PASSES - 1, t, c0, c0 + C), COPY)
-        for i, (c0, c1) in enumerate(ranges):
-            times_gate(nc.vector, RUN, xb[:, (c0 - lo) * PACK : (c1 - lo) * PACK], raw_s[:, :, c0 - lo : c1 - lo], gate_last[:, c0 - lo : c1 - lo])
-            if i > 0:
-                d0, d1 = ranges[i - 1]
-                quantise(PASSES - 1, d0, d1, xb[:, (d0 - lo) * PACK : (d1 - lo) * PACK])
-        quantise(PASSES - 1, c0, c1, xb[:, (c0 - lo) * PACK : (c1 - lo) * PACK])
+        b_sb = lanes.tile([P, E], F32, name="b_sb", offset=raw_place(last - 2) + half)
+        nc.sync.dma_start(b_sb[:], b)
+        activate(b_sb)
+
+        lo, n = ORDER[last][1] * SPAN, MULTIPLIED[last]
+        front = lanes.tile([P, BANK * PACK], BF16, name="front", offset=rounded_place(last), align_bytes=64)
+        rear = lanes.tile([P, BANK * PACK], BF16, name="rear", offset=rounded_place(last) + half // 2, align_bytes=64)
+        times_gate(nc.gpsimd, RUN_G, rear[:, (n - BANK) * PACK :], raw[:, :, n:SPAN], gate_sb[:, lo + n : lo + SPAN])
+        times_gate(nc.vector, RUN, front[:], raw[:, :, 0:BANK], spread_gate(lo)[:, 0:BANK])
+        times_gate(nc.vector, RUN, rear[:, 0 : (n - BANK) * PACK], raw[:, :, BANK:n], spread_gate(lo + BANK)[:, 0 : n - BANK])
+        quantise(last - 1, 0, BANK, before[:, 0 : BANK * PACK])
+        quantise(last, 0, BANK, front[:])
+        quantise(last - 1, BANK, SPAN, before[:, BANK * PACK :])
+        for c0, c1 in ((0, C), (C, C + P), (C + P, BANK)):
+            quantise(last, BANK + c0, BANK + c1, rear[:, c0 * PACK : c1 * PACK])
+        activate(b_sb)
 
         parts = keep.tile([P, TOP - 1, T], F32, name="gate_sb", align_bytes=64)
         joined = keep.tile([P, 2, T], F32, name="joined", align_bytes=64)

@@ -29,15 +29,18 @@ WINDOW = T + 32
 BANK = 512
 RUN = 4
 RUN_G = 2
+STEP = 64
 
 STEP = 64
 SPAN = 1024
 ORDER = [(0, 0), (0, 1), (1, 0), (1, 1), (0, 2), (1, 2), (0, 3), (1, 3)]
-GATHERED = [512,416,352,352,352,352,352,352]
-MULTIPLIED = [384,432,432,432,432,432,432,704]
+GATHERED = [512,416,320,320,320,320,320,192]
+MULTIPLIED = [384,448,448,448,448,448,512,512]
 FIRST_SPLIT = 768
-GROUP_CUTS = list(range(0, S - BANK + 1, BANK)) + [S - C, S - P, S]
-BACK_CUTS = [0, 384, 640, 896, 1024]
+GROUP_CUTS = list(range(0, S - SPAN, BANK)) + list(range(S - SPAN, S, C)) + [S - P, S]
+FIRST_CUTS = [256, 384, 640, 1024]
+LAST_CUTS = [256, 640, 896, 1024]
+LATE = 192
 
 
 def tile_moe_pre_lin_gelu_kernel(
@@ -47,7 +50,7 @@ def tile_moe_pre_lin_gelu_kernel(
     with ExitStack() as ctx:
         keep = ctx.enter_context(tc.tile_pool(name="keep", bufs=1))
         lanes = ctx.enter_context(tc.tile_pool(name="lanes", bufs=1))
-        cpool = ctx.enter_context(tc.tile_pool(name="cpool", bufs=4))
+        cpool = ctx.enter_context(tc.tile_pool(name="cpool", bufs=6))
         sums = ctx.enter_context(tc.psum_pool(name="sums", bufs=6))
         spread = ctx.enter_context(tc.psum_pool(name="spread", bufs=2))
 
@@ -57,6 +60,7 @@ def tile_moe_pre_lin_gelu_kernel(
         gate_sb = keep.tile([P, S], F32, name="gate_sb", align_bytes=64)
         rounds = len(ORDER)
         last = rounds - 1
+        spans = [SPAN] * last + [SPAN - LATE]
         raw_bytes = 4 * PACK * SPAN
         half = raw_bytes // 2
         lane_bytes = (rounds // 2 - 1) * (half + STEP) + raw_bytes
@@ -116,17 +120,17 @@ def tile_moe_pre_lin_gelu_kernel(
 
         def scalar_gather(r):
             a, j = ORDER[r]
-            raw = lanes.tile([P, PACK, SPAN], F32, name="raw%d" % r, offset=raw_place(r))
-            n = SPAN - GATHERED[r]
+            raw = lanes.tile([P, PACK, spans[r]], F32, name="raw%d" % r, offset=raw_place(r) + 4 * PACK * (SPAN - spans[r]))
+            n = spans[r] - GATHERED[r]
             for t in range(PACK):
                 nc.scalar.activation(raw[:, t, 0:n], listed(a, t, j * SPAN, j * SPAN + n), COPY)
             return raw
 
         def vector_gather(r, raw):
             a, j = ORDER[r]
-            n = SPAN - GATHERED[r]
+            n = spans[r] - GATHERED[r]
             for t in range(PACK):
-                nc.vector.tensor_copy(raw[:, t, n:SPAN], listed(a, t, j * SPAN + n, (j + 1) * SPAN))
+                nc.vector.tensor_copy(raw[:, t, n : spans[r]], listed(a, t, j * SPAN + n, j * SPAN + spans[r]))
 
         def times_gate(engine, run, xb, raw, weights):
             width = weights.shape[1]
@@ -139,11 +143,10 @@ def tile_moe_pre_lin_gelu_kernel(
 
         spreads = {}
 
-        def spread_gate(lo):
+        def spread_gate(lo, hi):
             if lo not in spreads:
-                hi = max(j * SPAN + n for n, (a, j) in zip(MULTIPLIED, ORDER) if j == lo // SPAN)
                 bank = spread.tile([P, BANK], F32, name="gate_ps")
-                for c0 in range(lo, min(hi, lo + BANK), P):
+                for c0 in range(lo, hi, P):
                     m = c0 // P
                     nc.tensor.transpose(bank[:, c0 - lo : c0 - lo + P], gate_cols[:, m : m + 1].to_broadcast([P, P]), identity[:])
                 spreads[lo] = bank
@@ -205,25 +208,30 @@ def tile_moe_pre_lin_gelu_kernel(
             ahead = scalar_gather(r + 1)
             if r == 0:
                 vector_gather(r + 1, ahead)
-            times_gate(nc.vector, RUN, xb[:, 0 : n * PACK], raw[:, :, 0:n], spread_gate(lo)[:, 0:n])
+            times_gate(nc.vector, RUN, xb[:, 0 : n * PACK], raw[:, :, 0:n], spread_gate(lo, lo + BANK)[:, 0:n])
             if r > 0:
                 vector_gather(r + 1, ahead)
                 quantise(r - 1, 0, SPAN, before[:])
             raw, before = ahead, xb
 
+        a, j = ORDER[last]
+        late = lanes.tile([P, PACK, LATE], F32, name="late", offset=raw_place(last))
+        for t in range(PACK):
+            nc.scalar.activation(late[:, t, :], listed(a, t, S - LATE, S), COPY)
         b_sb = lanes.tile([P, E], F32, name="b_sb", offset=raw_place(last - 2) + half)
         nc.sync.dma_start(b_sb[:], b)
         activate(b_sb)
 
-        lo, n = ORDER[last][1] * SPAN, MULTIPLIED[last]
+        lo, n = j * SPAN, SPAN - LATE
         front = lanes.tile([P, BANK * PACK], BF16, name="front", offset=rounded_place(last), align_bytes=64)
         rear = lanes.tile([P, BANK * PACK], BF16, name="rear", offset=rounded_place(last) + half // 2, align_bytes=64)
-        times_gate(nc.gpsimd, RUN_G, rear[:, (n - BANK) * PACK :], raw[:, :, n:SPAN], gate_sb[:, lo + n : lo + SPAN])
-        times_gate(nc.vector, RUN, front[:], raw[:, :, 0:BANK], spread_gate(lo)[:, 0:BANK])
-        times_gate(nc.vector, RUN, rear[:, 0 : (n - BANK) * PACK], raw[:, :, BANK:n], spread_gate(lo + BANK)[:, 0 : n - BANK])
-        quantise(last - 1, 0, BANK, before[:, 0 : BANK * PACK])
-        quantise(last, 0, BANK, front[:])
-        quantise(last - 1, BANK, SPAN, before[:, BANK * PACK :])
+        times_gate(nc.gpsimd, RUN_G, rear[:, 0 : (n - BANK) * PACK], raw[:, :, BANK:n], gate_sb[:, lo + BANK : lo + n])
+        times_gate(nc.vector, RUN, front[:], raw[:, :, 0:BANK], spread_gate(lo, lo + BANK)[:])
+        times_gate(nc.vector, RUN, rear[:, (n - BANK) * PACK :], late[:], spread_gate(S - C, S)[:, C - LATE : C])
+        for c0 in range(0, SPAN, C):
+            quantise(last - 1, c0, c0 + C, before[:, c0 * PACK : (c0 + C) * PACK])
+            if c0 < BANK:
+                quantise(last, c0, c0 + C, front[:, c0 * PACK : (c0 + C) * PACK])
         for c0, c1 in ((0, C), (C, C + P), (C + P, BANK)):
             quantise(last, BANK + c0, BANK + c1, rear[:, c0 * PACK : c1 * PACK])
         activate(b_sb)
@@ -238,33 +246,28 @@ def tile_moe_pre_lin_gelu_kernel(
         def fetch(r, lo, hi):
             nc.scalar.activation(parts[:, r, lo:hi], picked(r, lo, hi), COPY)
 
-        def fetch_onto(r, onto, lo, hi):
-            nc.vector.tensor_tensor(joined[:, r - 2, lo:hi], picked(r, lo, hi), parts[:, onto, lo:hi], ADD)
+        def fetch_onto(into, r, onto, lo, hi):
+            nc.vector.tensor_tensor(into[:, lo:hi], picked(r, lo, hi), onto[:, lo:hi], ADD)
 
-        def close(left, right, lo, hi):
-            nc.vector.tensor_tensor(total[:, lo:hi], left[:, lo:hi], right[:, lo:hi], ADD)
+        def add(into, left, right, lo, hi):
+            nc.vector.tensor_tensor(into[:, lo:hi], left[:, lo:hi], right[:, lo:hi], ADD)
+
+        own = FIRST_CUTS[0]
+        shared = list(zip(FIRST_CUTS[:-1], FIRST_CUTS[1:]))
+        ends = list(zip(LAST_CUTS[:-1], LAST_CUTS[1:]))
+        for lo, hi in shared:
+            fetch(0, lo, hi)
+        fetch(1, own, T)
+        for lo, hi in ends:
+            fetch(2, lo, hi)
+        chain = [parts[:, 0, :], joined[:, 0, :], joined[:, 1, :], total]
+        nc.vector.tensor_copy(chain[0][:, 0:own], picked(0, 0, own))
+        for r, (lo, hi) in enumerate(shared):
+            fetch_onto(joined[:, 0, :], TOP - 1, parts[:, 0, :], lo, hi)
+            fetch_onto(chain[r + 1], r + 1, chain[r], 0, own)
+        nc.sync.dma_start(out[:, 0:own], total[:, 0:own])
+        add(joined[:, 1, :], joined[:, 0, :], parts[:, 1, :], own, LAST_CUTS[1])
+        add(joined[:, 1, :], joined[:, 0, :], parts[:, 1, :], LAST_CUTS[1], T)
+        for lo, hi in ends:
+            add(total, joined[:, 1, :], parts[:, 2, :], lo, hi)
             nc.sync.dma_start(out[:, lo:hi], total[:, lo:hi])
-
-        def join(lo, hi, left):
-            nc.vector.tensor_tensor(joined[:, 0, lo:hi], left[:, lo:hi], parts[:, 1, lo:hi], ADD)
-
-        t0, t1, t2, t3, t4 = BACK_CUTS
-        fetch(0, t1, t2)
-        fetch(1, t1, t2)
-        for r in range(2):
-            fetch(r, t0, t1)
-            fetch(r, t2, t4)
-        fetch(2, t2, t3)
-        fetch(2, t3, t4)
-        nc.vector.tensor_copy(parts[:, 2, t0:t1], picked(2, t0, t1))
-        fetch_onto(2, 0, t1, t2)
-        fetch_onto(3, 1, t1, t2)
-        fetch_onto(3, 0, t0, t1)
-        close(joined[:, 0, :], joined[:, 1, :], t1, t2)
-        fetch_onto(3, 0, t2, t4)
-        join(t0, t1, parts[:, 2, :])
-        join(t2, t3, joined[:, 1, :])
-        close(joined[:, 0, :], joined[:, 1, :], t0, t1)
-        join(t3, t4, joined[:, 1, :])
-        for lo, hi in ((t2, t3), (t3, t4)):
-            close(joined[:, 0, :], parts[:, 2, :], lo, hi)

@@ -34,8 +34,8 @@ STEP = 64
 STEP = 64
 SPAN = 1024
 ORDER = [(0, 0), (0, 1), (1, 0), (1, 1), (0, 2), (1, 2), (0, 3), (1, 3)]
-GATHERED = [512,416,320,320,320,320,320,192]
-MULTIPLIED = [384,448,448,448,448,448,512,512]
+GATHERED = [512,416,352,352,352,352,352,256]
+MULTIPLIED = [384,432,432,432,432,432,512,512]
 FIRST_SPLIT = 768
 GROUP_CUTS = list(range(0, S - SPAN, BANK)) + list(range(S - SPAN, S, C)) + [S - P, S]
 FIRST_CUTS = [256, 384, 640, 1024]

@@ -34,7 +34,7 @@ STEP = 64
 STEP = 64
 SPAN = 1024
 ORDER = [(0, 0), (0, 1), (1, 0), (1, 1), (0, 2), (1, 2), (0, 3), (1, 3)]
-GATHERED = [512,416,352,352,352,352,352,256]
+GATHERED = [2048,1792,1408,1408,1408,1408,1408,1024]
 MULTIPLIED = [384,432,432,432,432,432,512,512]
 FIRST_SPLIT = 768
 GROUP_CUTS = list(range(0, S - SPAN, BANK)) + list(range(S - SPAN, S, C)) + [S - P, S]
@@ -118,19 +118,24 @@ def tile_moe_pre_lin_gelu_kernel(
         def listed(a, t, lo, hi):
             return windows[a][t][:].indirect(offs_sb[:, lo // LIST : hi // LIST])
 
+        def shares(r):
+            if r == 0:
+                return [(t, spans[r] - GATHERED[r] // PACK) for t in range(PACK)]
+            return [(t, min(spans[r], max(0, (PACK - t) * spans[r] - GATHERED[r]))) for t in range(PACK)]
+
         def scalar_gather(r):
             a, j = ORDER[r]
             raw = lanes.tile([P, PACK, spans[r]], F32, name="raw%d" % r, offset=raw_place(r) + 4 * PACK * (SPAN - spans[r]))
-            n = spans[r] - GATHERED[r]
-            for t in range(PACK):
-                nc.scalar.activation(raw[:, t, 0:n], listed(a, t, j * SPAN, j * SPAN + n), COPY)
+            for t, n in shares(r):
+                if n > 0:
+                    nc.scalar.activation(raw[:, t, 0:n], listed(a, t, j * SPAN, j * SPAN + n), COPY)
             return raw
 
         def vector_gather(r, raw):
             a, j = ORDER[r]
-            n = spans[r] - GATHERED[r]
-            for t in range(PACK):
-                nc.vector.tensor_copy(raw[:, t, n : spans[r]], listed(a, t, j * SPAN + n, j * SPAN + spans[r]))
+            for t, n in shares(r) if r == 0 else reversed(shares(r)):
+                if n < spans[r]:
+                    nc.vector.tensor_copy(raw[:, t, n : spans[r]], listed(a, t, j * SPAN + n, j * SPAN + spans[r]))
 
         def times_gate(engine, run, xb, raw, weights):
             width = weights.shape[1]
@@ -204,11 +209,11 @@ def tile_moe_pre_lin_gelu_kernel(
         for r in range(last):
             lo, n = ORDER[r][1] * SPAN, MULTIPLIED[r]
             xb = lanes.tile([P, SPAN * PACK], BF16, name="xb%d" % r, offset=rounded_place(r), align_bytes=64)
-            times_gate(nc.gpsimd, RUN_G, xb[:, n * PACK :], raw[:, :, n:SPAN], gate_sb[:, lo + n : lo + SPAN])
             ahead = scalar_gather(r + 1)
             if r == 0:
                 vector_gather(r + 1, ahead)
             times_gate(nc.vector, RUN, xb[:, 0 : n * PACK], raw[:, :, 0:n], spread_gate(lo, lo + BANK)[:, 0:n])
+            times_gate(nc.gpsimd, RUN_G, xb[:, n * PACK :], raw[:, :, n:SPAN], gate_sb[:, lo + n : lo + SPAN])
             if r > 0:
                 vector_gather(r + 1, ahead)
                 quantise(r - 1, 0, SPAN, before[:])

@@ -121,7 +121,7 @@ def tile_moe_pre_lin_gelu_kernel(
         def shares(r):
             if r == 0:
                 return [(t, spans[r] - GATHERED[r] // PACK) for t in range(PACK)]
-            return [(t, min(spans[r], max(0, (PACK - t) * spans[r] - GATHERED[r]))) for t in range(PACK)]
+            return [(t, min(spans[r], max(0, (t + 1) * spans[r] - GATHERED[r]))) for t in range(PACK)]
 
         def scalar_gather(r):
             a, j = ORDER[r]
@@ -133,7 +133,7 @@ def tile_moe_pre_lin_gelu_kernel(
 
         def vector_gather(r, raw):
             a, j = ORDER[r]
-            for t, n in shares(r) if r == 0 else reversed(shares(r)):
+            for t, n in shares(r):
                 if n < spans[r]:
                     nc.vector.tensor_copy(raw[:, t, n : spans[r]], listed(a, t, j * SPAN + n, j * SPAN + spans[r]))
 

@@ -35,7 +35,7 @@ STEP = 64
 SPAN = 1024
 ORDER = [(0, 0), (0, 1), (1, 0), (1, 1), (0, 2), (1, 2), (0, 3), (1, 3)]
 GATHERED = [2048,1792,1408,1408,1408,1408,1408,1024]
-MULTIPLIED = [384,432,432,432,432,432,512,512]
+MULTIPLIED = [384,456,456,456,456,456,512,512]
 FIRST_SPLIT = 768
 GROUP_CUTS = list(range(0, S - SPAN, BANK)) + list(range(S - SPAN, S, C)) + [S - P, S]
 FIRST_CUTS = [256, 384, 640, 1024]

@@ -1,7 +1,6 @@
 from contextlib import ExitStack
 
 import concourse.mybir as mybir
-from concourse.masks import make_identity
 
 K, T, E, C, N = 1024, 1024, 16, 256, 128
 S = E * C
@@ -30,12 +29,11 @@ BANK = 512
 RUN = 4
 RUN_G = 2
 STEP = 64
-
-STEP = 64
+QUAD = 32
 SPAN = 1024
 ORDER = [(0, 0), (0, 1), (1, 0), (1, 1), (0, 2), (1, 2), (0, 3), (1, 3)]
-GATHERED = [2048,1792,1408,1408,1408,1408,1408,1024]
-MULTIPLIED = [384,456,456,456,456,456,512,512]
+GATHERED = [0, 0, 1408, 1344, 1344, 1344, 1344, 1024]
+MULTIPLIED = [0, 640, 456, 456, 456, 456, 512, 512]
 FIRST_SPLIT = 768
 GROUP_CUTS = list(range(0, S - SPAN, BANK)) + list(range(S - SPAN, S, C)) + [S - P, S]
 FIRST_CUTS = [256, 384, 640, 1024]
@@ -66,41 +64,58 @@ def tile_moe_pre_lin_gelu_kernel(
         lane_bytes = (rounds // 2 - 1) * (half + STEP) + raw_bytes
 
         def raw_place(r):
-            return (r % 2) * lane_bytes + (r // 2) * (half + STEP)
+            if r == 0:
+                return raw_bytes
+            return ((r - 1) % 2) * lane_bytes + ((r - 1) // 2) * (half + STEP)
 
         def rounded_place(r):
-            return raw_place(r - 1) if r > 0 else 2 * lane_bytes
+            return raw_place(r - 1) if r > 1 else lane_bytes + raw_bytes + r * (half + STEP)
 
-        gate_rows = lanes.tile([P, P], F32, name="gate_rows", offset=raw_place(1))
+        gate_rows = [lanes.tile([P, P], F32, name="gate_rows%d" % h, offset=place) for h, place in enumerate((raw_place(1), rounded_place(1)))]
+        rows = S // P // 2
         gate_cols = keep.tile([P, S // P], F32, name="gate_cols")
         identity = keep.tile([P, P], F32, name="identity")
+        ones = keep.tile([P, QUAD], F32, name="ones", align_bytes=64)
+        column = keep.tile([P, QUAD], F32, name="column", align_bytes=64)
+        row = keep.tile([P, QUAD], F32, name="row", align_bytes=64)
         w_sb = keep.tile([P, E * PASSES * 2 * N], U8, name="w_sb", align_bytes=64)
         ws_sb = keep.tile([P, E * PASSES * N], U8, name="ws_sb", align_bytes=64)
         y = keep.tile([P, S], F32, name="y")
 
         x_rows = xT.rearrange("(a p t) c -> a t p c", a=PASSES, t=PACK)
 
+        idle = keep.tile([P, 2], F32, name="idle")
+        nc.vector.memset(idle[:, 0:1], 0.0)
         nc.vector.memset(ws_sb[:].bitcast(I32), 0)
-        nc.gpsimd.memset(gate_rows[:], 0.0)
-        make_identity(nc, identity[:])
+        for h in range(2):
+            nc.gpsimd.memset(gate_rows[h][:], 0.0)
+        nc.vector.memset(ones[:], 1.0)
+        nc.gpsimd.memset(identity[:], 0.0)
+        nc.vector.tensor_tensor_scan(column[:], ones[:], ones[:], 0.0, MULT, ADD)
+        nc.vector.transpose(row[:], column[:])
+        for q in range(0, P, QUAD):
+            nc.vector.tensor_tensor(identity[q : q + QUAD, q : q + QUAD], column[q : q + QUAD, :], row[q : q + QUAD, :], mybir.AluOpType.is_equal)
 
         needed = []
         for j in range(S // SPAN):
             needed.append((j * SPAN + min(n for n, (a, i) in zip(MULTIPLIED, ORDER) if i == j), (j + 1) * SPAN))
 
         nc.scalar.dma_start(windows[0][0][:, 0:FIRST_SPLIT], x_rows[0, 0][:, 0:FIRST_SPLIT])
-        idle = keep.tile([P, 2], F32, name="idle")
-        nc.vector.memset(idle[:, 0:1], 0.0)
         nc.scalar.activation(idle[:, 1:2], idle[:, 0:1], GELU)
         nc.sync.dma_start(offs_sb[:], offs)
         nc.sync.dma_start(windows[0][0][:, FIRST_SPLIT:T], x_rows[0, 0][:, FIRST_SPLIT:T])
-        for t in range(1, PACK):
+        nc.sync.dma_start(windows[0][1][:, 0:T], x_rows[0, 1])
+        gate_row = gate[0, :].rearrange("(h m n) -> h m n", h=2, n=P)
+        nc.sync.dma_start(gate_rows[0][0:rows, :], gate_row[0])
+        nc.sync.dma_start(gate_sb[:, 0:SPAN], gate[0:P, 0:SPAN])
+        for t in range(2, PACK):
             nc.sync.dma_start(windows[0][t][:, 0:T], x_rows[0, t])
-        nc.sync.dma_start(gate_rows[0 : S // P, :], gate[0, :].rearrange("(m n) -> m n", n=P))
-        for lo, hi in needed[:2]:
-            nc.sync.dma_start(gate_sb[:, lo:hi], gate[0:P, lo:hi])
-        for t in range(PACK):
+        nc.sync.dma_start(windows[1][0][:, 0:T], x_rows[1, 0])
+        nc.sync.dma_start(gate_rows[1][0:rows, :], gate_row[1])
+        for t in range(1, PACK):
             nc.sync.dma_start(windows[1][t][:, 0:T], x_rows[1, t])
+        lo, hi = needed[1]
+        nc.sync.dma_start(gate_sb[:, lo:hi], gate[0:P, lo:hi])
         nc.sync.dma_start(
             w_sb[:].bitcast(I32).rearrange("p (g n) -> p g n", g=E * PASSES),
             w_words.rearrange("e a p n -> p (e a) n").bitcast(I32),
@@ -119,8 +134,6 @@ def tile_moe_pre_lin_gelu_kernel(
             return windows[a][t][:].indirect(offs_sb[:, lo // LIST : hi // LIST])
 
         def shares(r):
-            if r == 0:
-                return [(t, spans[r] - GATHERED[r] // PACK) for t in range(PACK)]
             return [(t, min(spans[r], max(0, (t + 1) * spans[r] - GATHERED[r]))) for t in range(PACK)]
 
         def scalar_gather(r):
@@ -131,20 +144,24 @@ def tile_moe_pre_lin_gelu_kernel(
                     nc.scalar.activation(raw[:, t, 0:n], listed(a, t, j * SPAN, j * SPAN + n), COPY)
             return raw
 
-        def vector_gather(r, raw):
+        def vector_gather(r, raw, t0, t1):
             a, j = ORDER[r]
-            for t, n in shares(r):
+            for t, n in shares(r)[t0:t1]:
                 if n < spans[r]:
                     nc.vector.tensor_copy(raw[:, t, n : spans[r]], listed(a, t, j * SPAN + n, j * SPAN + spans[r]))
 
         def times_gate(engine, run, xb, raw, weights):
             width = weights.shape[1]
+            planes = raw.shape[1]
             engine.tensor_tensor(
-                xb.rearrange("p (c i t) -> p c t i", i=run, t=PACK),
+                xb.rearrange("p (c i) t -> p c t i", i=run),
                 raw.rearrange("p t (c i) -> p c t i", i=run),
-                weights.rearrange("p (c i) -> p c i", i=run).unsqueeze(2).to_broadcast([P, width // run, PACK, run]),
+                weights.rearrange("p (c i) -> p c i", i=run).unsqueeze(2).to_broadcast([P, width // run, planes, run]),
                 MULT,
             )
+
+        def by_slot(xb):
+            return xb.rearrange("p (s t) -> p s t", t=PACK)
 
         spreads = {}
 
@@ -200,23 +217,36 @@ def tile_moe_pre_lin_gelu_kernel(
             nc.vector.quantize_mx(out=codes[:].bitcast(FP8X4), scales=scales[:], in_=xb)
             multiply(a, j * SPAN + c0, j * SPAN + c1, codes, scales)
 
-        raw = scalar_gather(0)
-        vector_gather(0, raw)
-        turned = spread.tile([P, P], F32, name="gate_ps")
-        nc.tensor.transpose(turned[:], gate_rows[:], identity[:])
-        nc.vector.tensor_copy(gate_cols[:], turned[:, 0 : S // P])
-        before = None
-        for r in range(last):
+        raw0 = lanes.tile([P, PACK, SPAN], F32, name="raw0", offset=raw_place(0))
+        raw1 = lanes.tile([P, PACK, SPAN], F32, name="raw1", offset=raw_place(1))
+        middle = SPAN // 2
+        for t in range(2):
+            nc.scalar.activation(raw0[:, t, 0:middle], listed(0, t, 0, middle), COPY)
+            nc.vector.tensor_copy(raw0[:, t, middle:SPAN], listed(0, t, middle, SPAN))
+        turned = spread.tile([P, 2, P], F32, name="gate_ps")
+        nc.tensor.transpose(turned[:, 0, :], gate_rows[0][:], identity[:])
+        nc.vector.tensor_copy(gate_cols[:, 0:rows], turned[:, 0, 0:rows])
+        for raw, t, lo in ((raw1, 0, SPAN), (raw0, 2, 0), (raw1, 2, SPAN)):
+            nc.vector.tensor_copy(raw[:, t, :], listed(0, t, lo, lo + SPAN))
+            nc.scalar.activation(raw[:, t + 1, :], listed(0, t + 1, lo, lo + SPAN), COPY)
+        nc.tensor.transpose(turned[:, 1, :], gate_rows[1][:], identity[:])
+        nc.scalar.copy(gate_cols[:, rows:], turned[:, 1, 0:rows])
+        before = lanes.tile([P, SPAN * PACK], BF16, name="xb0", offset=rounded_place(0), align_bytes=64)
+        for t in (0, 2):
+            times_gate(nc.gpsimd, RUN_G, by_slot(before[:])[:, :, t : t + 2], raw0[:, t : t + 2, :], gate_sb[:, 0:SPAN])
+        raw = raw1
+        for r in range(1, last):
             lo, n = ORDER[r][1] * SPAN, MULTIPLIED[r]
             xb = lanes.tile([P, SPAN * PACK], BF16, name="xb%d" % r, offset=rounded_place(r), align_bytes=64)
             ahead = scalar_gather(r + 1)
-            if r == 0:
-                vector_gather(r + 1, ahead)
-            times_gate(nc.vector, RUN, xb[:, 0 : n * PACK], raw[:, :, 0:n], spread_gate(lo, lo + BANK)[:, 0:n])
-            times_gate(nc.gpsimd, RUN_G, xb[:, n * PACK :], raw[:, :, n:SPAN], gate_sb[:, lo + n : lo + SPAN])
-            if r > 0:
-                vector_gather(r + 1, ahead)
-                quantise(r - 1, 0, SPAN, before[:])
+            if r == 1:
+                vector_gather(r + 1, ahead, 0, 1)
+            for c0 in range(0, n, BANK):
+                c1 = min(n, c0 + BANK)
+                times_gate(nc.vector, RUN, by_slot(xb[:])[:, c0:c1, :], raw[:, :, c0:c1], spread_gate(lo + c0, lo + c1)[:, 0 : c1 - c0])
+            times_gate(nc.gpsimd, RUN_G, by_slot(xb[:])[:, n:SPAN, :], raw[:, :, n:SPAN], gate_sb[:, lo + n : lo + SPAN])
+            vector_gather(r + 1, ahead, 1 if r == 1 else 0, PACK)
+            quantise(r - 1, 0, SPAN, before[:])
             raw, before = ahead, xb
 
         a, j = ORDER[last]
@@ -230,15 +260,17 @@ def tile_moe_pre_lin_gelu_kernel(
         lo, n = j * SPAN, SPAN - LATE
         front = lanes.tile([P, BANK * PACK], BF16, name="front", offset=rounded_place(last), align_bytes=64)
         rear = lanes.tile([P, BANK * PACK], BF16, name="rear", offset=rounded_place(last) + half // 2, align_bytes=64)
-        times_gate(nc.gpsimd, RUN_G, rear[:, 0 : (n - BANK) * PACK], raw[:, :, BANK:n], gate_sb[:, lo + BANK : lo + n])
-        times_gate(nc.vector, RUN, front[:], raw[:, :, 0:BANK], spread_gate(lo, lo + BANK)[:])
-        times_gate(nc.vector, RUN, rear[:, (n - BANK) * PACK :], late[:], spread_gate(S - C, S)[:, C - LATE : C])
-        for c0 in range(0, SPAN, C):
-            quantise(last - 1, c0, c0 + C, before[:, c0 * PACK : (c0 + C) * PACK])
-            if c0 < BANK:
-                quantise(last, c0, c0 + C, front[:, c0 * PACK : (c0 + C) * PACK])
-        for c0, c1 in ((0, C), (C, C + P), (C + P, BANK)):
-            quantise(last, BANK + c0, BANK + c1, rear[:, c0 * PACK : c1 * PACK])
+        times_gate(nc.gpsimd, RUN_G, by_slot(rear[:])[:, 0 : n - BANK, :], raw[:, :, BANK:n], gate_sb[:, lo + BANK : lo + n])
+        times_gate(nc.vector, RUN, by_slot(front[:]), raw[:, :, 0:BANK], spread_gate(lo, lo + BANK)[:])
+        times_gate(nc.vector, RUN, by_slot(rear[:])[:, n - BANK :, :], late[:], spread_gate(S - C, S)[:, C - LATE : C])
+        for c0, c1 in zip(GROUP_CUTS[:-1], GROUP_CUTS[1:]):
+            if c0 >= lo:
+                c0, c1 = c0 - lo, c1 - lo
+                quantise(last - 1, c0, c1, before[:, c0 * PACK : c1 * PACK])
+                if c0 < BANK:
+                    quantise(last, c0, c1, front[:, c0 * PACK : c1 * PACK])
+                else:
+                    quantise(last, c0, c1, rear[:, (c0 - BANK) * PACK : (c1 - BANK) * PACK])
         activate(b_sb)
 
         parts = keep.tile([P, TOP - 1, T], F32, name="gate_sb", align_bytes=64)

@@ -27,7 +27,7 @@ LIST = 16
 WINDOW = T + 32
 BANK = 512
 RUN = 4
-RUN_G = 2
+RUN_G = 4
 STEP = 64
 QUAD = 32
 SPAN = 1024

@@ -36,8 +36,7 @@ GATHERED = [0, 0, 1408, 1344, 1344, 1344, 1344, 1024]
 MULTIPLIED = [0, 640, 456, 456, 456, 456, 512, 512]
 FIRST_SPLIT = 768
 GROUP_CUTS = list(range(0, S - SPAN, BANK)) + list(range(S - SPAN, S, C)) + [S - P, S]
-FIRST_CUTS = [256, 384, 640, 1024]
-LAST_CUTS = [256, 640, 896, 1024]
+BACK_CUTS = (256, 640, 832)
 LATE = 192
 
 
@@ -86,13 +85,13 @@ def tile_moe_pre_lin_gelu_kernel(
 
         idle = keep.tile([P, 2], F32, name="idle")
         nc.vector.memset(idle[:, 0:1], 0.0)
-        nc.vector.memset(ws_sb[:].bitcast(I32), 0)
-        for h in range(2):
-            nc.gpsimd.memset(gate_rows[h][:], 0.0)
         nc.vector.memset(ones[:], 1.0)
-        nc.gpsimd.memset(identity[:], 0.0)
+        for h in range(2):
+            nc.vector.memset(gate_rows[h][:], 0.0)
         nc.vector.tensor_tensor_scan(column[:], ones[:], ones[:], 0.0, MULT, ADD)
+        nc.vector.memset(identity[:], 0.0)
         nc.vector.transpose(row[:], column[:])
+        nc.vector.memset(ws_sb[:].bitcast(I32), 0)
         for q in range(0, P, QUAD):
             nc.vector.tensor_tensor(identity[q : q + QUAD, q : q + QUAD], column[q : q + QUAD, :], row[q : q + QUAD, :], mybir.AluOpType.is_equal)
 
@@ -289,22 +288,24 @@ def tile_moe_pre_lin_gelu_kernel(
         def add(into, left, right, lo, hi):
             nc.vector.tensor_tensor(into[:, lo:hi], left[:, lo:hi], right[:, lo:hi], ADD)
 
-        own = FIRST_CUTS[0]
-        shared = list(zip(FIRST_CUTS[:-1], FIRST_CUTS[1:]))
-        ends = list(zip(LAST_CUTS[:-1], LAST_CUTS[1:]))
-        for lo, hi in shared:
-            fetch(0, lo, hi)
-        fetch(1, own, T)
-        for lo, hi in ends:
-            fetch(2, lo, hi)
-        chain = [parts[:, 0, :], joined[:, 0, :], joined[:, 1, :], total]
-        nc.vector.tensor_copy(chain[0][:, 0:own], picked(0, 0, own))
-        for r, (lo, hi) in enumerate(shared):
-            fetch_onto(joined[:, 0, :], TOP - 1, parts[:, 0, :], lo, hi)
-            fetch_onto(chain[r + 1], r + 1, chain[r], 0, own)
-        nc.sync.dma_start(out[:, 0:own], total[:, 0:own])
-        add(joined[:, 1, :], joined[:, 0, :], parts[:, 1, :], own, LAST_CUTS[1])
-        add(joined[:, 1, :], joined[:, 0, :], parts[:, 1, :], LAST_CUTS[1], T)
-        for lo, hi in ends:
-            add(total, joined[:, 1, :], parts[:, 2, :], lo, hi)
+        q1, q2, q3 = BACK_CUTS
+        early = q1 + P
+        for r, lo, hi in ((0, q1, early), (0, early, q2), (1, q1, q2), (0, q2, T), (2, q1, q2), (1, q2, T), (2, q2, q3), (2, q3, T)):
+            fetch(r, lo, hi)
+        two, three = joined[:, 0, :], joined[:, 1, :]
+        nc.vector.tensor_copy(parts[:, 0, 0:q1], picked(0, 0, q1))
+        fetch_onto(two, TOP - 1, parts[:, 0, :], q1, early)
+        fetch_onto(two, 1, parts[:, 0, :], 0, q1)
+        fetch_onto(two, TOP - 1, parts[:, 0, :], early, q2)
+        fetch_onto(three, 2, two, 0, q1)
+        add(three, two, parts[:, 1, :], q1, q2)
+        fetch_onto(two, TOP - 1, parts[:, 0, :], q2, T)
+        add(total, three, parts[:, 2, :], q1, q2)
+        nc.sync.dma_start(out[:, q1:q2], total[:, q1:q2])
+        fetch_onto(total, TOP - 1, three, 0, q1)
+        nc.sync.dma_start(out[:, 0:q1], total[:, 0:q1])
+        for lo, hi in ((q2, q3), (q3, T)):
+            add(three, two, parts[:, 1, :], lo, hi)
+        for lo, hi in ((q2, q3), (q3, T)):
+            add(total, three, parts[:, 2, :], lo, hi)
             nc.sync.dma_start(out[:, lo:hi], total[:, lo:hi])

from contextlib import ExitStack

import concourse.mybir as mybir

K, T, E, C, N = 1024, 1024, 16, 256, 128
S = E * C
TOP = 4
FLOPS = 2 * K * N * S

F32 = mybir.dt.float32
BF16 = mybir.dt.bfloat16
I32 = mybir.dt.int32
U32 = mybir.dt.uint32
U16 = mybir.dt.uint16
U8 = mybir.dt.uint8
FP8X4 = mybir.dt.float8_e4m3fn_x4
FP4X4 = mybir.dt.float4_e2m1fn_x4
MULT = mybir.AluOpType.mult
ADD = mybir.AluOpType.add
GELU = mybir.ActivationFunctionType.Gelu_apprx_tanh
COPY = mybir.ActivationFunctionType.Copy

P = 128
PACK = 4
PASSES = K // (P * PACK)
LIST = 16
WINDOW = T + 32
BANK = 512
RUN = 4
RUN_G = 4
STEP = 64
QUAD = 32
SPAN = 1024
ORDER = [(0, 0), (0, 1), (1, 0), (1, 1), (0, 2), (1, 2), (0, 3), (1, 3)]
GATHERED = [0, 0, 1408, 1344, 1344, 1344, 1344, 1024]
MULTIPLIED = [0, 640, 456, 456, 456, 456, 512, 512]
FIRST_SPLIT = 768
GROUP_CUTS = list(range(0, S - SPAN, BANK)) + list(range(S - SPAN, S, C)) + [S - P, S]
BACK_CUTS = (256, 640, 832)
LATE = 192


def tile_moe_pre_lin_gelu_kernel(
    tc, xT, w_words, w_scales, b, gate, offs, pos1, pos2, pos3, pos4, out
):
    nc = tc.nc
    with ExitStack() as ctx:
        keep = ctx.enter_context(tc.tile_pool(name="keep", bufs=1))
        lanes = ctx.enter_context(tc.tile_pool(name="lanes", bufs=1))
        cpool = ctx.enter_context(tc.tile_pool(name="cpool", bufs=6))
        sums = ctx.enter_context(tc.psum_pool(name="sums", bufs=6))
        spread = ctx.enter_context(tc.psum_pool(name="spread", bufs=2))

        offs_sb = keep.tile([P, S // LIST], U16, name="offs_sb")
        pos_sb = [keep.tile([P, T // LIST], U16, name="pos_sb%d" % r) for r in range(TOP)]
        windows = [[keep.tile([P, WINDOW], F32, name="win%d_%d" % (a, t), align_bytes=64) for t in range(PACK)] for a in range(PASSES)]
        gate_sb = keep.tile([P, S], F32, name="gate_sb", align_bytes=64)
        rounds = len(ORDER)
        last = rounds - 1
        spans = [SPAN] * last + [SPAN - LATE]
        raw_bytes = 4 * PACK * SPAN
        half = raw_bytes // 2
        lane_bytes = (rounds // 2 - 1) * (half + STEP) + raw_bytes

        def raw_place(r):
            if r == 0:
                return raw_bytes
            return ((r - 1) % 2) * lane_bytes + ((r - 1) // 2) * (half + STEP)

        def rounded_place(r):
            return raw_place(r - 1) if r > 1 else lane_bytes + raw_bytes + r * (half + STEP)

        gate_rows = [lanes.tile([P, P], F32, name="gate_rows%d" % h, offset=place) for h, place in enumerate((raw_place(1), rounded_place(1)))]
        rows = S // P // 2
        gate_cols = keep.tile([P, S // P], F32, name="gate_cols")
        identity = keep.tile([P, P], F32, name="identity")
        ones = keep.tile([P, QUAD], F32, name="ones", align_bytes=64)
        column = keep.tile([P, QUAD], F32, name="column", align_bytes=64)
        row = keep.tile([P, QUAD], F32, name="row", align_bytes=64)
        w_sb = keep.tile([P, E * PASSES * 2 * N], U8, name="w_sb", align_bytes=64)
        ws_sb = keep.tile([P, E * PASSES * N], U8, name="ws_sb", align_bytes=64)
        y = keep.tile([P, S], F32, name="y")

        x_rows = xT.rearrange("(a p t) c -> a t p c", a=PASSES, t=PACK)

        idle = keep.tile([P, 2], F32, name="idle")
        nc.vector.memset(idle[:, 0:1], 0.0)
        nc.vector.memset(ones[:], 1.0)
        for h in range(2):
            nc.vector.memset(gate_rows[h][:], 0.0)
        nc.vector.tensor_tensor_scan(column[:], ones[:], ones[:], 0.0, MULT, ADD)
        nc.vector.memset(identity[:], 0.0)
        nc.vector.transpose(row[:], column[:])
        nc.vector.memset(ws_sb[:].bitcast(I32), 0)
        for q in range(0, P, QUAD):
            nc.vector.tensor_tensor(identity[q : q + QUAD, q : q + QUAD], column[q : q + QUAD, :], row[q : q + QUAD, :], mybir.AluOpType.is_equal)

        needed = []
        for j in range(S // SPAN):
            needed.append((j * SPAN + min(n for n, (a, i) in zip(MULTIPLIED, ORDER) if i == j), (j + 1) * SPAN))

        nc.scalar.dma_start(windows[0][0][:, 0:FIRST_SPLIT], x_rows[0, 0][:, 0:FIRST_SPLIT])
        nc.scalar.activation(idle[:, 1:2], idle[:, 0:1], GELU)
        nc.sync.dma_start(offs_sb[:], offs)
        nc.sync.dma_start(windows[0][0][:, FIRST_SPLIT:T], x_rows[0, 0][:, FIRST_SPLIT:T])
        nc.sync.dma_start(windows[0][1][:, 0:T], x_rows[0, 1])
        gate_row = gate[0, :].rearrange("(h m n) -> h m n", h=2, n=P)
        nc.sync.dma_start(gate_rows[0][0:rows, :], gate_row[0])
        nc.sync.dma_start(gate_sb[:, 0:SPAN], gate[0:P, 0:SPAN])
        for t in range(2, PACK):
            nc.sync.dma_start(windows[0][t][:, 0:T], x_rows[0, t])
        nc.sync.dma_start(windows[1][0][:, 0:T], x_rows[1, 0])
        nc.sync.dma_start(gate_rows[1][0:rows, :], gate_row[1])
        for t in range(1, PACK):
            nc.sync.dma_start(windows[1][t][:, 0:T], x_rows[1, t])
        lo, hi = needed[1]
        nc.sync.dma_start(gate_sb[:, lo:hi], gate[0:P, lo:hi])
        nc.sync.dma_start(
            w_sb[:].bitcast(I32).rearrange("p (g n) -> p g n", g=E * PASSES),
            w_words.rearrange("e a p n -> p (e a) n").bitcast(I32),
        )
        for q in range(4):
            nc.sync.dma_start(
                ws_sb[32 * q : 32 * q + 4, :].bitcast(I32).rearrange("p (g n) -> p g n", g=E * PASSES),
                w_scales[:, :, 4 * q : 4 * q + 4, :].rearrange("e a q n -> q (e a) n").bitcast(I32),
            )
        for lo, hi in needed[2:]:
            nc.sync.dma_start(gate_sb[:, lo:hi], gate[0:P, lo:hi])
        for r, pos in enumerate((pos1, pos2, pos3, pos4)):
            nc.sync.dma_start(pos_sb[r][:], pos)

        def listed(a, t, lo, hi):
            return windows[a][t][:].indirect(offs_sb[:, lo // LIST : hi // LIST])

        def shares(r):
            return [(t, min(spans[r], max(0, (t + 1) * spans[r] - GATHERED[r]))) for t in range(PACK)]

        def scalar_gather(r):
            a, j = ORDER[r]
            raw = lanes.tile([P, PACK, spans[r]], F32, name="raw%d" % r, offset=raw_place(r) + 4 * PACK * (SPAN - spans[r]))
            for t, n in shares(r):
                if n > 0:
                    nc.scalar.activation(raw[:, t, 0:n], listed(a, t, j * SPAN, j * SPAN + n), COPY)
            return raw

        def vector_gather(r, raw, t0, t1):
            a, j = ORDER[r]
            for t, n in shares(r)[t0:t1]:
                if n < spans[r]:
                    nc.vector.tensor_copy(raw[:, t, n : spans[r]], listed(a, t, j * SPAN + n, j * SPAN + spans[r]))

        def times_gate(engine, run, xb, raw, weights):
            width = weights.shape[1]
            planes = raw.shape[1]
            engine.tensor_tensor(
                xb.rearrange("p (c i) t -> p c t i", i=run),
                raw.rearrange("p t (c i) -> p c t i", i=run),
                weights.rearrange("p (c i) -> p c i", i=run).unsqueeze(2).to_broadcast([P, width // run, planes, run]),
                MULT,
            )

        def by_slot(xb):
            return xb.rearrange("p (s t) -> p s t", t=PACK)

        spreads = {}

        def spread_gate(lo, hi):
            if lo not in spreads:
                bank = spread.tile([P, BANK], F32, name="gate_ps")
                for c0 in range(lo, hi, P):
                    m = c0 // P
                    nc.tensor.transpose(bank[:, c0 - lo : c0 - lo + P], gate_cols[:, m : m + 1].to_broadcast([P, P]), identity[:])
                spreads[lo] = bank
            return spreads[lo]

        banks = {}
        todo = {}
        closed = []

        def multiply(a, c0, c1, codes, scales):
            m0 = c0
            while m0 < c1:
                lo, hi = [(lo, hi) for lo, hi in zip(GROUP_CUTS[:-1], GROUP_CUTS[1:]) if lo <= m0 < hi][0]
                width = min(C - m0 % C, c1 - m0, hi - m0)
                matrix = (m0 // C) * PASSES + a
                first = lo not in banks
                if first:
                    banks[lo] = sums.tile([P, hi - lo], F32, name="acc")
                    todo[lo] = PASSES * (hi - lo)
                todo[lo] = todo[lo] - width
                nc.tensor.matmul_mx(
                    out=banks[lo][:, m0 - lo : m0 - lo + width],
                    lhsT=w_sb[:, matrix * 2 * N : (matrix + 1) * 2 * N].bitcast(FP4X4),
                    lhsT_scale=ws_sb[:, matrix * N : (matrix + 1) * N],
                    rhs=codes[:, m0 - c0 : m0 - c0 + width].bitcast(FP8X4),
                    rhs_scale=scales[:, m0 - c0 : m0 - c0 + width],
                    start=first,
                    stop=(todo[lo] == 0),
                )
                if todo[lo] == 0:
                    closed.append((lo, hi))
                m0 = m0 + width

        def activate(b_sb):
            for lo, hi in closed:
                for e0 in range(lo, hi, C):
                    e1 = min(e0 + C, hi)
                    bias = b_sb[:, e0 // C : e0 // C + 1]
                    nc.scalar.activation(y[:, e0:e1], banks[lo][:, e0 - lo : e1 - lo], GELU, bias=bias)
            closed.clear()

        def quantise(r, c0, c1, xb):
            a, j = ORDER[r]
            codes = cpool.tile([P, c1 - c0], U32, name="codes", align_bytes=64)
            scales = cpool.tile([P, c1 - c0], U8, name="scales", align_bytes=64)
            nc.vector.quantize_mx(out=codes[:].bitcast(FP8X4), scales=scales[:], in_=xb)
            multiply(a, j * SPAN + c0, j * SPAN + c1, codes, scales)

        raw0 = lanes.tile([P, PACK, SPAN], F32, name="raw0", offset=raw_place(0))
        raw1 = lanes.tile([P, PACK, SPAN], F32, name="raw1", offset=raw_place(1))
        middle = SPAN // 2
        for t in range(2):
            nc.scalar.activation(raw0[:, t, 0:middle], listed(0, t, 0, middle), COPY)
            nc.vector.tensor_copy(raw0[:, t, middle:SPAN], listed(0, t, middle, SPAN))
        turned = spread.tile([P, 2, P], F32, name="gate_ps")
        nc.tensor.transpose(turned[:, 0, :], gate_rows[0][:], identity[:])
        nc.vector.tensor_copy(gate_cols[:, 0:rows], turned[:, 0, 0:rows])
        for raw, t, lo in ((raw1, 0, SPAN), (raw0, 2, 0), (raw1, 2, SPAN)):
            nc.vector.tensor_copy(raw[:, t, :], listed(0, t, lo, lo + SPAN))
            nc.scalar.activation(raw[:, t + 1, :], listed(0, t + 1, lo, lo + SPAN), COPY)
        nc.tensor.transpose(turned[:, 1, :], gate_rows[1][:], identity[:])
        nc.scalar.copy(gate_cols[:, rows:], turned[:, 1, 0:rows])
        before = lanes.tile([P, SPAN * PACK], BF16, name="xb0", offset=rounded_place(0), align_bytes=64)
        for t in (0, 2):
            times_gate(nc.gpsimd, RUN_G, by_slot(before[:])[:, :, t : t + 2], raw0[:, t : t + 2, :], gate_sb[:, 0:SPAN])
        raw = raw1
        for r in range(1, last):
            lo, n = ORDER[r][1] * SPAN, MULTIPLIED[r]
            xb = lanes.tile([P, SPAN * PACK], BF16, name="xb%d" % r, offset=rounded_place(r), align_bytes=64)
            ahead = scalar_gather(r + 1)
            if r == 1:
                vector_gather(r + 1, ahead, 0, 1)
            for c0 in range(0, n, BANK):
                c1 = min(n, c0 + BANK)
                times_gate(nc.vector, RUN, by_slot(xb[:])[:, c0:c1, :], raw[:, :, c0:c1], spread_gate(lo + c0, lo + c1)[:, 0 : c1 - c0])
            times_gate(nc.gpsimd, RUN_G, by_slot(xb[:])[:, n:SPAN, :], raw[:, :, n:SPAN], gate_sb[:, lo + n : lo + SPAN])
            vector_gather(r + 1, ahead, 1 if r == 1 else 0, PACK)
            quantise(r - 1, 0, SPAN, before[:])
            raw, before = ahead, xb

        a, j = ORDER[last]
        late = lanes.tile([P, PACK, LATE], F32, name="late", offset=raw_place(last))
        for t in range(PACK):
            nc.scalar.activation(late[:, t, :], listed(a, t, S - LATE, S), COPY)
        b_sb = lanes.tile([P, E], F32, name="b_sb", offset=raw_place(last - 2) + half)
        nc.sync.dma_start(b_sb[:], b)
        activate(b_sb)

        lo, n = j * SPAN, SPAN - LATE
        front = lanes.tile([P, BANK * PACK], BF16, name="front", offset=rounded_place(last), align_bytes=64)
        rear = lanes.tile([P, BANK * PACK], BF16, name="rear", offset=rounded_place(last) + half // 2, align_bytes=64)
        times_gate(nc.gpsimd, RUN_G, by_slot(rear[:])[:, 0 : n - BANK, :], raw[:, :, BANK:n], gate_sb[:, lo + BANK : lo + n])
        times_gate(nc.vector, RUN, by_slot(front[:]), raw[:, :, 0:BANK], spread_gate(lo, lo + BANK)[:])
        times_gate(nc.vector, RUN, by_slot(rear[:])[:, n - BANK :, :], late[:], spread_gate(S - C, S)[:, C - LATE : C])
        for c0, c1 in zip(GROUP_CUTS[:-1], GROUP_CUTS[1:]):
            if c0 >= lo:
                c0, c1 = c0 - lo, c1 - lo
                quantise(last - 1, c0, c1, before[:, c0 * PACK : c1 * PACK])
                if c0 < BANK:
                    quantise(last, c0, c1, front[:, c0 * PACK : c1 * PACK])
                else:
                    quantise(last, c0, c1, rear[:, (c0 - BANK) * PACK : (c1 - BANK) * PACK])
        activate(b_sb)

        parts = keep.tile([P, TOP - 1, T], F32, name="gate_sb", align_bytes=64)
        joined = keep.tile([P, 2, T], F32, name="joined", align_bytes=64)
        total = keep.tile([P, T], F32, name="win0_0", align_bytes=64)

        def picked(r, lo, hi):
            return y[:].indirect(pos_sb[r][:, lo // LIST : hi // LIST])

        def fetch(r, lo, hi):
            nc.scalar.activation(parts[:, r, lo:hi], picked(r, lo, hi), COPY)

        def fetch_onto(into, r, onto, lo, hi):
            nc.vector.tensor_tensor(into[:, lo:hi], picked(r, lo, hi), onto[:, lo:hi], ADD)

        def add(into, left, right, lo, hi):
            nc.vector.tensor_tensor(into[:, lo:hi], left[:, lo:hi], right[:, lo:hi], ADD)

        q1, q2, q3 = BACK_CUTS
        early = q1 + P
        for r, lo, hi in ((0, q1, early), (0, early, q2), (1, q1, q2), (0, q2, T), (2, q1, q2), (1, q2, T), (2, q2, q3), (2, q3, T)):
            fetch(r, lo, hi)
        two, three = joined[:, 0, :], joined[:, 1, :]
        nc.vector.tensor_copy(parts[:, 0, 0:q1], picked(0, 0, q1))
        fetch_onto(two, TOP - 1, parts[:, 0, :], q1, early)
        fetch_onto(two, 1, parts[:, 0, :], 0, q1)
        fetch_onto(two, TOP - 1, parts[:, 0, :], early, q2)
        fetch_onto(three, 2, two, 0, q1)
        add(three, two, parts[:, 1, :], q1, q2)
        fetch_onto(two, TOP - 1, parts[:, 0, :], q2, T)
        add(total, three, parts[:, 2, :], q1, q2)
        nc.sync.dma_start(out[:, q1:q2], total[:, q1:q2])
        fetch_onto(total, TOP - 1, three, 0, q1)
        nc.sync.dma_start(out[:, 0:q1], total[:, 0:q1])
        for lo, hi in ((q2, q3), (q3, T)):
            add(three, two, parts[:, 1, :], lo, hi)
        for lo, hi in ((q2, q3), (q3, T)):
            add(total, three, parts[:, 2, :], lo, hi)
            nc.sync.dma_start(out[:, lo:hi], total[:, lo:hi])
